import numpy as np, ml_dtypes
CORES = [36,164,52,180,100,228,116,244]
N = 8
import mx_ref
BF = ml_dtypes.bfloat16
def pick(q, e):
    c = np.concatenate([q[0].reshape(128, -1, 4), np.zeros((128, 1, 4), np.uint8)], axis=1); s = np.concatenate([q[1], np.ones((16, 1), np.uint8)], axis=1)
    return (np.ascontiguousarray(c[:, e].reshape(128, -1)), np.ascontiguousarray(s[:, e]))
def join(*qs):
    return (np.concatenate([q[0] for q in qs], axis=1), np.concatenate([q[1] for q in qs], axis=1))
def put(q, e, v):
    c, s = q[0].reshape(128, -1, 4).copy(), q[1].copy(); c[:, e] = v[0].reshape(128, -1, 4); s[:, e] = v[1]
    return (c.reshape(128, -1), s)
def pk(c, s):
    return (np.ascontiguousarray(c), mx_ref.live(s))
def emit(q):
    return q[0], q[1]
def decode(q):
    o = []
    for b in range(4):
        e = np.zeros((128, 128, 4), np.float32); e[np.arange(128), np.arange(128), b] = 1
        o.append(mx_ref.matmul(mx_ref.quantize(e.reshape(128, 512).astype(BF)), q))
    return np.stack(o, axis=2).reshape(128, -1)
def cut(t, i, w=512):
    return t[:, w * i:w * i + w]
def f(rng, *shape):
    return mx_ref.flush((rng.standard_normal(shape, dtype=np.float32) * np.exp2(rng.integers(-2, 3, shape[:-1] + (1,)))).astype(BF))
def wide(rng, *shape, cols=0):
    v = rng.standard_normal(shape, dtype=np.float32) * np.exp2(rng.integers(-12, 13, shape)).astype(np.float32)
    if cols: v *= np.repeat(np.exp2(rng.integers(-cols, cols + 1, shape[:-2] + (1, shape[-1] // 4))) * (rng.random(shape[:-2] + (1, shape[-1] // 4)) > 0.0625), 4, axis=-1).astype(np.float32)
    return mx_ref.flush(v.astype(BF))
P, K, R, O = 192, 32, 3, 1
def big(v):
    v = v.astype(np.float32)
    v[np.abs(v) < np.float32(2.0 ** -16)] = 0
    return v.astype(BF)
def plain(rng):
    u = np.array(f(rng, N, 128, 512))
    u[:, :, 4 * R:] = 0
    return {"c": big(f(rng, N, 128, 4 * P)), "u": u, "w": f(rng, N, 128, 512 * O)}
def bf(v, *shape):
    return np.ascontiguousarray(v).reshape(shape).astype(np.float32).astype(BF)
def signs(rng):
    return rng.choice([-1.0, 1.0], (128, 1, 4))
def heavy(rng, way):
    d, g = plain(rng), signs(rng)
    size = np.exp2(rng.integers(0, 3, (N, P)))
    size[np.arange(N), rng.integers(0, P, N)] = 1024
    d["c"] = bf((1 + rng.random((N, 128, P, 4))) * size[:, None, :, None] * g * 2.0 ** 18, N, 128, 4 * P)
    d["u"][:, :, :4 * R] = bf((1 + rng.random((N, 128, R, 4))) * g * np.asarray(way)[:, None] * 2.0 ** 28, N, 128, 4 * R)
    return d
def setup_inputs(rng):
    return plain(rng)
def setup_inputs_one(rng):
    return heavy(rng, np.ones(R))
def setup_inputs_chain(rng):
    return heavy(rng, np.where(np.arange(R) == 0, 1.0, -1.0))
def setup_inputs_apart(rng):
    d, g = plain(rng), signs(rng)
    v = np.zeros((N, 128, P, 4))
    for r in range(N):
        at = rng.permutation(P)
        a, b = at[:K], at[K:2 * K]
        v[r][np.arange(K), a] = 32 * (1 + rng.random((K, 4)))
        v[r][np.arange(K), b] = 32 * (1 + rng.random((K, 4)))
        v[r][64:96, a] = -(1 + 0.125 * rng.random((32, K, 4)))
        v[r][64:96, at[K:]] = 4096
        v[r][96:, at[K:]] = 1 + rng.random((32, P - K, 4))
    d["c"] = bf(v * g * 2.0 ** 18, N, 128, 4 * P)
    q = (1 + rng.random((N, 128, R, 4))) * g
    q[:, :64] = 0
    d["u"][:, :, :4 * R] = bf(q, N, 128, 4 * R)
    return d
def setup_inputs_ties(rng):
    d, g = plain(rng), signs(rng)
    v = np.abs(d["c"].astype(np.float32)).reshape(N, 128, P, 4)[:, :, :8] * g
    v[:, :, 0] = 0
    h = [rng.permutation(np.arange(P) % 8) for r in range(N)]
    for r in range(0, N, 2):
        i = int(np.flatnonzero(h[r] == 0)[0])
        h[r][i] = h[r][0]
        h[r][0] = 0
    d["c"] = bf(np.stack([v[r][:, h[r]] for r in range(N)]), N, 128, 4 * P)
    d["u"][:, :, :4] = bf(np.abs(d["u"][:, :, :4].astype(np.float32)).reshape(N, 128, 1, 4) * g, N, 128, 4)
    return d
def setup_inputs_spread(rng):
    d = plain(rng)
    d["u"][:, :, 4:8] = 0
    return {**d, "c": big(wide(rng, N, 128, 4 * P, cols=6))}
def check_inputs(d):
    b = []
    for k, low in (("c", 2.0 ** -16), ("u", 2.0 ** -30), ("w", 2.0 ** -30)):
        v = np.abs(d[k].astype(np.float32))
        if not (np.isfinite(v).all() and ((v == 0) | (v >= low) & (v <= 2.0 ** 30)).all()): b.append("a value of " + k)
    if (d["u"][:, :, 4 * R:].astype(np.float32) != 0).any(): b.append("u has numbers behind its first R columns")
    return b
def reference(c, u, w):
    tg = np.zeros((N, R, K), np.float32)
    cs = [mx_ref.quantize(np.ascontiguousarray(c[r])) for r in range(N)]
    qu = [mx_ref.quantize(np.ascontiguousarray(u[r])) for r in range(N)]
    half, zero = np.float32(0.5), np.float32(0)
    for t in range(R):
        left, sent = [], []
        for r in range(N):
            s = mx_ref.matmul(qu[r], cs[r])[t] + zero
            left.append(np.argsort(s, kind="stable")[:K])
            sent.append(pick(cs[r], left[r]))
        for r in range(N):
            a = sent[r ^ (1 << t)]
            z = mx_ref.matmul(pick(a, np.concatenate([np.arange(K), np.full(128 - K, -1)])), cs[r])[:K] + zero
            z[:, left[r]] = -np.inf
            to = np.argmax(z, axis=1)
            merge = np.sort(np.unique(to, return_index=True)[1])
            fill = np.setdiff1d(np.arange(K), merge)
            places = np.sort(left[r])[:len(fill)]
            v = decode(join(cs[r], a)).reshape(128, P + K, 4)
            v[:, to[merge]] = half * v[:, to[merge]] + half * v[:, P + merge]
            new = mx_ref.quantize(np.ascontiguousarray(v[:, :P]).reshape(128, -1).astype(BF))
            q = put(cs[r], to[merge], pick(new, to[merge]))
            cs[r] = put(q, places, pick(a, fill))
            tg[r, t, merge] = to[merge]
            tg[r, t, fill] = -1 - places
    oc, osc, y = np.zeros((N, 128, 4 * P), np.uint8), np.zeros((N, 16, P), np.uint8), np.zeros((N, 128, O * P), np.float32)
    for r in range(N):
        oc[r], osc[r] = emit(cs[r])
        for o in range(O):
            y[r, :, o * P:o * P + P] = mx_ref.matmul(mx_ref.quantize(np.ascontiguousarray(cut(w[r], o))), cs[r])
    return {"oc": oc, "osc": osc, "tg": tg, "y": y}

@@ -1,0 +1,533 @@
+from concourse.mybir import dt, AluOpType as Op, AxisListType, ActivationFunctionType as Act
+
+N, P, K, R = 8, 192, 32, 3
+TINY = 1e-30
+BIG = 2.0 ** 30
+LOW = -1e29
+WAKE, SLACK = 0.18, 0.3
+LOAD, ISSUE, FLIGHT = 1.1, 0.4, 1.0
+MMC = 0.0012
+
+MXC, U8, F32, BF, I32, U16 = "float8_e4m3fn_x4", "uint8", "float32", "bfloat16", "int32", "uint16"
+SCRATCH = {}
+
+
+def _buf(name, cols, dtype, where="sbuf"):
+    SCRATCH[name] = (where, [128, cols], dtype)
+
+
+def _pair(name, cols):
+    _buf(name + "q", cols, MXC)
+    _buf(name + "s", cols, U8)
+
+
+for _t in range(R):
+    _pair("x%d" % _t, P)
+    _pair("v%d" % _t, P + 160)
+    _pair("n%d" % _t, K)
+    _pair("u%d" % _t, 320)
+    _buf("sc%d" % _t, 32, F32)
+    _buf("cr%d" % _t, 64, F32)
+    _buf("gi%d" % _t, P, BF)
+_pair("x3", P)
+for _n, _c in (("w", 128), ("eb", 512), ("kc", 512), ("e", 128), ("cm", P), ("mk", P), ("xo", 128), ("wf", 128), ("xf", 128)):
+    _pair(_n, _c)
+for _n, _c in (("ct", 4 * P), ("ut", 16), ("wt", 512), ("ub", 1280), ("st", 2048), ("kst", 2048), ("et", 512), ("cmt", 4 * P),
+               ("mkt", 4 * P), ("zz", 544), ("wft", 512), ("mt", 512), ("oneb", P), ("er", 256), ("cw", 256), ("rb", 128), ("rk0", P), ("rk1", P)):
+    _buf(_n, _c, BF)
+for _n, _c in (("th0", P), ("th1", P), ("thn", P), ("zf", P), ("one32", 32), ("up32", 32), ("eye32", 32), ("mw", 16), ("mwb", 16), ("m8", 8),
+               ("nk", 16), ("d0", 64), ("d1", 64), ("ms", 64), ("d16", 8), ("dm", 8), ("cf", 16), ("ohb", 16), ("ohh", 16), ("oha", 16),
+               ("pm", 200), ("tb", 32), ("tt", 32), ("ne", 64), ("dg", 32), ("xa", 24), ("hd", 4 * P), ("ha", 128),
+               ("yw", 256), ("yo", P), ("tgb", 16), ("js0", 16), ("js1", P), ("js2", 200), ("js3", 16), ("js4", 64), ("js5", P)):
+    _buf(_n, _c, F32)
+_buf("ic", 16, I32)
+_buf("ol", 2, U16)
+_buf("om", 8, U16)
+_buf("of", 12, U16)
+for _n in range(8):
+    _buf("b%d" % _n, 512, F32, "psum")
+
+SEMAPHORES = ["sv", "ss", "stn", "sg", "lc", "lu", "lw", "oc_", "oy_"] + ["os%d" % k for k in range(4)] + ["tg_%d" % k for k in range(R)] \
+    + ["arr%d" % k for k in range(R)] + ["sent%d" % k for k in range(R)] + ["cq%d" % k for k in range(R)] + ["cs%d" % k for k in range(R)]
+
+
+def _cross(a, b):
+    if a[1] >= b[2] or b[1] >= a[2] or a[3] >= b[4] or b[3] >= a[4]:
+        return False
+    m = min(a[5], b[5])
+    if m > 1 and a[5] % m == 0 and b[5] % m == 0:
+        return (a[3] - b[3]) % m == 0
+    return True
+
+
+def _within(a, b):
+    if not (a[1] <= b[1] and b[2] <= a[2] and a[3] <= b[3] and b[4] <= a[4]):
+        return False
+    return a[5] == 1 or (a[5] == b[5] and (a[3] - b[3]) % a[5] == 0)
+
+
+def _size(x):
+    return (x[4] - x[3] + x[5] - 1) // x[5]
+
+
+def _order(nodes):
+    users = [[] for m in nodes]
+    for m in nodes:
+        for d in m["after"]:
+            users[d].append(m["n"])
+    way = [0.0] * len(nodes)
+    for m in reversed(nodes):
+        way[m["n"]] = max([m["late"]] + [m["late"] + WAKE * nodes[k]["after"][m["n"]] + way[k] for k in users[m["n"]]])
+    left = [len(m["after"]) for m in nodes]
+    ready = [0.0] * len(nodes)
+    free = {}
+    able = [m["n"] for m in nodes if not m["after"]]
+    done = []
+    while able:
+        best = None
+        for q in set(nodes[k]["q"] for k in able):
+            ks = [k for k in able if nodes[k]["q"] == q]
+            t0 = max(free.get(q, 0.0), min(ready[k] for k in ks))
+            ks = [k for k in ks if ready[k] <= t0 + SLACK]
+            k = max(ks, key=lambda i: (way[i], -i))
+            now = [i for i in ks if ready[i] <= t0 and t0 + 1.8 * nodes[i]["busy"] <= ready[k] + 0.02]
+            if ready[k] > t0 and now:
+                k = max(now, key=lambda i: (way[i], -i))
+            t = max(t0, ready[k])
+            if best is None or (t, q) < best[:2]:
+                best = (t, q, k)
+        t, q, k = best
+        able.remove(k)
+        free[q] = t + nodes[k]["busy"]
+        done.append(k)
+        for i in users[k]:
+            ready[i] = max(ready[i], t + nodes[k]["late"] + (WAKE if nodes[i]["after"][k] else 0.0))
+            left[i] -= 1
+            if not left[i]:
+                able.append(i)
+    return done
+
+
+def rank_program(g, core, T, topo):
+    rank = T.rank_of(core)
+    if rank is None:
+        return
+    queue = {"V": g.vector, "S": g.scalar, "T": g.tensor, "G": g, "Y": g.sync}
+    own = {"V": "sv", "S": "ss", "T": "stn", "G": "sg"}
+    log = {}
+    nodes = []
+
+    def A(name, c0, c1, step=1, p0=0, p1=128):
+        return (name, p0, p1, c0, c1, step)
+
+    def ap(x):
+        return T[x[0]][x[1]:x[2], x[3]:x[4]:x[5]] if x[5] > 1 else T[x[0]][x[1]:x[2], x[3]:x[4]]
+
+    def psum(x):
+        return SCRATCH[x[0]][0] == "psum"
+
+    def add(q, reads, writes, busy, late, issue, sem=None, val=0):
+        after = {}
+        node = {"q": q, "n": len(nodes), "after": after, "busy": busy, "late": late, "issue": issue, "sem": sem, "val": val}
+        for views, w in ((reads, False), (writes, True)):
+            for x in views:
+                for y, m, yw in log.get(x[0], []):
+                    if psum(x):
+                        if q == "T" and m["q"] == "T":
+                            after.setdefault(m["n"], False)
+                        elif q != m["q"] or w or yw:
+                            after[m["n"]] = True
+                    elif (w or yw) and _cross(x, y):
+                        after[m["n"]] = True
+        for x in writes:
+            log[x[0]] = [e for e in log.get(x[0], []) if not _within(x, e[0]) or (psum(x) and q == "T" and e[1]["q"] == "T")]
+        for views, w in ((reads, False), (writes, True)):
+            for x in views:
+                log.setdefault(x[0], []).append((x, node, w))
+        nodes.append(node)
+        return node
+
+    def do(q, reads, writes, call, kind=""):
+        n = max(_size(x) for x in reads[:1] + writes[:1])
+        if kind == "quant":
+            cost = 0.015 + 0.000275 * _size(reads[0])
+        elif kind == "pick":
+            cost = 0.07 + 0.0016 * _size(writes[0])
+        elif q == "T":
+            cost = MMC * (_size(writes[0]) + 16)
+        elif q == "G":
+            cost = 0.2 + 0.002 * n
+        else:
+            two = q == "V" and all(SCRATCH[x[0]][2] in (BF, U16) for x in reads[:1] + writes[:1])
+            cost = max(64, n * (0.5 if two else 1)) * 0.00104
+        return add(q, reads, writes, cost, cost, call)
+
+    def dma(q, out, in_, sem, reads, writes):
+        add(q, reads, writes, 0.1, LOAD, lambda: queue[q].dma_start(out, in_), sem, 16)
+
+    def emit():
+        count = {"V": 0, "S": 0, "T": 0, "G": 0}
+        known = {q: {} for q in queue}
+        every = {}
+        done = _order(nodes)
+        at = {k: i for i, k in enumerate(done)}
+        for k in done:
+            m = nodes[k]
+            q = m["q"]
+            if q in queue:
+                for d in sorted(m["after"], reverse=True, key=lambda i: at[i]):
+                    o = nodes[d]
+                    if not m["after"][d] or known[q].get(o["sem"], 0) >= o["val"]:
+                        continue
+                    queue[q].wait_ge(T.sem[o["sem"]], o["val"])
+                    for s, v in list(o["clock"].items()) + [(o["sem"], o["val"])]:
+                        known[q][s] = max(known[q].get(s, 0), v)
+            if m["sem"] is None:
+                count[q] += 1
+                m["sem"], m["val"] = own[q], count[q]
+                m["issue"]().then_inc(T.sem[own[q]], 1)
+            elif m["issue"] is not None:
+                ins = m["issue"]()
+                if m["sem"][0:4] != "sent":
+                    ins.then_inc(T.sem[m["sem"]], 16)
+            m["clock"] = dict(known.get(q, {}))
+            every[m["sem"]] = max(m["val"], every.get(m["sem"], 0))
+        final = ["sg", "stn", "ss", "sv"] + ["os%d" % k for k in range(4)] + ["tg_%d" % (R - 1), "oc_", "oy_"]
+        for s in [e for e in every if e not in final] + final:
+            g.wait_ge(T.sem[s], every[s])
+
+    V, S = g.vector, g.scalar
+
+    def val(s):
+        return ap(s) if isinstance(s, tuple) else s
+
+    def fill(x, v):
+        do("V", [], [x], lambda: V.memset(ap(x), v))
+
+    def copy(o, i):
+        do("V", [i], [o], lambda: V.tensor_copy(ap(o), ap(i)))
+
+    def ts(o, i, s1, s2, op0, op1=None):
+        rd = [i] + [s for s in (s1, s2) if isinstance(s, tuple)]
+        if op1 is None:
+            do("V", rd, [o], lambda: V.tensor_scalar(ap(o), ap(i), val(s1), None, op0))
+        else:
+            do("V", rd, [o], lambda: V.tensor_scalar(ap(o), ap(i), val(s1), val(s2), op0, op1))
+
+    def tt(o, i0, i1, op):
+        do("V", [i0, i1], [o], lambda: V.tensor_tensor(ap(o), ap(i0), ap(i1), op))
+
+    def red(o, i, op):
+        do("V", [i], [o], lambda: V.tensor_reduce(ap(o), ap(i), AxisListType.X, op))
+
+    def scan(o, d0, d1, init, op0, op1):
+        rd = [d0, d1] + ([init] if isinstance(init, tuple) else [])
+        do("V", rd, [o], lambda: V.tensor_tensor_scan(ap(o), ap(d0), ap(d1), val(init), op0, op1))
+
+    def turn(o, i):
+        do("V", [i], [o], lambda: V.transpose(ap(o), ap(i)))
+
+    def act(o, i, f=Act.Identity, bias=0.0, scale=1.0, acc=None):
+        rd = [i] + [s for s in (bias, scale) if isinstance(s, tuple)]
+        if acc is None:
+            do("S", rd, [o], lambda: S.activation(ap(o), ap(i), f, bias=val(bias), scale=val(scale)))
+        else:
+            do("S", rd, [o, acc], lambda: S.activation(ap(o), ap(i), f, bias=val(bias), scale=val(scale), accum_out=ap(acc)))
+
+    def quant(n, c0, c1, i):
+        q, s = A(n + "q", c0, c1), A(n + "s", c0, c1)
+        do("V", [i], [q, s], lambda: V.quantize_mx(ap(q), ap(s), ap(i)), "quant")
+
+    def mm(o, l, r, start=True, stop=True):
+        lq, ls, rq, rs = A(l[0] + "q", l[1], l[2]), A(l[0] + "s", l[1], l[2]), A(r[0] + "q", r[1], r[2]), A(r[0] + "s", r[1], r[2])
+        x = A(o, 0, r[2] - r[1])
+        return do("T", [lq, ls, rq, rs], [x], lambda: g.tensor.matmul_mx(ap(x), ap(lq), ap(ls), ap(rq), ap(rs), start, stop))
+
+    def pick_codes(o, i, off):
+        do("V", [i, off], [o], lambda: V.tensor_copy(ap(o).bitcast(dt.uint32), ap(i).bitcast(dt.uint32).indirect(ap(off))), "pick")
+
+    def pick_s(o, i, off):
+        do("S", [i, off], [o], lambda: S.activation(ap(o), ap(i).indirect(ap(off)), Act.Copy), "pick")
+
+    def pick_v(o, i, off):
+        do("V", [i, off], [o], lambda: V.tensor_copy(ap(o), ap(i).indirect(ap(off))), "pick")
+
+    def iota(o, pattern, base, cm):
+        if SCRATCH[o[0]][2] != I32:
+            do("G", [], [o], lambda: g.iota(ap(o), pattern, base, cm, allow_small_or_imprecise_dtypes=True))
+        else:
+            do("G", [], [o], lambda: g.iota(ap(o), pattern, base, cm))
+
+    def sel(o, i, pattern, op, base, cm):
+        do("G", [i], [o], lambda: g.affine_select(ap(o), ap(i), pattern, op, 0.0, base, cm))
+
+    L = 32
+
+    def whole(n, c):
+        return A(n, 0, c)
+
+    def Z(n, c0, c1, step=1):
+        return A(n, c0, c1, step, 0, L)
+
+    def cf(k, p1=128):
+        return A("cf", k, k + 1, 1, 0, p1)
+
+    dma("Y", T.ct[:, :], T.c[:, :], "lc", [], [whole("ct", 4 * P)])
+    dma("S", T.ut[:, 0:16], T.u[:, 0:16], "lu", [], [whole("ut", 16)])
+    dma("Y", T.wt[:, :], T.w[:, :], "lw", [whole("ct", 4 * P)], [whole("wt", 512)])
+
+    fill(whole("zz", 544), 0.0)
+    fill(whole("thn", P), -TINY)
+    fill(whole("oneb", P), 1.0)
+    fill(whole("zf", P), 0.0)
+    iota(A("ic", 0, 1), [[0, 1]], 0, 1)
+    iota(whole("er", 256), [[0, 8], [1, 16], [16, 2]], 0, 0)
+    for h in range(2):
+        sel(whole("th%d" % h, P), whole("thn", P), [[-1, P]], Op.is_gt, 64 * h, 1)
+    zero = whole("zz", 512)
+    for x in (A("kst", 0, 512), A("st", 0, 512), A("kst", 512, 1024), A("kst", 1536, 2048)):
+        act(x, zero, Act.Copy)
+    act(A("kst", 1024, 1536), zero, bias=-BIG)
+    for x in (whole("wft", 512), whole("mt", 512)):
+        act(x, zero, Act.Copy)
+    ts(A("ic", 1, 2), A("ic", 0, 1), 112, None, Op.bitwise_and)
+    ts(A("ic", 2, 3), A("ic", 0, 1), 15, None, Op.bitwise_and)
+    copy(A("cf", 0, 2), A("ic", 1, 3))
+    ts(cf(2), cf(0), 64.0, None, Op.add)
+    copy(cf(3), cf(1))
+    fill(A("cf", 2, 4, 1, 0, 64), 0.0)
+    for e, k in ((0, 0), (6, 0), (8, 1), (14, 1)):
+        copy(A("kst", e, e + 2), A("cf", k, 4, 2))
+    quant("kc", 0, 128, A("kst", 0, 512))
+
+    def query(t):
+        for b in range(4):
+            one = A("ut", 4 * t + b, 4 * t + b + 1)
+            if t == 0 and b < 2:
+                ts(A("ub", 512 + b, 1280, 4), A("oneb", 0, P), one, None, Op.mult)
+            else:
+                act(A("ub", 512 + b, 1280, 4), whole("zf", P), bias=one)
+        for b in range(4):
+            one = A("ut", 4 * t + b, 4 * t + b + 1)
+            ts(A("ub", b, 512, 4), A("oneb", 0, 128), one, -1.0, Op.mult, Op.mult)
+        quant("u%d" % t, 0, 320, whole("ub", 1280))
+
+    query(0)
+    quant("x0", 0, P, whole("ct", 4 * P))
+    fill(A("cmt", 2, 4 * P, 4), 0.0)
+    fill(A("cmt", 3, 4 * P, 4), 0.0)
+    for t in range(R):
+        quant("v%d" % t, P + K, P + 160, zero)
+    fill(Z("one32", 0, 32), 1.0)
+    fill(Z("pm", 0, 1), LOW)
+    fill(Z("ne", 32, 64), 0.0)
+    fill(Z("d0", 0, 32), 1.0)
+    fill(Z("d0", 32, 33), -1.0)
+    fill(Z("d0", 48, 64), 0.0)
+    fill(Z("d1", 32, 48), 0.0)
+    iota(whole("cw", 256), [[0, 8], [1, 16], [0, 2]], 1, 0)
+    iota(whole("mw", 16), [[1, 16]], 0, 0)
+    iota(Z("nk", 0, 16), [[-1, 16]], 0, 0)
+    iota(whole("mwb", 12), [[2, 12]], -12, 0)
+    sel(A("st", 0, 512, 4), A("oneb", 0, 128), [[-1, 128]], Op.is_equal, 0, 1)
+    iota(whole("rb", 128), [[0, 8], [1, 4], [0, 4]], 0, 0)
+    iota(Z("m8", 0, 8), [[1, 8]], 0, 0)
+    sel(Z("up32", 0, 32), Z("one32", 0, 32), [[1, 32]], Op.is_gt, 0, -1)
+    sel(Z("eye32", 0, 32), Z("one32", 0, 32), [[1, 32]], Op.is_equal, 0, -1)
+    JT, ONES, NEG, W1 = ("kc", 0, 128), ("kc", 128, 256), ("kc", 256, 384), ("kc", 384, 512)
+
+    def columns():
+        for k, m in ((3, 3), (4, 31), (6, 16)):
+            ts(A("ic", k, k + 1), A("ic", 0, 1), m, None, Op.bitwise_and)
+        ts(A("ic", 5, 6), A("ic", 4, 5), 2, None, Op.arith_shift_right)
+        fill(A("kst", 512, 1024, 4), 1.0)
+        fill(A("kst", 513, 1024, 4, 64, 128), 1.0)
+        copy(A("cf", 4, 8), A("ic", 3, 7))
+        ts(cf(10), cf(1), 1.0, None, Op.add)
+        ts(cf(9), cf(7), 224.0, None, Op.add)
+        ts(cf(11), cf(5), -BIG, None, Op.mult)
+        ts(cf(12), cf(5), -1.0, -0.5, Op.mult, Op.add)
+        for b in range(2):
+            ts(Z("kst", 1536 + b, 2048, 4), Z("rb", 0, 128), cf(4, L), None, Op.is_equal)
+        quant("kc", 128, 512, A("kst", 512, 2048))
+
+    def decoders():
+        for b in range(1, 4):
+            act(A("st", 512 * b + b, 512 * b + 512, 4), A("st", 0, 512, 4), Act.Copy)
+        quant("eb", 0, 512, whole("st", 2048))
+
+    def later():
+        ts(Z("d16", 0, 8), Z("m8", 0, 8), cf(6, L), 16.0, Op.is_equal, Op.mult)
+        ts(Z("dm", 0, 8), Z("m8", 0, 8), cf(6, L), -16000.0, Op.not_equal, Op.mult)
+        ts(Z("dm", 0, 8), Z("dm", 0, 8), -1.0, None, Op.add)
+        fill(A("wft", 0, 512, 4, 32, 33), 1.0)
+        ts(A("wft", 2, 512, 4, 32, 33), A("cw", 0, 256, 2, 32, 33), -1.0, None, Op.add)
+        ts(A("zz", 32, 80, 4, 32, 33), A("mw", 0, 12, 1, 32, 33), 16.0, None, Op.mult)
+        fill(A("zz", 34, 80, 4, 32, 33), 1.0)
+
+    def place(t, part):
+        c = "sc%d" % t
+
+        def sc(k):
+            return Z(c, k, k + 1)
+        if part == 1:
+            ts(sc(23), sc(1), 1.0, sc(9), Op.subtract, Op.mult)
+            ts(sc(24), sc(5), -0.5, None, Op.mult)
+            ts(sc(25), sc(5), -97.0, sc(23), Op.mult, Op.add)
+            tt(Z("dg", 0, 32), Z("cr%d" % t, 0, 32), Z("eye32", 0, 32), Op.mult)
+            red(sc(20), Z("dg", 0, 32), Op.add)
+            act(Z("js5", 0, P), Z("gi%d" % t, 0, P), Act.Sign, bias=sc(20), scale=-1.0 / BIG, acc=sc(22))
+        else:
+            act(Z("tgb", t, t + 1), sc(22), scale=sc(24), bias=sc(25))
+            dma("Y", T.tg[t:t + 1, :], T.tgb[0:L, t:t + 1], "tg_%d" % t, [Z("tgb", t, t + 1)], [])
+
+    for t in range(R):
+        x, v, n, u, nx, c, cr, gi = "x%d" % t, "v%d" % t, "n%d" % t, "u%d" % t, "x%d" % (t + 1), "sc%d" % t, "cr%d" % t, "gi%d" % t
+        last = t == R - 1
+
+        def sc(k):
+            return Z(c, k, k + 1)
+
+        def sca(k):
+            return A(c, k, k + 1)
+        pair = []
+        for h in range(2):
+            pair.append(mm("b%d" % h, (x, 64 * h, 64 * h + 128), (u, 128, 320), True, False))
+            pair.append(mm("b%d" % h, (u, 0, 128), (x, 0, P), False, True))
+        pair[2]["after"].setdefault(pair[1]["n"], False)
+        if t > 0:
+            place(t - 1, 1)
+        tt(A("cmt", 0, 4 * P, 4), A("b0", 0, P), whole("th0", P), Op.is_gt)
+        if t == 0:
+            for b in (1, 2, 3):
+                act(A("st", 512 * b, 512 * b + 512), A("kst", 0, 512), Act.Copy, scale=0.0)
+        for h in range(2):
+            if h == 1:
+                tt(A("cmt", 1, 4 * P, 4), A("b1", 0, P), whole("th1", P), Op.is_gt)
+            scan(A("rk%d" % h, 0, P), A("cmt", h, 4 * P, 4), A("zz", 80, 80 + P), 0.0, Op.add, Op.add)
+            ts(A("et", h, 512, 2), whole("er", 256), A("rk%d" % h, P - 1, P), None, Op.is_equal)
+        quant("e", 0, 128, whole("et", 512))
+        mm("b2", ("e", 0, 128), JT)
+        quant("cm", 0, P, whole("cmt", 4 * P))
+        for m in range(2):
+            ts(A("ol", m, m + 1), A("b2", m, m + 1), A("b2", m + 2, m + 3), None, Op.add)
+        pick_codes(A(n + "q", 0, K), A(x + "q", 0, P), A("ol", 0, 2))
+        pick_s(A(n + "s", 0, K), A(x + "s", 0, P), A("ol", 0, 2))
+        dst = T.cores[rank ^ (1 << t)]
+        rid, pid = topo.addr(dst, core)
+        mask, en = topo.mask(core, dst), len(topo.engines(core, dst))
+        to = (T.sem["arr%d" % t], T.sem["sent%d" % t], pid, rid, mask)
+        vq, nq, vs, ns = T[v + "q"][:, P:P + K], T[n + "q"][:, 0:K], T[v + "s"][:, P:P + K], T[n + "s"][:, 0:K]
+        m1 = add("G", [A(n + "q", 0, K)], [], ISSUE, ISSUE, lambda vq=vq, nq=nq, to=to: g.remote_dma(vq.bitcast(dt.uint8), nq.bitcast(dt.uint8), *to), "sent%d" % t, 2 * en)
+        m2 = add("G", [A(n + "s", 0, K)], [], ISSUE, ISSUE, lambda vs=vs, ns=ns, to=to: g.remote_dma(vs, ns, *to), "sent%d" % t, 2 * en)
+        m2["after"][m1["n"]] = False
+        fly = add("arrive", [], [A(v + "q", P, P + K), A(v + "s", P, P + K)], FLIGHT, FLIGHT, None, "arr%d" % t, 2 * en)
+        fly["after"].update({m1["n"]: False, m2["n"]: False})
+        dma("Y", T[v + "q"][:, 0:P].bitcast(dt.uint8), T[x + "q"][:, 0:P].bitcast(dt.uint8), "cq%d" % t, [A(x + "q", 0, P)], [A(v + "q", 0, P)])
+        dma("Y", T[v + "s"][:, 0:P], T[x + "s"][:, 0:P], "cs%d" % t, [A(x + "s", 0, P)], [A(v + "s", 0, P)])
+        if t == 0:
+            columns()
+            decoders()
+        mm("b4", ONES, ("cm", 0, P))
+        ts(A("mkt", 0, 4 * P, 4), A("b4", 0, P), 159.5, BIG, Op.is_gt, Op.mult)
+        copy(A("mkt", 1, 4 * P, 4), A("mkt", 0, 4 * P, 4))
+        act(A("mkt", 2, 4 * P, 4), A("mkt", 0, 4 * P, 4), Act.Copy)
+        copy(A("mkt", 3, 4 * P, 4), A("mkt", 0, 4 * P, 4))
+        scan(A(gi, 0, P), A("mkt", 0, 4 * P, 4), A("zz", 80, 80 + P), cf(11), Op.add, Op.add)
+        quant("mk", 0, P, whole("mkt", 4 * P))
+        act(A("js0", 0, 12), A(gi, 15, P, 16), Act.Sign, bias=0.5, scale=-1.0 / BIG, acc=sca(10))
+        act(A("js1", 0, P), A(gi, 0, P), Act.Sign, bias=0.5, scale=-1.0 / BIG, acc=sca(11))
+        if t == 0:
+            later()
+        for b in range(4):
+            bank = ("b6", "b7", "b0", "b1")[b]
+            mm(bank, ("eb", 128 * b, 128 * b + 128), (x, 0, P))
+            act(A("hd", b, 4 * P, 4), A(bank, 0, P), Act.Copy, scale=0.5)
+        for k in range(3):
+            mm("b5", NEG, ("mk", 0, P), k == 0, False)
+        ts(A("ohb", 0, 12), A("mwb", 0, 12), sca(10), None, Op.is_equal)
+        ts(Z("ohh", 0, 12), Z("mwb", 0, 12), sc(10), 0.5, Op.is_equal, Op.mult)
+        ts(sc(12), sc(10), -8.0, 112.0, Op.mult, Op.add)
+        ts(sca(13), sca(10), -16.0, sca(11), Op.mult, Op.add)
+        ts(sca(14), sca(13), 0.5, 1.0, Op.mult, Op.add)
+        ts(sc(15), sc(13), -0.5, 16.0, Op.mult, Op.add)
+        ts(sca(16), sca(13), -0.5, None, Op.mult)
+        ts(A("wft", 1, 512, 2), whole("cw", 256), sca(14), None, Op.is_equal)
+        act(A("zz", 35, 80, 4, 64, 96), A("ohb", 0, 12, 1, 64, 96), scale=A(c, 16, 17, 1, 64, 96))
+        ts(Z("d0", 33, 48), Z("mw", 1, 16), sc(15), None, Op.is_lt)
+        ts(Z("d1", 48, 64), Z("nk", 0, 16), sc(15), 0.0, Op.add, Op.max)
+        if t == 0:
+            quant("w", 0, 128, whole("wt", 512))
+        if not last:
+            query(t + 1)
+        else:
+            mm("b2", ("w", 0, 128), (x, 0, P))
+            act(A("yw", 0, P), A("b2", 0, P), Act.Copy)
+        if t > 0:
+            place(t - 1, 2)
+
+        mm("b5", (v, P, P + 128), (x, 0, P), False, True)
+        for b in range(4):
+            mm(("b6", "b7", "b4", "b1")[b], ("eb", 128 * b, 128 * b + 128), (v, P, P + 128))
+
+        def half(b):
+            act(A("ha", b, 128, 4), A(("b6", "b7", "b4", "b1")[b], 0, K), Act.Copy, scale=0.5)
+        scan(Z("pm", 1, 1 + P), A("b5", 0, P, 1, 0, L), Z("zf", 0, P), LOW, Op.max, Op.add)
+        top = Z("pm", P, P + 1)
+        half(0)
+        act(Z("js2", 0, 1 + P), Z("pm", 0, 1 + P), Act.Sign, bias=top, scale=-1.0, acc=sc(1))
+        act(Z("js3", 0, 12), Z("pm", 16, 1 + P, 16), Act.Sign, bias=top, scale=-1.0, acc=sc(0))
+        act(Z("tb", 0, 32), Z("up32", 0, 32), scale=sc(1))
+        act(sc(3), sc(0), scale=-16.0, bias=sc(1))
+        act(Z("zz", 0, 32, 4), Z("d16", 0, 8), scale=sc(0))
+        ts(Z("oha", 0, 12), Z("mw", 0, 12), sc(0), None, Op.is_equal)
+        act(sc(2), sc(0), scale=-16.0, bias=cf(9, L))
+        act(Z("xa", 0, 24, 2), Z("oha", 0, 12), scale=sc(2))
+        act(sc(4), sc(3), scale=-1.0, bias=cf(10, L))
+        half(1)
+        act(Z("xa", 1, 24, 2), Z("oha", 0, 12), scale=sc(4))
+        half(2)
+        half(3)
+        ts(Z("zz", 1, 32, 4), Z("dm", 0, 8), sc(3), 0.0, Op.add, Op.max)
+        turn(Z("tt", 0, 32), Z("tb", 0, 32))
+        quant("xo", 0, 128, A("zz", 0, 512))
+        mm("b3", W1, ("xo", 0, 128))
+        ts(Z("ne", 0, 32), Z("tt", 0, 32), sc(1), None, Op.is_equal)
+        ts(Z("wft", 0, 512, 2), Z("cw", 0, 256), sc(3), None, Op.is_equal)
+        scan(Z("ms", 0, 64), Z("ne", 0, 64), Z("zf", 0, 64), 0.0, Op.max, Op.max)
+        act(sc(9), Z("ms", 31, 32), scale=-1.0, bias=1.0)
+        act(sc(5), Z("ms", 31, 32))
+        act(Z("zz", 32, 80, 2), Z("xa", 0, 24), scale=sc(9))
+        quant("wf", 0, 128, whole("wft", 512))
+        ts(A("om", 0, 8), A("b3", 0, 8), 4.0, cf(4), Op.mult, Op.add)
+        turn(Z("d1", 0, 32), Z("ms", 32, 64))
+        scan(Z(cr, 0, 64), Z("d0", 0, 64), Z("d1", 0, 64), cf(12, L), Op.mult, Op.add)
+        act(Z("js4", 0, 64), Z(cr, 0, 64), Act.Sign, scale=-1.0, acc=sc(7))
+        ts(sc(6), Z(cr, 31, 32), 0.0, sc(12), Op.is_gt, Op.mult)
+        ts(Z("zz", 33, 80, 4), Z("ohb", 0, 12), sc(6), None, Op.mult)
+        act(Z("zz", 35, 80, 4), Z("ohh", 0, 12), scale=sc(7))
+        quant("xf", 0, 128, A("zz", 32, 544))
+        mm("b2", ("wf", 0, 128), ("xf", 0, 128))
+        ho, hi_, of, ha = A("mt", 0, 128), A("hd", 0, 4 * P), A("om", 0, 8), A("ha", 0, 128)
+        do("V", [hi_, of, ha], [ho], lambda: V.tensor_tensor(ap(ho), ap(hi_).indirect(ap(of)), ap(ha), Op.add), "pick")
+        quant(v, P + K, P + 160, whole("mt", 512))
+        copy(A("of", 0, 12), A("b2", 0, 12))
+        if not last:
+            for a, b in ((0, 8), (8, 12)):
+                pick_codes(A(nx + "q", 16 * a, 16 * b), A(v + "q", 0, 256), A("of", a, b))
+                pick_s(A(nx + "s", 16 * a, 16 * b), A(v + "s", 0, 256), A("of", a, b))
+        else:
+            mm("b3", ("w", 0, 128), (v, P, P + 128))
+            act(A("yw", P, P + 64), A("b3", 0, 64), Act.Copy)
+            for a, b in ((0, 6), (6, 12)):
+                pick_codes(A(nx + "q", 16 * a, 16 * b), A(v + "q", 0, 256), A("of", a, b))
+            pick_s(A("yo", 0, P), A("yw", 0, 256), A("of", 0, 12))
+            dma("Y", T.oc[:, :], T.x3q[:, 0:P].bitcast(dt.uint8), "oc_", [A("x3q", 0, P)], [])
+            dma("S", T.y[:, :], T.yo[:, 0:P], "oy_", [A("yo", 0, P)], [])
+            pick_v(A(nx + "s", 0, 96), A(v + "s", 0, 256), A("of", 0, 6))
+            pick_s(A(nx + "s", 96, P), A(v + "s", 0, 256), A("of", 6, 12))
+            for k in range(4):
+                dma("Y", T.osc[4 * k:4 * k + 4, :], T.x3s[32 * k:32 * k + 4, 0:P], "os%d" % k, [A("x3s", 0, P)], [])
+            place(t, 1)
+            place(t, 2)
+    emit()

@@ -1,12 +1,17 @@
 from concourse.mybir import dt, AluOpType as Op, AxisListType, ActivationFunctionType as Act
 
 N, P, K, R = 8, 192, 32, 3
-TINY = 1e-30
+CAND = (2,)
+TINY = 2.0 ** -100
 BIG = 2.0 ** 30
 LOW = -1e29
-WAKE, SLACK = 0.18, 0.3
-LOAD, ISSUE, FLIGHT = 1.1, 0.4, 1.0
-MMC = 0.0012
+ADD = (2,)
+HUGE = 2.0 ** 80
+XF, Z0 = 160, 208
+ORDER = """
+2 1 40 39 5 0 18 17 14 19 6 21 3 23 27 20 4 61 65 41 37 22 59 9 62 57 8 7 42 38 43 44 11 46 47 45 53 24 10 36 48 12 169 167 25 29 26 92 28 33 13 31 30 32 168 67 68 69 70 71 98 105 96 89 87 16 88 15 52 51 50 49 73 72 74 75 171 76 34 77 99 64 113 35 116 106 91 170 95 121 63 97 78 83 102 136 79 80 101 81 111 82 94 137 147 148 139 110 84 85 123 108 60 66 145 104 151 142 138 172 140 103 54 141 86 143 93 90 144 107 146 176 173 149 153 154 155 177 174 156 159 175 161 162 158 254 252 152 255 100 160 257 253 181 179 178 165 256 182 183 180 163 166 261 157 258 184 164 187 189 203 186 56 109 55 117 58 185 195 188 118 122 114 204 198 206 211 205 212 199 196 197 190 192 194 150 193 207 191 124 200 208 213 209 214 210 216 215 201 217 259 244 202 125 218 219 245 220 221 222 223 224 225 226 227 242 241 120 112 443 126 127 128 260 243 132 115 129 133 130 228 291 262 263 264 265 246 292 229 230 232 231 233 234 235 293 294 240 266 282 236 237 267 238 239 313 270 297 298 247 248 131 134 119 268 283 286 284 269 295 285 288 271 249 287 272 290 289 296 315 277 273 274 299 300 301 323 304 302 317 319 305 303 307 306 308 309 310 275 316 318 320 328 135 351 312 325 327 326 324 329 321 311 343 330 276 352 333 331 332 278 334 342 354 372 344 336 340 341 355 356 345 374 373 279 322 335 353 375 346 360 281 357 347 358 338 280 365 361 363 364 359 362 348 367 377 376 339 380 366 368 337 369 370 371 379 381 408 393 394 250 350 382 385 378 411 395 412 396 397 399 383 384 410 398 402 400 386 387 401 403 409 405 406 413 414 415 404 388 407 419 349 251 392 390 389 391 417 420 446 418 314 447 416 421 422 423 435 430 428 424 426 431 427 448 451 433 432 437 453 436 434 454 450 468 425 452 444 449 438 441 442 455 456 440 459 457 458 460 467 462 429 445 461 475 470 476 439 471 478 477 469 464 466 463 465 480 479 483 472 484 473 481 485 488 486 482 487 474 509 489 492 510 506 507 508 511 493 512 513 490 491 497 494 495 498 500 501 496 499 503 505 502 504
+"""
+MOVE = {}
 
 MXC, U8, F32, BF, I32, U16 = "float8_e4m3fn_x4", "uint8", "float32", "bfloat16", "int32", "uint16"
 SCRATCH = {}
@@ -26,29 +31,35 @@ for _t in range(R):
     _pair("v%d" % _t, P + 160)
     _pair("n%d" % _t, K)
     _pair("u%d" % _t, 320)
-    _buf("sc%d" % _t, 32, F32)
+    _buf("sc%d" % _t, 48, F32)
     _buf("cr%d" % _t, 64, F32)
     _buf("gi%d" % _t, P, BF)
+    if _t in CAND:
+        _pair("cd%d" % _t, 224)
 _pair("x3", P)
-for _n, _c in (("w", 128), ("eb", 512), ("kc", 512), ("e", 128), ("cm", P), ("mk", P), ("xo", 128), ("wf", 128), ("xf", 128)):
+for _n, _c in (("w", 128), ("eb", 512), ("kc", 512), ("e", 128), ("cm", P), ("mk", P), ("xo", 128), ("wf", 128), ("xf", 128),
+               ("uu", P), ("c2", 128), ("wk", 256)):
     _pair(_n, _c)
-for _n, _c in (("ct", 4 * P), ("ut", 16), ("wt", 512), ("ub", 1280), ("st", 2048), ("kst", 2048), ("et", 512), ("cmt", 4 * P),
-               ("mkt", 4 * P), ("zz", 544), ("wft", 512), ("mt", 512), ("oneb", P), ("er", 256), ("cw", 256), ("rb", 128), ("rk0", P), ("rk1", P)):
+for _n, _c in (("ct", 4 * P), ("ut", 16), ("wt", 512), ("ub", 1280), ("st", 520), ("ng", 512), ("k1", 512), ("et", 512), ("cmt", 4 * P),
+               ("mkt", 4 * P), ("zz", Z0 + 4 * P), ("wft", 512), ("mt", 512), ("oneb", 512), ("er", 256), ("cw", 256), ("rb", 128),
+               ("rk", 2 * P), ("th", 3 * P), ("up32", 32), ("cm2", 4 * P), ("uut", 840), ("c2t", 512), ("wc", 512),
+               ("kr", P), ("sg", 3 * P), ("jk", 2240)):
     _buf(_n, _c, BF)
-for _n, _c in (("th0", P), ("th1", P), ("thn", P), ("zf", P), ("one32", 32), ("up32", 32), ("eye32", 32), ("mw", 16), ("mwb", 16), ("m8", 8),
-               ("nk", 16), ("d0", 64), ("d1", 64), ("ms", 64), ("d16", 8), ("dm", 8), ("cf", 16), ("ohb", 16), ("ohh", 16), ("oha", 16),
-               ("pm", 200), ("tb", 32), ("tt", 32), ("ne", 64), ("dg", 32), ("xa", 24), ("hd", 4 * P), ("ha", 128),
-               ("yw", 256), ("yo", P), ("tgb", 16), ("js0", 16), ("js1", P), ("js2", 200), ("js3", 16), ("js4", 64), ("js5", P)):
+for _n, _c in (("mw", 16), ("mwb", 16), ("nk", 16), ("d0", 64), ("d1", 64), ("ms", 64), ("d16", 40), ("dm", 40), ("cf", 24), ("oh", 48),
+               ("zm", P), ("pm", 216), ("tb", 64), ("ne", 64), ("dg", 40), ("xa", 24), ("hd", 4 * P), ("ha", 128),
+               ("yw", 256), ("yo", P), ("tgb", 16), ("kb", 32), ("pl", 96), ("bc", 96), ("hq", 40), ("th2", 128)):
     _buf(_n, _c, F32)
 _buf("ic", 16, I32)
 _buf("ol", 2, U16)
 _buf("om", 8, U16)
 _buf("of", 12, U16)
+_buf("oo", 4, U16)
 for _n in range(8):
     _buf("b%d" % _n, 512, F32, "psum")
+SHARE = {"rk0": ("rk", 0), "rk1": ("rk", P), "th0": ("th", 0), "th1": ("th", P), "thn": ("th", 2 * P), "go": ("sg", P), "mr": ("sg", 2 * P),
+         "ohb": ("oh", 0), "ohh": ("oh", 16), "oha": ("oh", 32), "tt": ("tb", 32), "lr": ("bc", 32)}
 
-SEMAPHORES = ["sv", "ss", "stn", "sg", "lc", "lu", "lw", "oc_", "oy_"] + ["os%d" % k for k in range(4)] + ["tg_%d" % k for k in range(R)] \
-    + ["arr%d" % k for k in range(R)] + ["sent%d" % k for k in range(R)] + ["cq%d" % k for k in range(R)] + ["cs%d" % k for k in range(R)]
+SEMAPHORES = ["sv", "ss", "stn", "sg"] + ["dm%d" % k for k in range(48)] + ["arr%d" % k for k in range(R)] + ["sent%d" % k for k in range(R)]
 
 
 def _cross(a, b):
@@ -66,48 +77,6 @@ def _within(a, b):
     return a[5] == 1 or (a[5] == b[5] and (a[3] - b[3]) % a[5] == 0)
 
 
-def _size(x):
-    return (x[4] - x[3] + x[5] - 1) // x[5]
-
-
-def _order(nodes):
-    users = [[] for m in nodes]
-    for m in nodes:
-        for d in m["after"]:
-            users[d].append(m["n"])
-    way = [0.0] * len(nodes)
-    for m in reversed(nodes):
-        way[m["n"]] = max([m["late"]] + [m["late"] + WAKE * nodes[k]["after"][m["n"]] + way[k] for k in users[m["n"]]])
-    left = [len(m["after"]) for m in nodes]
-    ready = [0.0] * len(nodes)
-    free = {}
-    able = [m["n"] for m in nodes if not m["after"]]
-    done = []
-    while able:
-        best = None
-        for q in set(nodes[k]["q"] for k in able):
-            ks = [k for k in able if nodes[k]["q"] == q]
-            t0 = max(free.get(q, 0.0), min(ready[k] for k in ks))
-            ks = [k for k in ks if ready[k] <= t0 + SLACK]
-            k = max(ks, key=lambda i: (way[i], -i))
-            now = [i for i in ks if ready[i] <= t0 and t0 + 1.8 * nodes[i]["busy"] <= ready[k] + 0.02]
-            if ready[k] > t0 and now:
-                k = max(now, key=lambda i: (way[i], -i))
-            t = max(t0, ready[k])
-            if best is None or (t, q) < best[:2]:
-                best = (t, q, k)
-        t, q, k = best
-        able.remove(k)
-        free[q] = t + nodes[k]["busy"]
-        done.append(k)
-        for i in users[k]:
-            ready[i] = max(ready[i], t + nodes[k]["late"] + (WAKE if nodes[i]["after"][k] else 0.0))
-            left[i] -= 1
-            if not left[i]:
-                able.append(i)
-    return done
-
-
 def rank_program(g, core, T, topo):
     rank = T.rank_of(core)
     if rank is None:
@@ -116,9 +85,11 @@ def rank_program(g, core, T, topo):
     own = {"V": "sv", "S": "ss", "T": "stn", "G": "sg"}
     log = {}
     nodes = []
+    dmas = [0]
 
     def A(name, c0, c1, step=1, p0=0, p1=128):
-        return (name, p0, p1, c0, c1, step)
+        name, at = SHARE.get(name, (name, 0))
+        return (name, p0, p1, at + c0, at + c1, step)
 
     def ap(x):
         return T[x[0]][x[1]:x[2], x[3]:x[4]:x[5]] if x[5] > 1 else T[x[0]][x[1]:x[2], x[3]:x[4]]
@@ -126,9 +97,9 @@ def rank_program(g, core, T, topo):
     def psum(x):
         return SCRATCH[x[0]][0] == "psum"
 
-    def add(q, reads, writes, busy, late, issue, sem=None, val=0):
+    def add(q, reads, writes, kind, issue, sem=None, val=0):
         after = {}
-        node = {"q": q, "n": len(nodes), "after": after, "busy": busy, "late": late, "issue": issue, "sem": sem, "val": val}
+        node = {"q": q, "n": len(nodes), "after": after, "k": kind, "r": reads, "w": writes, "issue": issue, "sem": sem, "val": val}
         for views, w in ((reads, False), (writes, True)):
             for x in views:
                 for y, m, yw in log.get(x[0], []):
@@ -147,30 +118,17 @@ def rank_program(g, core, T, topo):
         nodes.append(node)
         return node
 
-    def do(q, reads, writes, call, kind=""):
-        n = max(_size(x) for x in reads[:1] + writes[:1])
-        if kind == "quant":
-            cost = 0.015 + 0.000275 * _size(reads[0])
-        elif kind == "pick":
-            cost = 0.07 + 0.0016 * _size(writes[0])
-        elif q == "T":
-            cost = MMC * (_size(writes[0]) + 16)
-        elif q == "G":
-            cost = 0.2 + 0.002 * n
-        else:
-            two = q == "V" and all(SCRATCH[x[0]][2] in (BF, U16) for x in reads[:1] + writes[:1])
-            cost = max(64, n * (0.5 if two else 1)) * 0.00104
-        return add(q, reads, writes, cost, cost, call)
-
-    def dma(q, out, in_, sem, reads, writes):
-        add(q, reads, writes, 0.1, LOAD, lambda: queue[q].dma_start(out, in_), sem, 16)
+    def dma(q, out, in_, reads, writes, size):
+        dmas[0] += 1
+        return add(q, reads, writes, ("dma", size), lambda: queue[q].dma_start(out, in_), "dm%d" % (dmas[0] - 1), 16)
 
     def emit():
         count = {"V": 0, "S": 0, "T": 0, "G": 0}
         known = {q: {} for q in queue}
         every = {}
-        done = _order(nodes)
+        done = [int(k) for k in ORDER.split()]
         at = {k: i for i, k in enumerate(done)}
+        assert sorted(done) == list(range(len(nodes))) and all(at[d] < at[m["n"]] for m in nodes for d in m["after"])
         for k in done:
             m = nodes[k]
             q = m["q"]
@@ -191,9 +149,9 @@ def rank_program(g, core, T, topo):
                 if m["sem"][0:4] != "sent":
                     ins.then_inc(T.sem[m["sem"]], 16)
             m["clock"] = dict(known.get(q, {}))
-            every[m["sem"]] = max(m["val"], every.get(m["sem"], 0))
-        final = ["sg", "stn", "ss", "sv"] + ["os%d" % k for k in range(4)] + ["tg_%d" % (R - 1), "oc_", "oy_"]
-        for s in [e for e in every if e not in final] + final:
+            every.pop(m["sem"], None)
+            every[m["sem"]] = m["val"]
+        for s in every:
             g.wait_ge(T.sem[s], every[s])
 
     V, S = g.vector, g.scalar
@@ -202,64 +160,88 @@ def rank_program(g, core, T, topo):
         return ap(s) if isinstance(s, tuple) else s
 
     def fill(x, v):
-        do("V", [], [x], lambda: V.memset(ap(x), v))
+        add("V", [], [x], "fill", lambda: V.memset(ap(x), v))
 
     def copy(o, i):
-        do("V", [i], [o], lambda: V.tensor_copy(ap(o), ap(i)))
+        add("V", [i], [o], "v", lambda: V.tensor_copy(ap(o), ap(i)))
 
     def ts(o, i, s1, s2, op0, op1=None):
         rd = [i] + [s for s in (s1, s2) if isinstance(s, tuple)]
         if op1 is None:
-            do("V", rd, [o], lambda: V.tensor_scalar(ap(o), ap(i), val(s1), None, op0))
+            add("V", rd, [o], "v", lambda: V.tensor_scalar(ap(o), ap(i), val(s1), None, op0))
         else:
-            do("V", rd, [o], lambda: V.tensor_scalar(ap(o), ap(i), val(s1), val(s2), op0, op1))
+            add("V", rd, [o], "v", lambda: V.tensor_scalar(ap(o), ap(i), val(s1), val(s2), op0, op1))
 
     def tt(o, i0, i1, op):
-        do("V", [i0, i1], [o], lambda: V.tensor_tensor(ap(o), ap(i0), ap(i1), op))
+        add("V", [i0, i1], [o], "tt", lambda: V.tensor_tensor(ap(o), ap(i0), ap(i1), op))
 
-    def red(o, i, op):
-        do("V", [i], [o], lambda: V.tensor_reduce(ap(o), ap(i), AxisListType.X, op))
+    def red(o, i, op, size=False):
+        if size:
+            add("V", [i], [o], "red", lambda: V.tensor_reduce(ap(o), ap(i), AxisListType.X, op, apply_absolute_value=True))
+        else:
+            add("V", [i], [o], "red", lambda: V.tensor_reduce(ap(o), ap(i), AxisListType.X, op))
 
     def scan(o, d0, d1, init, op0, op1):
         rd = [d0, d1] + ([init] if isinstance(init, tuple) else [])
-        do("V", rd, [o], lambda: V.tensor_tensor_scan(ap(o), ap(d0), ap(d1), val(init), op0, op1))
+        add("V", rd, [o], "scan", lambda: V.tensor_tensor_scan(ap(o), ap(d0), ap(d1), val(init), op0, op1))
 
     def turn(o, i):
-        do("V", [i], [o], lambda: V.transpose(ap(o), ap(i)))
+        add("V", [i], [o], "v", lambda: V.transpose(ap(o), ap(i)))
 
     def act(o, i, f=Act.Identity, bias=0.0, scale=1.0, acc=None):
         rd = [i] + [s for s in (bias, scale) if isinstance(s, tuple)]
         if acc is None:
-            do("S", rd, [o], lambda: S.activation(ap(o), ap(i), f, bias=val(bias), scale=val(scale)))
+            add("S", rd, [o], "act", lambda: S.activation(ap(o), ap(i), f, bias=val(bias), scale=val(scale)))
         else:
-            do("S", rd, [o, acc], lambda: S.activation(ap(o), ap(i), f, bias=val(bias), scale=val(scale), accum_out=ap(acc)))
+            add("S", rd, [o, acc], "acc", lambda: S.activation(ap(o), ap(i), f, bias=val(bias), scale=val(scale), accum_out=ap(acc)))
+
+    def lin(tag, q, o, i, scale=1.0, bias=0.0):
+        if MOVE.get(tag, q) == "S":
+            act(o, i, scale=scale, bias=bias)
+        else:
+            ts(o, i, scale, bias, Op.mult, Op.add)
 
     def quant(n, c0, c1, i):
         q, s = A(n + "q", c0, c1), A(n + "s", c0, c1)
-        do("V", [i], [q, s], lambda: V.quantize_mx(ap(q), ap(s), ap(i)), "quant")
+        add("V", [i], [q, s], "quant", lambda: V.quantize_mx(ap(q), ap(s), ap(i)))
 
     def mm(o, l, r, start=True, stop=True):
         lq, ls, rq, rs = A(l[0] + "q", l[1], l[2]), A(l[0] + "s", l[1], l[2]), A(r[0] + "q", r[1], r[2]), A(r[0] + "s", r[1], r[2])
         x = A(o, 0, r[2] - r[1])
-        return do("T", [lq, ls, rq, rs], [x], lambda: g.tensor.matmul_mx(ap(x), ap(lq), ap(ls), ap(rq), ap(rs), start, stop))
+        return add("T", [lq, ls, rq, rs], [x], "mm", lambda: g.tensor.matmul_mx(ap(x), ap(lq), ap(ls), ap(rq), ap(rs), start, stop))
 
     def pick_codes(o, i, off):
-        do("V", [i, off], [o], lambda: V.tensor_copy(ap(o).bitcast(dt.uint32), ap(i).bitcast(dt.uint32).indirect(ap(off))), "pick")
+        add("V", [i, off], [o], "pick", lambda: V.tensor_copy(ap(o).bitcast(dt.uint32), ap(i).bitcast(dt.uint32).indirect(ap(off))))
 
-    def pick_s(o, i, off):
-        do("S", [i, off], [o], lambda: S.activation(ap(o), ap(i).indirect(ap(off)), Act.Copy), "pick")
-
-    def pick_v(o, i, off):
-        do("V", [i, off], [o], lambda: V.tensor_copy(ap(o), ap(i).indirect(ap(off))), "pick")
+    def pick(tag, q, o, i, off):
+        if MOVE.get(tag, q) == "S":
+            add("S", [i, off], [o], "pick", lambda: S.activation(ap(o), ap(i).indirect(ap(off)), Act.Copy))
+        else:
+            add("V", [i, off], [o], "pick", lambda: V.tensor_copy(ap(o), ap(i).indirect(ap(off))))
 
     def iota(o, pattern, base, cm):
         if SCRATCH[o[0]][2] != I32:
-            do("G", [], [o], lambda: g.iota(ap(o), pattern, base, cm, allow_small_or_imprecise_dtypes=True))
+            add("G", [], [o], "iota", lambda: g.iota(ap(o), pattern, base, cm, allow_small_or_imprecise_dtypes=True))
         else:
-            do("G", [], [o], lambda: g.iota(ap(o), pattern, base, cm))
+            add("G", [], [o], "iota", lambda: g.iota(ap(o), pattern, base, cm))
+
+    def const(tag, q, o, v):
+        if MOVE.get(tag, q) == "V":
+            fill(o, float(v))
+        else:
+            iota(o, [[0, (o[4] - o[3] + o[5] - 1) // o[5]]], v, 0)
 
     def sel(o, i, pattern, op, base, cm):
-        do("G", [i], [o], lambda: g.affine_select(ap(o), ap(i), pattern, op, 0.0, base, cm))
+        add("G", [i], [o], "sel", lambda: g.affine_select(ap(o), ap(i), pattern, op, 0.0, base, cm))
+
+    def move(o, i, q="Y"):
+        code = SCRATCH[o[0]][2] == MXC
+        n = (o[4] - o[3]) * {MXC: 4, U8: 1, BF: 2, F32: 4}[SCRATCH[o[0]][2]]
+        return dma(q, ap(o).bitcast(dt.uint8) if code else ap(o), ap(i).bitcast(dt.uint8) if code else ap(i), [i], [o], n)
+
+    def move_pair(o, a, i, b, n):
+        move(A(o + "q", a, a + n), A(i + "q", b, b + n))
+        move(A(o + "s", a, a + n), A(i + "s", b, b + n))
 
     L = 32
 
@@ -272,98 +254,130 @@ def rank_program(g, core, T, topo):
     def cf(k, p1=128):
         return A("cf", k, k + 1, 1, 0, p1)
 
-    dma("Y", T.ct[:, :], T.c[:, :], "lc", [], [whole("ct", 4 * P)])
-    dma("S", T.ut[:, 0:16], T.u[:, 0:16], "lu", [], [whole("ut", 16)])
-    dma("Y", T.wt[:, :], T.w[:, :], "lw", [whole("ct", 4 * P)], [whole("wt", 512)])
+    def zero(n, p0=0, p1=128):
+        return A("zz", Z0, Z0 + n, 1, p0, p1)
 
-    fill(whole("zz", 544), 0.0)
+    def junk(k, n, p0=0, p1=128):
+        return A("jk", 200 * k, 200 * k + n, 1, p0, p1)
+
+    lc = dma("Y", T.ct[:, :], T.c[:, :], [], [whole("ct", 4 * P)], 8 * P)
+    dma("S", T.ut[:, 0:16], T.u[:, 0:16], [], [whole("ut", 16)], 32)
+
+    fill(A("zz", Z0, Z0 + 4 * P), 0.0)
+    fill(A("zz", 0, Z0), 0.0)
     fill(whole("thn", P), -TINY)
-    fill(whole("oneb", P), 1.0)
-    fill(whole("zf", P), 0.0)
+    fill(whole("oneb", 512), 1.0)
     iota(A("ic", 0, 1), [[0, 1]], 0, 1)
     iota(whole("er", 256), [[0, 8], [1, 16], [16, 2]], 0, 0)
-    for h in range(2):
-        sel(whole("th%d" % h, P), whole("thn", P), [[-1, P]], Op.is_gt, 64 * h, 1)
-    zero = whole("zz", 512)
-    for x in (A("kst", 0, 512), A("st", 0, 512), A("kst", 512, 1024), A("kst", 1536, 2048)):
-        act(x, zero, Act.Copy)
-    act(A("kst", 1024, 1536), zero, bias=-BIG)
-    for x in (whole("wft", 512), whole("mt", 512)):
-        act(x, zero, Act.Copy)
-    ts(A("ic", 1, 2), A("ic", 0, 1), 112, None, Op.bitwise_and)
-    ts(A("ic", 2, 3), A("ic", 0, 1), 15, None, Op.bitwise_and)
-    copy(A("cf", 0, 2), A("ic", 1, 3))
-    ts(cf(2), cf(0), 64.0, None, Op.add)
-    copy(cf(3), cf(1))
+    sel(whole("th0", P), whole("thn", P), [[-1, P]], Op.is_gt, 0, 1)
+    sel(whole("th1", P), whole("thn", P), [[-1, P]], Op.is_gt, 64, 1)
+    fill(A("th1", 0, P, 1, 0, 64), HUGE)
+    lin("ng", "S", whole("ng", 512), zero(512), 1.0, -BIG)
+    for b in (2, 3):
+        lin("cz%d" % b, "S", A("cmt", b, 4 * P, 4), zero(P))
+    tiles = [whole("st", 520), A("mt", 128, 512), A("uut", 64, 64 + 4 * P), whole("cm2", 4 * P)]
+    for x in tiles:
+        move(x, zero(x[4] - x[3]))["after"][lc["n"]] = True
+    move(whole("wc", 512), whole("oneb", 512))["after"][lc["n"]] = True
+    dma("Y", T.wt[:, :], T.w[:, :], [], [whole("wt", 512)], 1024)["after"][lc["n"]] = True
+    for k, m in ((1, 15), (2, 31), (3, 3)):
+        ts(A("ic", k, k + 1), A("ic", 0, 1), m, None, Op.bitwise_and)
+    ts(A("ic", 4, 5), A("ic", 0, 1), 2, 7, Op.arith_shift_right, Op.bitwise_and)
+    copy(A("cf", 16, 21), A("ic", 0, 5))
+    c_p, c_lo, c_g, c_b, c_m = (cf(k) for k in range(16, 21))
+    lin("c0", "S", cf(0), c_lo, -1.0, c_p)
+    lin("c1", "S", cf(1), c_lo)
     fill(A("cf", 2, 4, 1, 0, 64), 0.0)
+    lin("c2", "S", A("cf", 2, 3, 1, 64, 128), A("cf", 0, 1, 1, 64, 128), 1.0, 64.0)
+    lin("c3", "S", A("cf", 3, 4, 1, 64, 128), A("cf", 17, 18, 1, 64, 128))
     for e, k in ((0, 0), (6, 0), (8, 1), (14, 1)):
-        copy(A("kst", e, e + 2), A("cf", k, 4, 2))
-    quant("kc", 0, 128, A("kst", 0, 512))
+        lin("jt%d" % e, "S", A("zz", e, e + 2), A("cf", k, 4, 2))
+    quant("kc", 0, 128, whole("zz", 512))
+    fill(A("zz", 0, 16), 0.0)
+    quant("kc", 128, 256, whole("ng", 512))
+    JT, NEG, X1, X2, W0, W1 = ("kc", 0, 128), ("kc", 128, 256), ("kc", 256, 384), ("kc", 384, 512), ("wk", 0, 128), ("wk", 128, 256)
 
     def query(t):
         for b in range(4):
             one = A("ut", 4 * t + b, 4 * t + b + 1)
-            if t == 0 and b < 2:
+            if MOVE.get("q%d%d" % (t, b), "V" if t == 0 and b < 2 else "S") == "V":
                 ts(A("ub", 512 + b, 1280, 4), A("oneb", 0, P), one, None, Op.mult)
             else:
-                act(A("ub", 512 + b, 1280, 4), whole("zf", P), bias=one)
+                act(A("ub", 512 + b, 1280, 4), zero(P), bias=one)
         for b in range(4):
             one = A("ut", 4 * t + b, 4 * t + b + 1)
             ts(A("ub", b, 512, 4), A("oneb", 0, 128), one, -1.0, Op.mult, Op.mult)
-        quant("u%d" % t, 0, 320, whole("ub", 1280))
+        quant("u%d" % t, 0, 128, A("ub", 0, 512))
+        quant("u%d" % t, 128, 320, A("ub", 512, 1280))
 
     query(0)
     quant("x0", 0, P, whole("ct", 4 * P))
-    fill(A("cmt", 2, 4 * P, 4), 0.0)
-    fill(A("cmt", 3, 4 * P, 4), 0.0)
+    quant("v0", P + K, P + 160, zero(512))
     for t in range(R):
-        quant("v%d" % t, P + K, P + 160, zero)
-    fill(Z("one32", 0, 32), 1.0)
-    fill(Z("pm", 0, 1), LOW)
-    fill(Z("ne", 32, 64), 0.0)
-    fill(Z("d0", 0, 32), 1.0)
-    fill(Z("d0", 32, 33), -1.0)
-    fill(Z("d0", 48, 64), 0.0)
-    fill(Z("d1", 32, 48), 0.0)
+        if t + 1 in CAND:
+            move_pair("cd%d" % (t + 1), 96, "v0", P + K, 128)
+        elif t > 0:
+            move_pair("v%d" % t, P + K, "v0", P + K, 128)
+    fill(Z("pm", 0, 17), LOW)
+    fill(Z("dg", 32, 33), 95.5)
+    const("ne", "G", Z("ne", 32, 64), 0)
+    const("d0a", "G", Z("d0", 0, 32), 1)
+    const("d0b", "G", Z("d0", 32, 33), -1)
+    const("d0c", "G", Z("d0", 48, 64), 0)
+    const("d1", "G", Z("d1", 32, 48), 0)
     iota(whole("cw", 256), [[0, 8], [1, 16], [0, 2]], 1, 0)
     iota(whole("mw", 16), [[1, 16]], 0, 0)
     iota(Z("nk", 0, 16), [[-1, 16]], 0, 0)
     iota(whole("mwb", 12), [[2, 12]], -12, 0)
-    sel(A("st", 0, 512, 4), A("oneb", 0, 128), [[-1, 128]], Op.is_equal, 0, 1)
+    eye = A("st", 3, 515, 4)
+    sel(eye, A("oneb", 0, 128), [[-1, 128]], Op.is_equal, 0, 1)
     iota(whole("rb", 128), [[0, 8], [1, 4], [0, 4]], 0, 0)
-    iota(Z("m8", 0, 8), [[1, 8]], 0, 0)
-    sel(Z("up32", 0, 32), Z("one32", 0, 32), [[1, 32]], Op.is_gt, 0, -1)
-    sel(Z("eye32", 0, 32), Z("one32", 0, 32), [[1, 32]], Op.is_equal, 0, -1)
-    JT, ONES, NEG, W1 = ("kc", 0, 128), ("kc", 128, 256), ("kc", 256, 384), ("kc", 384, 512)
+    sel(Z("up32", 0, 32), Z("oneb", 0, 32), [[1, 32]], Op.is_gt, 0, -1)
 
     def columns():
-        for k, m in ((3, 3), (4, 31), (6, 16)):
-            ts(A("ic", k, k + 1), A("ic", 0, 1), m, None, Op.bitwise_and)
-        ts(A("ic", 5, 6), A("ic", 4, 5), 2, None, Op.arith_shift_right)
-        fill(A("kst", 512, 1024, 4), 1.0)
-        fill(A("kst", 513, 1024, 4, 64, 128), 1.0)
-        copy(A("cf", 4, 8), A("ic", 3, 7))
-        ts(cf(10), cf(1), 1.0, None, Op.add)
-        ts(cf(9), cf(7), 224.0, None, Op.add)
-        ts(cf(11), cf(5), -BIG, None, Op.mult)
-        ts(cf(12), cf(5), -1.0, -0.5, Op.mult, Op.add)
+        lin("c7", "S", cf(7), c_lo, -1.0, c_g)
+        lin("c10", "S", cf(10), c_lo, 1.0, 1.0)
+        lin("c9", "S", cf(9), cf(7), 1.0, 240.0)
+        lin("c11", "S", cf(11), c_g, -BIG, 95.5 * BIG)
+        lin("c15", "S", cf(15), c_g, -HUGE, 95.5 * HUGE)
+        lin("c12", "S", cf(12), c_g, -1.0, -0.5)
+        lin("c4", "S", cf(4), c_b, 1.0, -68.0)
         for b in range(2):
-            ts(Z("kst", 1536 + b, 2048, 4), Z("rb", 0, 128), cf(4, L), None, Op.is_equal)
-        quant("kc", 128, 512, A("kst", 512, 2048))
-
-    def decoders():
-        for b in range(1, 4):
-            act(A("st", 512 * b + b, 512 * b + 512, 4), A("st", 0, 512, 4), Act.Copy)
-        quant("eb", 0, 512, whole("st", 2048))
+            ts(A("k1", b, 512, 4), whole("rb", 128), c_b, None, Op.is_equal)
+            sel(A("k1", 2 + b, 512, 4), A("oneb", 0, 128), [[0, 4], [1, 32]], Op.is_gt, 0, -1)
+        quant("kc", 256, 384, whole("k1", 512))
+        for b in range(4):
+            quant("eb", 128 * b, 128 * b + 128, A("st", 3 - b, 515 - b))
 
     def later():
-        ts(Z("d16", 0, 8), Z("m8", 0, 8), cf(6, L), 16.0, Op.is_equal, Op.mult)
-        ts(Z("dm", 0, 8), Z("m8", 0, 8), cf(6, L), -16000.0, Op.not_equal, Op.mult)
-        ts(Z("dm", 0, 8), Z("dm", 0, 8), -1.0, None, Op.add)
-        fill(A("wft", 0, 512, 4, 32, 33), 1.0)
-        ts(A("wft", 2, 512, 4, 32, 33), A("cw", 0, 256, 2, 32, 33), -1.0, None, Op.add)
-        ts(A("zz", 32, 80, 4, 32, 33), A("mw", 0, 12, 1, 32, 33), 16.0, None, Op.mult)
-        fill(A("zz", 34, 80, 4, 32, 33), 1.0)
+        ts(Z("d16", 32, 40), Z("mw", 0, 8), A("cf", 20, 21, 1, 0, L), 16.0, Op.is_equal, Op.mult)
+        lin("d16", "S", Z("d16", 0, 32), Z("st", 3, 131, 4), 16.0)
+        lin("dm", "S", Z("dm", 0, 40), Z("d16", 0, 40), 61.5, -1000.0)
+        const("wf0", "G", A("wft", 0, 512, 4), 1)
+        iota(A("wft", 2, 512, 4), [[0, 8], [1, 16]], 0, 0)
+        lin("zz0", "S", A("zz", XF, XF + 48, 4, 32, 33), A("mw", 0, 12, 1, 32, 33), 16.0)
+        lin("zz2", "S", A("zz", XF + 2, XF + 48, 4, 32, 33), A("oneb", 0, 12, 1, 32, 33))
+
+    def candidates():
+        iota(whole("kr", P), [[2, P]], -P, 0)
+        lin("c13", "S", cf(13), c_lo, -2.0, -1.0)
+        lin("c14", "S", cf(14), cf(0), 2.0)
+        for b in (2, 3):
+            sel(A("c2t", b, 512, 4), A("oneb", 0, 128), [[0, 128]], Op.is_equal, -32, 1)
+            lin("xc%d" % b, "S", A("zz", b - 2, 128, 4, 32, 33), A("oneb", 0, 32, 1, 32, 33))
+        iota(A("c2t", 2, 512, 4, 0, 1), [[0, 8], [1, 16]], 0, 0)
+        iota(A("c2t", 3, 512, 4, 0, 1), [[1, 8], [0, 16]], 0, 0)
+        iota(A("wc", 2, 512, 4), [[0, 8], [-1, 16]], 0, 0)
+        lin("wc2", "S", A("wc", 2, 512, 4, 0, 1), A("oneb", 0, 128, 1, 0, 1), 1.0 / 256)
+        for m in range(2):
+            const("wc%d" % m, "G", A("wc", 3, 512, 4), -16 * m)
+            lin("wd%d" % m, "S", A("wc", 3, 512, 4, 0, 1), A("oneb", 0, 128, 1, 0, 1), 1.0 / 16)
+            quant("wk", 128 * m, 128 * m + 128, whole("wc", 512))
+        for b in range(2):
+            const("x3%d" % b, "G", A("wc", b, 512, 4), (-224, -2)[b])
+            const("x2%d" % b, "G", Z("wc", b, 512, 4), 2)
+            sel(Z("wc", 2 + b, 512, 4), Z("oneb", 0, 128), [[-31, 2], [0, 2], [1, 32]], Op.is_ge, 31, -1)
+        quant("kc", 384, 512, whole("wc", 512))
 
     def place(t, part):
         c = "sc%d" % t
@@ -371,163 +385,230 @@ def rank_program(g, core, T, topo):
         def sc(k):
             return Z(c, k, k + 1)
         if part == 1:
-            ts(sc(23), sc(1), 1.0, sc(9), Op.subtract, Op.mult)
-            ts(sc(24), sc(5), -0.5, None, Op.mult)
-            ts(sc(25), sc(5), -97.0, sc(23), Op.mult, Op.add)
-            tt(Z("dg", 0, 32), Z("cr%d" % t, 0, 32), Z("eye32", 0, 32), Op.mult)
-            red(sc(20), Z("dg", 0, 32), Op.add)
-            act(Z("js5", 0, P), Z("gi%d" % t, 0, P), Act.Sign, bias=sc(20), scale=-1.0 / BIG, acc=sc(22))
+            ts(sc(23), sc(1), 17.0, sc(9), Op.subtract, Op.mult)
+            lin("p24%d" % t, "V", sc(24), sc(5), -0.5)
+            lin("p25%d" % t, "V", sc(25), sc(5), -97.0, sc(23))
+            tt(Z("dg", 0, 32), Z("cr%d" % t, 0, 32), Z("st", 3, 131, 4), Op.mult)
+            red(sc(20), Z("dg", 0, 33), Op.add)
+            act(junk(3, P, 0, L), Z("gi%d" % t, 0, P), Act.Sign, bias=sc(20), scale=-1.0 / (HUGE if t in ADD else BIG), acc=sc(22))
         else:
             act(Z("tgb", t, t + 1), sc(22), scale=sc(24), bias=sc(25))
-            dma("Y", T.tg[t:t + 1, :], T.tgb[0:L, t:t + 1], "tg_%d" % t, [Z("tgb", t, t + 1)], [])
+            dma("Y", T.tg[t:t + 1, :], T.tgb[0:L, t:t + 1], [Z("tgb", t, t + 1)], [], 4)
+
+    def differences(tile, banks, x, u):
+        pair = []
+        for h in range(2):
+            pair.append(mm(banks[h], (x, 64 * h, 64 * h + 128), (u, 128, 320), True, False))
+            pair.append(mm(banks[h], (u, 0, 128), (x, 0, P), False, True))
+        pair[2]["after"].setdefault(pair[1]["n"], False)
+        for h in range(2):
+            tt(A(tile, h, 4 * P, 4), A(banks[h], 0, P), whole("th%d" % h, P), Op.is_gt)
 
     for t in range(R):
         x, v, n, u, nx, c, cr, gi = "x%d" % t, "v%d" % t, "n%d" % t, "u%d" % t, "x%d" % (t + 1), "sc%d" % t, "cr%d" % t, "gi%d" % t
         last = t == R - 1
+        ahead = t + 1 in CAND
+        land, at = ("cd%d" % (t + 1), 64) if ahead else (v, P)
 
         def sc(k):
             return Z(c, k, k + 1)
 
-        def sca(k):
-            return A(c, k, k + 1)
-        pair = []
-        for h in range(2):
-            pair.append(mm("b%d" % h, (x, 64 * h, 64 * h + 128), (u, 128, 320), True, False))
-            pair.append(mm("b%d" % h, (u, 0, 128), (x, 0, P), False, True))
-        pair[2]["after"].setdefault(pair[1]["n"], False)
+        def sca(k, p0=0, p1=128):
+            return A(c, k, k + 1, 1, p0, p1)
+        if t not in CAND:
+            differences("cmt", ("b0", "b1"), x, u)
+            for h in range(2):
+                scan(A("rk%d" % h, 0, P), A("cmt", h, 4 * P, 4), zero(P), 0.0, Op.add, Op.add)
+                ts(A("et", h, 512, 2), whole("er", 256), A("rk%d" % h, P - 1, P), None, Op.is_equal)
+            quant("e", 0, 128, whole("et", 512))
+            mm("b2", ("e", 0, 128), JT)
+            for m in range(2):
+                ts(A("ol", m, m + 1), A("b2", m, m + 1), A("b2", m + 2, m + 3), None, Op.add)
+            src, wide, edge = x, P, -159.5 * BIG
+        else:
+            cd = "cd%d" % t
+            mm("b6", (u, 0, 128), (cd, 0, 128), True, False)
+            mm("b6", (cd, 0, 128), (u, 128, 256), False, True)
+            tt(A("c2t", 0, 512, 4), A("b6", 0, 128), whole("th2", 128), Op.is_lt)
+            quant("c2", 0, 128, whole("c2t", 512))
+            for m in range(2):
+                mm(("b7", "b4")[m], (W0, W1)[m], ("c2", 0, 128))
+                red(sca(40 + m), A(("b7", "b4")[m], 0, 128), Op.min, True)
+            ts(A("ol", 0, 2), A(c, 40, 42), 256.0, None, Op.mult)
+            mm("b1", ("c2", 0, 128), W0)
+            ts(sca(42), A("b1", 0, 1), 32.0, None, Op.is_lt)
+            ts(A("cmt", 0, 4 * P, 4), whole("kr", P), A("kb", 0, 1), sca(42), Op.is_equal, Op.mult)
+            src, wide, edge = cd, 128, -0.5 * BIG
+        pick_codes(A(n + "q", 0, K), A(src + "q", 0, wide), A("ol", 0, 2))
+        pick("n%d" % t, "S", A(n + "s", 0, K), A(src + "s", 0, wide), A("ol", 0, 2))
+        quant("cm", 0, P, whole("cmt", 4 * P))
         if t > 0:
             place(t - 1, 1)
-        tt(A("cmt", 0, 4 * P, 4), A("b0", 0, P), whole("th0", P), Op.is_gt)
-        if t == 0:
-            for b in (1, 2, 3):
-                act(A("st", 512 * b, 512 * b + 512), A("kst", 0, 512), Act.Copy, scale=0.0)
-        for h in range(2):
-            if h == 1:
-                tt(A("cmt", 1, 4 * P, 4), A("b1", 0, P), whole("th1", P), Op.is_gt)
-            scan(A("rk%d" % h, 0, P), A("cmt", h, 4 * P, 4), A("zz", 80, 80 + P), 0.0, Op.add, Op.add)
-            ts(A("et", h, 512, 2), whole("er", 256), A("rk%d" % h, P - 1, P), None, Op.is_equal)
-        quant("e", 0, 128, whole("et", 512))
-        mm("b2", ("e", 0, 128), JT)
-        quant("cm", 0, P, whole("cmt", 4 * P))
-        for m in range(2):
-            ts(A("ol", m, m + 1), A("b2", m, m + 1), A("b2", m + 2, m + 3), None, Op.add)
-        pick_codes(A(n + "q", 0, K), A(x + "q", 0, P), A("ol", 0, 2))
-        pick_s(A(n + "s", 0, K), A(x + "s", 0, P), A("ol", 0, 2))
         dst = T.cores[rank ^ (1 << t)]
         rid, pid = topo.addr(dst, core)
         mask, en = topo.mask(core, dst), len(topo.engines(core, dst))
         to = (T.sem["arr%d" % t], T.sem["sent%d" % t], pid, rid, mask)
-        vq, nq, vs, ns = T[v + "q"][:, P:P + K], T[n + "q"][:, 0:K], T[v + "s"][:, P:P + K], T[n + "s"][:, 0:K]
-        m1 = add("G", [A(n + "q", 0, K)], [], ISSUE, ISSUE, lambda vq=vq, nq=nq, to=to: g.remote_dma(vq.bitcast(dt.uint8), nq.bitcast(dt.uint8), *to), "sent%d" % t, 2 * en)
-        m2 = add("G", [A(n + "s", 0, K)], [], ISSUE, ISSUE, lambda vs=vs, ns=ns, to=to: g.remote_dma(vs, ns, *to), "sent%d" % t, 2 * en)
+        vq, nq, vs, ns = T[land + "q"][:, at:at + K], T[n + "q"][:, 0:K], T[land + "s"][:, at:at + K], T[n + "s"][:, 0:K]
+        m1 = add("G", [A(n + "q", 0, K)], [], "send", lambda vq=vq, nq=nq, to=to: g.remote_dma(vq.bitcast(dt.uint8), nq.bitcast(dt.uint8), *to), "sent%d" % t, 2 * en)
+        m2 = add("G", [A(n + "s", 0, K)], [], "send", lambda vs=vs, ns=ns, to=to: g.remote_dma(vs, ns, *to), "sent%d" % t, 2 * en)
         m2["after"][m1["n"]] = False
-        fly = add("arrive", [], [A(v + "q", P, P + K), A(v + "s", P, P + K)], FLIGHT, FLIGHT, None, "arr%d" % t, 2 * en)
+        fly = add("arrive", [], [A(land + "q", at, at + K), A(land + "s", at, at + K)], "fly", None, "arr%d" % t, 2 * en)
         fly["after"].update({m1["n"]: False, m2["n"]: False})
-        dma("Y", T[v + "q"][:, 0:P].bitcast(dt.uint8), T[x + "q"][:, 0:P].bitcast(dt.uint8), "cq%d" % t, [A(x + "q", 0, P)], [A(v + "q", 0, P)])
-        dma("Y", T[v + "s"][:, 0:P], T[x + "s"][:, 0:P], "cs%d" % t, [A(x + "s", 0, P)], [A(v + "s", 0, P)])
+        move_pair(v, 0, x, 0, P)
         if t == 0:
             columns()
-            decoders()
-        mm("b4", ONES, ("cm", 0, P))
-        ts(A("mkt", 0, 4 * P, 4), A("b4", 0, P), 159.5, BIG, Op.is_gt, Op.mult)
-        copy(A("mkt", 1, 4 * P, 4), A("mkt", 0, 4 * P, 4))
-        act(A("mkt", 2, 4 * P, 4), A("mkt", 0, 4 * P, 4), Act.Copy)
-        copy(A("mkt", 3, 4 * P, 4), A("mkt", 0, 4 * P, 4))
-        scan(A(gi, 0, P), A("mkt", 0, 4 * P, 4), A("zz", 80, 80 + P), cf(11), Op.add, Op.add)
-        quant("mk", 0, P, whole("mkt", 4 * P))
-        act(A("js0", 0, 12), A(gi, 15, P, 16), Act.Sign, bias=0.5, scale=-1.0 / BIG, acc=sca(10))
-        act(A("js1", 0, P), A(gi, 0, P), Act.Sign, bias=0.5, scale=-1.0 / BIG, acc=sca(11))
-        if t == 0:
             later()
+            if CAND:
+                candidates()
+        if ahead:
+            query(t + 1)
+            differences("cm2", ("b3", "b5"), x, "u%d" % (t + 1))
+            quant("uu", 0, P, whole("cm2", 4 * P))
+            mm("b3", NEG, ("uu", 0, P))
+            lin("cm1", "S", A("cmt", 1, 4 * P, 4), zero(P))
+            act(whole("sg", P), A("b3", 0, P), Act.Sign, bias=-127.5, scale=-1.0 / BIG)
+            scan(whole("go", P), whole("sg", P), A("oneb", 0, P), cf(13), Op.add, Op.add)
+            for m in range(4):
+                act(junk(4 + m, P), whole("go", P), Act.Sign, bias=32.0 * m, scale=-1.0, acc=sca(32 + m))
+            own_key = A("kb", 0, 1, 1, 0, 64)
+            act(junk(8, P, 0, 64), A("go", 0, P, 1, 0, 64), Act.Sign, bias=cf(14, 64), scale=-1.0, acc=own_key)
+            ts(whole("oo", 4), A(c, 32, 36), 0.5, 96.0, Op.mult, Op.add)
+            pick_codes(A(land + "q", 0, 64), A(x + "q", 0, P), whole("oo", 4))
+            pick("os%d" % t, "S", A(land + "s", 0, 64), A(x + "s", 0, P), whole("oo", 4))
+            pick("pl%d" % t, "S", A("pl", 0, 64), whole("kr", P), whole("oo", 4))
+        mm("b4", NEG, ("cm", 0, P))
+        if t in ADD:
+            unit, row, first = HUGE, whole("mr", P), cf(15)
+            ts(row, A("b4", 0, P), edge, unit, Op.is_lt, Op.mult)
+        else:
+            unit, row, first = BIG, A("mkt", 0, 4 * P, 4), cf(11)
+            ts(row, A("b4", 0, P), edge, unit, Op.is_lt, Op.mult)
+            for b in range(1, 4):
+                lin("mk%d%d" % (t, b), "VVSV"[b], A("mkt", b, 4 * P, 4), row)
+            quant("mk", 0, P, whole("mkt", 4 * P))
+        scan(A(gi, 0, P), row, zero(P), first, Op.add, Op.add)
+        act(junk(0, 12), A(gi, 15, P, 16), Act.Sign, bias=96.0, scale=-1.0 / unit, acc=sca(10))
+        act(junk(1, P), A(gi, 0, P), Act.Sign, bias=96.0, scale=-1.0 / unit, acc=sca(11))
         for b in range(4):
             bank = ("b6", "b7", "b0", "b1")[b]
             mm(bank, ("eb", 128 * b, 128 * b + 128), (x, 0, P))
-            act(A("hd", b, 4 * P, 4), A(bank, 0, P), Act.Copy, scale=0.5)
-        for k in range(3):
+            lin("hd%d%d" % (t, b), "S", A("hd", b, 4 * P, 4), A(bank, 0, P), 0.5)
+        for k in range(0 if t in ADD else 3):
             mm("b5", NEG, ("mk", 0, P), k == 0, False)
         ts(A("ohb", 0, 12), A("mwb", 0, 12), sca(10), None, Op.is_equal)
         ts(Z("ohh", 0, 12), Z("mwb", 0, 12), sc(10), 0.5, Op.is_equal, Op.mult)
-        ts(sc(12), sc(10), -8.0, 112.0, Op.mult, Op.add)
-        ts(sca(13), sca(10), -16.0, sca(11), Op.mult, Op.add)
-        ts(sca(14), sca(13), 0.5, 1.0, Op.mult, Op.add)
-        ts(sc(15), sc(13), -0.5, 16.0, Op.mult, Op.add)
-        ts(sca(16), sca(13), -0.5, None, Op.mult)
+        lin("s12%d" % t, "V", sc(12), sc(10), -8.0, 112.0)
+        lin("s13%d" % t, "V", sca(13), sca(10), -16.0, sca(11))
+        lin("s14%d" % t, "V", sca(14), sca(13), 0.5, 1.0)
+        lin("s15%d" % t, "V", sc(15), sc(13), -0.5, 16.0)
+        lin("s16%d" % t, "V", sca(16), sca(13), -0.5)
         ts(A("wft", 1, 512, 2), whole("cw", 256), sca(14), None, Op.is_equal)
-        act(A("zz", 35, 80, 4, 64, 96), A("ohb", 0, 12, 1, 64, 96), scale=A(c, 16, 17, 1, 64, 96))
+        lin("z35%d" % t, "S", A("zz", XF + 3, XF + 48, 4, 64, 96), A("ohb", 0, 12, 1, 64, 96), sca(16, 64, 96))
         ts(Z("d0", 33, 48), Z("mw", 1, 16), sc(15), None, Op.is_lt)
         ts(Z("d1", 48, 64), Z("nk", 0, 16), sc(15), 0.0, Op.add, Op.max)
-        if t == 0:
-            quant("w", 0, 128, whole("wt", 512))
-        if not last:
+        if not last and not ahead:
             query(t + 1)
-        else:
+        if last:
+            quant("w", 0, 128, whole("wt", 512))
             mm("b2", ("w", 0, 128), (x, 0, P))
-            act(A("yw", 0, P), A("b2", 0, P), Act.Copy)
+            lin("yw0", "S", A("yw", 0, P), A("b2", 0, P))
         if t > 0:
             place(t - 1, 2)
+        if ahead:
+            lin("bc%d" % t, "S", A("bc", 0, 32, 1, 0, 64), zero(32, 0, 64), 1.0, sca(11, 0, 64))
+            turn(A("lr", 0, 32, 1, 0, 64), A("bc", 0, 32, 1, 0, 64))
+            for k in range(2):
+                lin("ky%d%d" % (t, k), "S", sca(36 + k, 0, 64), own_key, 1.0, (-1.0, 1.0)[k])
+                act(junk(9, 32, 0, 64) if k else junk(0, 32, 0, 64), A("lr", 0, 32, 1, 0, 64), Act.Sign, bias=sca(36 + k, 0, 64), scale=-1.0,
+                    acc=sca(28 + k, 0, 64))
+            ts(sca(30, 0, 64), sca(29, 0, 64), sca(28, 0, 64), -500.0, Op.subtract, Op.mult)
+            ts(A("hq", 32, 33, 1, 0, 64), sca(30, 0, 64), sca(28, 0, 64), 1160.0, Op.add, Op.add)
 
-        mm("b5", (v, P, P + 128), (x, 0, P), False, True)
+        mm("b5", (land, at, at + 128), (x, 0, P), t in ADD, True)
         for b in range(4):
-            mm(("b6", "b7", "b4", "b1")[b], ("eb", 128 * b, 128 * b + 128), (v, P, P + 128))
+            mm(("b6", "b7", "b4", "b1")[b], ("eb", 128 * b, 128 * b + 128), (land, at, at + 128))
 
         def half(b):
-            act(A("ha", b, 128, 4), A(("b6", "b7", "b4", "b1")[b], 0, K), Act.Copy, scale=0.5)
-        scan(Z("pm", 1, 1 + P), A("b5", 0, P, 1, 0, L), Z("zf", 0, P), LOW, Op.max, Op.add)
-        top = Z("pm", P, P + 1)
-        half(0)
-        act(Z("js2", 0, 1 + P), Z("pm", 0, 1 + P), Act.Sign, bias=top, scale=-1.0, acc=sc(1))
-        act(Z("js3", 0, 12), Z("pm", 16, 1 + P, 16), Act.Sign, bias=top, scale=-1.0, acc=sc(0))
-        act(Z("tb", 0, 32), Z("up32", 0, 32), scale=sc(1))
-        act(sc(3), sc(0), scale=-16.0, bias=sc(1))
-        act(Z("zz", 0, 32, 4), Z("d16", 0, 8), scale=sc(0))
-        ts(Z("oha", 0, 12), Z("mw", 0, 12), sc(0), None, Op.is_equal)
-        act(sc(2), sc(0), scale=-16.0, bias=cf(9, L))
-        act(Z("xa", 0, 24, 2), Z("oha", 0, 12), scale=sc(2))
-        act(sc(4), sc(3), scale=-1.0, bias=cf(10, L))
-        half(1)
-        act(Z("xa", 1, 24, 2), Z("oha", 0, 12), scale=sc(4))
-        half(2)
-        half(3)
-        ts(Z("zz", 1, 32, 4), Z("dm", 0, 8), sc(3), 0.0, Op.add, Op.max)
-        turn(Z("tt", 0, 32), Z("tb", 0, 32))
+            lin("ha%d%d" % (t, b), "S", A("ha", b, 128, 4), A(("b6", "b7", "b4", "b1")[b], 0, K), 0.5)
+        if t in ADD:
+            tt(Z("zm", 0, P), A("b5", 0, P, 1, 0, L), Z("mr", 0, P), Op.subtract)
+        scan(Z("pm", 17, 17 + P), Z("zm" if t in ADD else "b5", 0, P), zero(P, 0, L), LOW, Op.max, Op.add)
+        top = Z("pm", P + 16, P + 17)
+        act(Z("uut", 2, 4 * (17 + P), 4), Z("pm", 0, 17 + P), Act.Sign, bias=top, scale=-1.0, acc=sc(1))
+        act(junk(2, 12, 0, L), Z("pm", 16, 1 + P, 16), Act.Sign, bias=top, scale=-1.0, acc=sc(0))
+        lo = 0 if ahead else 32
+        act(Z("zz", 4 * lo + 1, XF, 4), Z("dm", lo, 40), Act.Relu, scale=sc(0), bias=sc(1))
+        lin("xo%d" % t, "V", Z("zz", 4 * lo, XF, 4), Z("d16", lo, 40), sc(0))
+        lin("tb%d" % t, "S", Z("tb", 0, 32), Z("up32", 0, 32), sc(1))
+        lin("s3%d" % t, "S", sc(3), sc(0), -16.0, sc(1))
+        ts(Z("oha", 0, 12), Z("mw", 1, 13), sc(0), None, Op.is_equal)
+        lin("s2%d" % t, "S", sc(2), sc(0), -16.0, cf(9, L))
+        lin("xa0%d" % t, "S", Z("xa", 0, 24, 2), Z("oha", 0, 12), sc(2))
+        lin("s4%d" % t, "S", sc(4), sc(3), -1.0, cf(10, L))
+        lin("xa1%d" % t, "S", Z("xa", 1, 24, 2), Z("oha", 0, 12), sc(4))
+        for b in range(4):
+            half(b)
         quant("xo", 0, 128, A("zz", 0, 512))
-        mm("b3", W1, ("xo", 0, 128))
+        mm("b3", X1, ("xo", 0, 128))
+        ts(A("om", 0, 8), A("b3", 32, 40), 4.0, cf(4), Op.mult, Op.add)
+        ho, hi_, of, ha = A("mt", 0, 128), A("hd", 0, 4 * P), A("om", 0, 8), A("ha", 0, 128)
+        add("V", [hi_, of, ha], [ho], "pick", lambda ho=ho, hi_=hi_, of=of, ha=ha: V.tensor_tensor(ap(ho), ap(hi_).indirect(ap(of)), ap(ha), Op.add))
+        quant(land, at + K, at + 160, whole("mt", 512))
+        if ahead:
+            move_pair(v, P, land, at, 64)
+            ts(Z("uut", 67, 64 + 4 * P, 4), Z("pm", 17, 17 + P), top, -1.0, Op.is_lt, Op.mult)
+            quant("uu", 0, P, A("uut", 64, 64 + 4 * P))
+            mm("b0", X2, ("xo", 0, 128))
+            mm("b5", X1, ("uu", 0, P))
+            mm("b2", X2, ("uu", 0, P))
+            act(junk(4, P), A("b5", 0, P), Act.Sign, bias=0.5, scale=-1.0, acc=sca(17))
+            act(junk(5, P), A("b2", 0, P), Act.Sign, bias=0.5, scale=-1.0, acc=sca(18))
+            act(junk(6, P), A(gi, 0, P), Act.Sign, bias=sca(17), scale=-2.0 / unit, acc=sca(19))
+            turn(A("kb", 0, 32, 1, 96, 128), A("b0", 0, 32, 1, 96, 128))
+            ts(A("hq", 0, 32, 1, 0, 64), A("b0", 0, 32, 1, 0, 64), A("kb", 0, 1, 1, 0, 64), 4000.0, Op.not_equal, Op.mult)
+            red(sca(27, 0, 64), A("hq", 0, 33, 1, 0, 64), Op.min)
+            ts(sca(21, 0, 64), sca(18, 0, 64), sca(27, 0, 64), -HUGE, Op.is_gt, Op.mult)
+            ts(sca(21, 64, 96), sca(18, 64, 96), sca(17, 64, 96), -HUGE, Op.not_equal, Op.mult)
+            ts(sca(21, 96, 128), sca(18, 96, 128), sca(17, 96, 128), -HUGE, Op.is_equal, Op.mult)
+            lin("bl%d" % t, "S", A("bc", 64, 96), zero(32), 1.0, sca(19))
+            turn(A("pl", 64, 96), A("bc", 64, 96))
+            lin("kl%d" % t, "S", A("kb", 0, 1, 1, 64, 96), sca(19, 64, 96))
+            lin("bk%d" % t, "S", sca(26), A("kb", 0, 1), -TINY, sca(21))
+            lin("t0%d" % t, "S", A("th2", 0, 96), whole("pl", 96), TINY, sca(26))
+            lin("t1%d" % t, "S", A("th2", 96, 128), A("b0", 0, 32), TINY, sca(26))
+            ts(A("c2t", 1, 512, 4), eye, sca(21), -32.0 / HUGE, Op.mult, Op.mult)
+        turn(Z("tt", 0, 32), Z("tb", 0, 32))
         ts(Z("ne", 0, 32), Z("tt", 0, 32), sc(1), None, Op.is_equal)
         ts(Z("wft", 0, 512, 2), Z("cw", 0, 256), sc(3), None, Op.is_equal)
-        scan(Z("ms", 0, 64), Z("ne", 0, 64), Z("zf", 0, 64), 0.0, Op.max, Op.max)
-        act(sc(9), Z("ms", 31, 32), scale=-1.0, bias=1.0)
-        act(sc(5), Z("ms", 31, 32))
-        act(Z("zz", 32, 80, 2), Z("xa", 0, 24), scale=sc(9))
+        scan(Z("ms", 0, 64), Z("ne", 0, 64), zero(64, 0, L), 0.0, Op.max, Op.max)
+        lin("s9%d" % t, "S", sc(9), Z("ms", 31, 32), -1.0, 1.0)
+        lin("s5%d" % t, "S", sc(5), Z("ms", 31, 32))
+        lin("zx%d" % t, "S", Z("zz", XF, XF + 48, 2), Z("xa", 0, 24), sc(9))
         quant("wf", 0, 128, whole("wft", 512))
-        ts(A("om", 0, 8), A("b3", 0, 8), 4.0, cf(4), Op.mult, Op.add)
         turn(Z("d1", 0, 32), Z("ms", 32, 64))
         scan(Z(cr, 0, 64), Z("d0", 0, 64), Z("d1", 0, 64), cf(12, L), Op.mult, Op.add)
-        act(Z("js4", 0, 64), Z(cr, 0, 64), Act.Sign, scale=-1.0, acc=sc(7))
+        act(junk(10, 64, 0, L), Z(cr, 0, 64), Act.Sign, scale=-1.0, acc=sc(7))
         ts(sc(6), Z(cr, 31, 32), 0.0, sc(12), Op.is_gt, Op.mult)
-        ts(Z("zz", 33, 80, 4), Z("ohb", 0, 12), sc(6), None, Op.mult)
-        act(Z("zz", 35, 80, 4), Z("ohh", 0, 12), scale=sc(7))
-        quant("xf", 0, 128, A("zz", 32, 544))
-        mm("b2", ("wf", 0, 128), ("xf", 0, 128))
-        ho, hi_, of, ha = A("mt", 0, 128), A("hd", 0, 4 * P), A("om", 0, 8), A("ha", 0, 128)
-        do("V", [hi_, of, ha], [ho], lambda: V.tensor_tensor(ap(ho), ap(hi_).indirect(ap(of)), ap(ha), Op.add), "pick")
-        quant(v, P + K, P + 160, whole("mt", 512))
-        copy(A("of", 0, 12), A("b2", 0, 12))
+        lin("z1%d" % t, "V", Z("zz", XF + 1, XF + 48, 4), Z("ohb", 0, 12), sc(6))
+        lin("z3%d" % t, "S", Z("zz", XF + 3, XF + 48, 4), Z("ohh", 0, 12), sc(7))
+        quant("xf", 0, 128, A("zz", XF, XF + 512))
+        mm("b3" if ahead else "b2", ("wf", 0, 128), ("xf", 0, 128))
+        copy(A("of", 0, 12), A("b3" if ahead else "b2", 0, 12))
         if not last:
             for a, b in ((0, 8), (8, 12)):
                 pick_codes(A(nx + "q", 16 * a, 16 * b), A(v + "q", 0, 256), A("of", a, b))
-                pick_s(A(nx + "s", 16 * a, 16 * b), A(v + "s", 0, 256), A("of", a, b))
+                pick("xs%d%d" % (t, a), "S", A(nx + "s", 16 * a, 16 * b), A(v + "s", 0, 256), A("of", a, b))
         else:
             mm("b3", ("w", 0, 128), (v, P, P + 128))
-            act(A("yw", P, P + 64), A("b3", 0, 64), Act.Copy)
+            lin("yw1", "S", A("yw", P, P + 64), A("b3", 0, 64))
             for a, b in ((0, 6), (6, 12)):
                 pick_codes(A(nx + "q", 16 * a, 16 * b), A(v + "q", 0, 256), A("of", a, b))
-            pick_s(A("yo", 0, P), A("yw", 0, 256), A("of", 0, 12))
-            dma("Y", T.oc[:, :], T.x3q[:, 0:P].bitcast(dt.uint8), "oc_", [A("x3q", 0, P)], [])
-            dma("S", T.y[:, :], T.yo[:, 0:P], "oy_", [A("yo", 0, P)], [])
-            pick_v(A(nx + "s", 0, 96), A(v + "s", 0, 256), A("of", 0, 6))
-            pick_s(A(nx + "s", 96, P), A(v + "s", 0, 256), A("of", 6, 12))
+                pick("yo%d" % a, "S", A("yo", 16 * a, 16 * b), A("yw", 0, 256), A("of", a, b))
+                pick("xs3%d" % a, "VS"[a // 6], A(nx + "s", 16 * a, 16 * b), A(v + "s", 0, 256), A("of", a, b))
+            dma("Y", T.oc[:, :], T.x3q[:, 0:P].bitcast(dt.uint8), [A("x3q", 0, P)], [], 4 * P)
+            dma(MOVE.get("oy", "Y"), T.y[:, :], T.yo[:, 0:P], [A("yo", 0, P)], [], 4 * P)
             for k in range(4):
-                dma("Y", T.osc[4 * k:4 * k + 4, :], T.x3s[32 * k:32 * k + 4, 0:P], "os%d" % k, [A("x3s", 0, P)], [])
+                dma(MOVE.get("oz%d" % k, "YS"[k % 2]), T.osc[4 * k:4 * k + 4, :], T.x3s[32 * k:32 * k + 4, 0:P], [A("x3s", 0, P)], [], 8)
             place(t, 1)
             place(t, 2)
     emit()

@@ -1,17 +1,17 @@
 from concourse.mybir import dt, AluOpType as Op, AxisListType, ActivationFunctionType as Act
 
 N, P, K, R = 8, 192, 32, 3
-CAND = (2,)
+CAND = (1, 2)
 TINY = 2.0 ** -100
-BIG = 2.0 ** 30
 LOW = -1e29
-ADD = (2,)
 HUGE = 2.0 ** 80
 XF, Z0 = 160, 208
 ORDER = """
-2 1 40 39 5 0 18 17 14 19 6 21 3 23 27 20 4 61 65 41 37 22 59 9 62 57 8 7 42 38 43 44 11 46 47 45 53 24 10 36 48 12 169 167 25 29 26 92 28 33 13 31 30 32 168 67 68 69 70 71 98 105 96 89 87 16 88 15 52 51 50 49 73 72 74 75 171 76 34 77 99 64 113 35 116 106 91 170 95 121 63 97 78 83 102 136 79 80 101 81 111 82 94 137 147 148 139 110 84 85 123 108 60 66 145 104 151 142 138 172 140 103 54 141 86 143 93 90 144 107 146 176 173 149 153 154 155 177 174 156 159 175 161 162 158 254 252 152 255 100 160 257 253 181 179 178 165 256 182 183 180 163 166 261 157 258 184 164 187 189 203 186 56 109 55 117 58 185 195 188 118 122 114 204 198 206 211 205 212 199 196 197 190 192 194 150 193 207 191 124 200 208 213 209 214 210 216 215 201 217 259 244 202 125 218 219 245 220 221 222 223 224 225 226 227 242 241 120 112 443 126 127 128 260 243 132 115 129 133 130 228 291 262 263 264 265 246 292 229 230 232 231 233 234 235 293 294 240 266 282 236 237 267 238 239 313 270 297 298 247 248 131 134 119 268 283 286 284 269 295 285 288 271 249 287 272 290 289 296 315 277 273 274 299 300 301 323 304 302 317 319 305 303 307 306 308 309 310 275 316 318 320 328 135 351 312 325 327 326 324 329 321 311 343 330 276 352 333 331 332 278 334 342 354 372 344 336 340 341 355 356 345 374 373 279 322 335 353 375 346 360 281 357 347 358 338 280 365 361 363 364 359 362 348 367 377 376 339 380 366 368 337 369 370 371 379 381 408 393 394 250 350 382 385 378 411 395 412 396 397 399 383 384 410 398 402 400 386 387 401 403 409 405 406 413 414 415 404 388 407 419 349 251 392 390 389 391 417 420 446 418 314 447 416 421 422 423 435 430 428 424 426 431 427 448 451 433 432 437 453 436 434 454 450 468 425 452 444 449 438 441 442 455 456 440 459 457 458 460 467 462 429 445 461 475 470 476 439 471 478 477 469 464 466 463 465 480 479 483 472 484 473 481 485 488 486 482 487 474 509 489 492 510 506 507 508 511 493 512 513 490 491 497 494 495 498 500 501 496 499 503 505 502 504
+6 1 2 0 27 7 10 9 11 23 22 20 21 5 24 25 26 58 29 121 28 41 43 49 3 36 40 39 44 42 37 4 38 30 32 33 31 48 46 45 34 152 150 148 126 47 88 59 125 120 91 154 64 65 66 67 35 12 157 18 17 13 51 16 159 53 158 54 50 85 15 52 149 117 151 93 122 89 113 155 128 92 153 136 133 134 289 60 8 68 69 63 129 131 109 124 70 72 71 73 56 135 74 75 80 156 77 76 137 78 138 119 115 285 79 123 118 61 180 160 161 162 163 181 100 284 139 182 164 186 165 99 166 102 283 108 290 101 184 183 62 288 287 130 110 142 292 187 114 185 81 82 86 95 167 190 188 169 170 191 286 192 193 291 189 96 97 83 199 144 105 141 143 107 111 103 116 132 87 112 203 200 202 201 204 94 194 172 175 171 145 196 195 205 206 140 98 221 197 146 207 222 173 209 208 224 174 226 210 211 147 214 168 213 176 198 212 215 223 225 216 230 229 217 232 228 227 231 177 233 234 236 178 179 294 293 14 84 55 218 220 219 235 237 240 245 241 239 246 238 263 264 265 242 127 243 244 248 249 252 247 266 255 256 267 269 268 270 257 272 258 271 275 259 273 276 260 262 261 295 296 297 298 278 279 57 274 280 250 277 299 300 251 301 314 318 320 315 319 90 333 316 321 302 338 253 339 317 303 327 326 334 324 336 304 341 340 355 309 342 307 328 325 343 330 329 356 335 322 337 305 323 348 346 347 331 345 344 332 358 306 360 357 349 359 308 362 361 364 363 350 366 365 310 351 311 370 368 312 367 352 313 369 371 379 375 384 373 385 374 380 397 398 372 377 376 382 378 383 399 381 400 401 403 406 389 390 402 391 404 407 405 408 409 282 254 353 354 281 19 392 417 410 396 386 394 411 418 412 413 395 393 387 104 419 442 420 421 422 434 423 424 414 427 428 435 437 445 443 432 431 106 450 436 451 444 439 452 429 440 430 438 441 425 446 448 449 456 453 454 457 465 426 459 455 472 467 473 474 468 447 475 458 479 461 463 466 476 433 477 464 462 469 480 485 460 481 482 478 483 484 504 470 506 471 486 507 489 503 505 490 508 509 416 415 510 388 487 488 494 491 495 492 497 498 496 493 502 500 501 499
 """
-MOVE = {}
+MOVE = {_w[:-1]: _w[-1] for _w in """
+cz3V cw0S cw1S d0aV d0cV dmV wf1G wf2S cxS cy2S cy3S cy0S wc32S wc3V wd0S wd1S x22S r10S r11S r12S q13S r13S cm10V hd03V xo0S ha02V ha03V bk0V t10V u150V utg0V q21S r21S q22S r22S q23S hd12V hd13V ha10V ha11V ha12V ha13V xd1V bk1V t11V utg1V hd20V hd23V s122S s132S s142S s162S tb2V z12S yw1V p242S
+""".split()}
 
 MXC, U8, F32, BF, I32, U16 = "float8_e4m3fn_x4", "uint8", "float32", "bfloat16", "int32", "uint16"
 SCRATCH = {}
@@ -37,17 +37,17 @@ for _t in range(R):
     if _t in CAND:
         _pair("cd%d" % _t, 224)
 _pair("x3", P)
-for _n, _c in (("w", 128), ("eb", 512), ("kc", 512), ("e", 128), ("cm", P), ("mk", P), ("xo", 128), ("wf", 128), ("xf", 128),
+for _n, _c in (("w", 128), ("eb", 512), ("kc", 512), ("e", 128), ("cm", P), ("xo", 128), ("wf", 128), ("xf", 128),
                ("uu", P), ("c2", 128), ("wk", 256)):
     _pair(_n, _c)
-for _n, _c in (("ct", 4 * P), ("ut", 16), ("wt", 512), ("ub", 1280), ("st", 520), ("ng", 512), ("k1", 512), ("et", 512), ("cmt", 4 * P),
-               ("mkt", 4 * P), ("zz", Z0 + 4 * P), ("wft", 512), ("mt", 512), ("oneb", 512), ("er", 256), ("cw", 256), ("rb", 128),
-               ("rk", 2 * P), ("th", 3 * P), ("up32", 32), ("cm2", 4 * P), ("uut", 840), ("c2t", 512), ("wc", 512),
-               ("kr", P), ("sg", 3 * P), ("jk", 2240)):
+for _n, _c in (("ct", 4 * P), ("ut", 16), ("wt", 512), ("ub", 1280), ("st", 520), ("k1", 512), ("et", 512), ("cmt", 4 * P),
+               ("zz", Z0 + 4 * P), ("wft", 512), ("mt", 512), ("oneb", 512), ("er", 256), ("cw", 256), ("rb", 128),
+               ("rk", 2 * P), ("th", 512), ("up32", 32), ("un", 16), ("cm2", 4 * P), ("uut", 840), ("c2t", 512), ("wc", 512),
+               ("kr", P), ("cx", 256), ("sg", 3 * P), ("jk", 2240)):
     _buf(_n, _c, BF)
-for _n, _c in (("mw", 16), ("mwb", 16), ("nk", 16), ("d0", 64), ("d1", 64), ("ms", 64), ("d16", 40), ("dm", 40), ("cf", 24), ("oh", 48),
+for _n, _c in (("mw", 64), ("d0", 64), ("d1", 64), ("ms", 64), ("d16", 40), ("dm", 40), ("cf", 32), ("oh", 48),
                ("zm", P), ("pm", 216), ("tb", 64), ("ne", 64), ("dg", 40), ("xa", 24), ("hd", 4 * P), ("ha", 128),
-               ("yw", 256), ("yo", P), ("tgb", 16), ("kb", 32), ("pl", 96), ("bc", 96), ("hq", 40), ("th2", 128)):
+               ("yw", 256), ("yo", P), ("tgb", 16), ("kb", 32), ("pl", 96), ("bc", 200), ("th2", 128)):
     _buf(_n, _c, F32)
 _buf("ic", 16, I32)
 _buf("ol", 2, U16)
@@ -56,8 +56,9 @@ _buf("of", 12, U16)
 _buf("oo", 4, U16)
 for _n in range(8):
     _buf("b%d" % _n, 512, F32, "psum")
-SHARE = {"rk0": ("rk", 0), "rk1": ("rk", P), "th0": ("th", 0), "th1": ("th", P), "thn": ("th", 2 * P), "go": ("sg", P), "mr": ("sg", 2 * P),
-         "ohb": ("oh", 0), "ohh": ("oh", 16), "oha": ("oh", 32), "tt": ("tb", 32), "lr": ("bc", 32)}
+SHARE = {"rk0": ("rk", 0), "rk1": ("rk", P), "th0": ("th", 64), "th1": ("th", 0), "thn": ("th", 256), "go": ("sg", P), "mr": ("sg", 2 * P),
+         "ohb": ("oh", 0), "ohh": ("oh", 16), "oha": ("oh", 32), "tt": ("tb", 32), "lr": ("bc", 136), "mwb": ("mw", 16), "m32": ("mw", 32),
+         "nk": ("mw", 48), "hq": ("bc", 96)}
 
 SEMAPHORES = ["sv", "ss", "stn", "sg"] + ["dm%d" % k for k in range(48)] + ["arr%d" % k for k in range(R)] + ["sent%d" % k for k in range(R)]
 
@@ -97,16 +98,16 @@ def rank_program(g, core, T, topo):
     def psum(x):
         return SCRATCH[x[0]][0] == "psum"
 
-    def add(q, reads, writes, kind, issue, sem=None, val=0):
+    def add(q, reads, writes, kind, issue, sem=None, val=0, tag=None):
         after = {}
-        node = {"q": q, "n": len(nodes), "after": after, "k": kind, "r": reads, "w": writes, "issue": issue, "sem": sem, "val": val}
+        node = {"q": q, "n": len(nodes), "after": after, "k": kind, "r": reads, "w": writes, "issue": issue, "sem": sem, "val": val, "tag": tag}
         for views, w in ((reads, False), (writes, True)):
             for x in views:
                 for y, m, yw in log.get(x[0], []):
                     if psum(x):
                         if q == "T" and m["q"] == "T":
                             after.setdefault(m["n"], False)
-                        elif q != m["q"] or w or yw:
+                        elif q != m["q"] or w or yw or tag or m["tag"]:
                             after[m["n"]] = True
                     elif (w or yw) and _cross(x, y):
                         after[m["n"]] = True
@@ -196,10 +197,11 @@ def rank_program(g, core, T, topo):
             add("S", rd, [o, acc], "acc", lambda: S.activation(ap(o), ap(i), f, bias=val(bias), scale=val(scale), accum_out=ap(acc)))
 
     def lin(tag, q, o, i, scale=1.0, bias=0.0):
+        rd = [i] + [s for s in (bias, scale) if isinstance(s, tuple)]
         if MOVE.get(tag, q) == "S":
-            act(o, i, scale=scale, bias=bias)
+            add("S", rd, [o], "lin", lambda: S.activation(ap(o), ap(i), Act.Identity, bias=val(bias), scale=val(scale)), tag=tag)
         else:
-            ts(o, i, scale, bias, Op.mult, Op.add)
+            add("V", rd, [o], "lin", lambda: V.tensor_scalar(ap(o), ap(i), val(scale), val(bias), Op.mult, Op.add), tag=tag)
 
     def quant(n, c0, c1, i):
         q, s = A(n + "q", c0, c1), A(n + "s", c0, c1)
@@ -215,9 +217,9 @@ def rank_program(g, core, T, topo):
 
     def pick(tag, q, o, i, off):
         if MOVE.get(tag, q) == "S":
-            add("S", [i, off], [o], "pick", lambda: S.activation(ap(o), ap(i).indirect(ap(off)), Act.Copy))
+            add("S", [i, off], [o], "pick", lambda: S.activation(ap(o), ap(i).indirect(ap(off)), Act.Copy), tag=tag)
         else:
-            add("V", [i, off], [o], "pick", lambda: V.tensor_copy(ap(o), ap(i).indirect(ap(off))))
+            add("V", [i, off], [o], "pick", lambda: V.tensor_copy(ap(o), ap(i).indirect(ap(off))), tag=tag)
 
     def iota(o, pattern, base, cm):
         if SCRATCH[o[0]][2] != I32:
@@ -227,9 +229,10 @@ def rank_program(g, core, T, topo):
 
     def const(tag, q, o, v):
         if MOVE.get(tag, q) == "V":
-            fill(o, float(v))
+            add("V", [], [o], "const", lambda: V.memset(ap(o), float(v)), tag=tag)
         else:
-            iota(o, [[0, (o[4] - o[3] + o[5] - 1) // o[5]]], v, 0)
+            n = (o[4] - o[3] + o[5] - 1) // o[5]
+            add("G", [], [o], "const", lambda: g.iota(ap(o), [[0, n]], v, 0, allow_small_or_imprecise_dtypes=True), tag=tag)
 
     def sel(o, i, pattern, op, base, cm):
         add("G", [i], [o], "sel", lambda: g.affine_select(ap(o), ap(i), pattern, op, 0.0, base, cm))
@@ -265,17 +268,16 @@ def rank_program(g, core, T, topo):
 
     fill(A("zz", Z0, Z0 + 4 * P), 0.0)
     fill(A("zz", 0, Z0), 0.0)
-    fill(whole("thn", P), -TINY)
+    fill(whole("thn", 256), -TINY)
     fill(whole("oneb", 512), 1.0)
     iota(A("ic", 0, 1), [[0, 1]], 0, 1)
     iota(whole("er", 256), [[0, 8], [1, 16], [16, 2]], 0, 0)
-    sel(whole("th0", P), whole("thn", P), [[-1, P]], Op.is_gt, 0, 1)
-    sel(whole("th1", P), whole("thn", P), [[-1, P]], Op.is_gt, 64, 1)
-    fill(A("th1", 0, P, 1, 0, 64), HUGE)
-    lin("ng", "S", whole("ng", 512), zero(512), 1.0, -BIG)
+    sel(whole("th1", 256), whole("thn", 256), [[-1, 256]], Op.is_gt, 64, 1)
+    lin("cz1", "S", A("cmt", 1, 4 * P, 4, 0, 64), zero(P, 0, 64))
+    lin("ez1", "S", A("et", 1, 512, 2, 0, 64), zero(256, 0, 64))
     for b in (2, 3):
         lin("cz%d" % b, "S", A("cmt", b, 4 * P, 4), zero(P))
-    tiles = [whole("st", 520), A("mt", 128, 512), A("uut", 64, 64 + 4 * P), whole("cm2", 4 * P)]
+    tiles = [whole("st", 520), A("mt", 128, 512), A("uut", 64, 64 + 4 * P), whole("cm2", 4 * P), whole("c2t", 512)]
     for x in tiles:
         move(x, zero(x[4] - x[3]))["after"][lc["n"]] = True
     move(whole("wc", 512), whole("oneb", 512))["after"][lc["n"]] = True
@@ -294,23 +296,25 @@ def rank_program(g, core, T, topo):
         lin("jt%d" % e, "S", A("zz", e, e + 2), A("cf", k, 4, 2))
     quant("kc", 0, 128, whole("zz", 512))
     fill(A("zz", 0, 16), 0.0)
-    quant("kc", 128, 256, whole("ng", 512))
-    JT, NEG, X1, X2, W0, W1 = ("kc", 0, 128), ("kc", 128, 256), ("kc", 256, 384), ("kc", 384, 512), ("wk", 0, 128), ("wk", 128, 256)
+    quant("kc", 128, 256, whole("oneb", 512))
+    JT, ONES, X1, X2, W0, W1 = ("kc", 0, 128), ("kc", 128, 256), ("kc", 256, 384), ("kc", 384, 512), ("wk", 0, 128), ("wk", 128, 256)
 
     def query(t):
+        n = P if t == 0 else 128
         for b in range(4):
             one = A("ut", 4 * t + b, 4 * t + b + 1)
-            if MOVE.get("q%d%d" % (t, b), "V" if t == 0 and b < 2 else "S") == "V":
-                ts(A("ub", 512 + b, 1280, 4), A("oneb", 0, P), one, None, Op.mult)
+            lin("q%d%d" % (t, b), "V" if t > 0 or b < 2 else "S", A("ub", 512 + b, 512 + 4 * n, 4), zero(n), 1.0, one)
+            if t == 0:
+                ts(A("ub", b, 512, 4), A("oneb", 0, 128), one, -1.0, Op.mult, Op.mult)
             else:
-                act(A("ub", 512 + b, 1280, 4), zero(P), bias=one)
-        for b in range(4):
-            one = A("ut", 4 * t + b, 4 * t + b + 1)
-            ts(A("ub", b, 512, 4), A("oneb", 0, 128), one, -1.0, Op.mult, Op.mult)
+                lin("r%d%d" % (t, b), "V", A("ub", b, 512, 4), zero(128), 1.0, A("un", 4 * t + b, 4 * t + b + 1))
         quant("u%d" % t, 0, 128, A("ub", 0, 512))
-        quant("u%d" % t, 128, 320, A("ub", 512, 1280))
+        quant("u%d" % t, 128, 128 + n, A("ub", 512, 512 + 4 * n))
+        if n < P:
+            move_pair("u%d" % t, 256, "u%d" % t, 128, 64)
 
     query(0)
+    lin("un", "S", whole("un", 12), whole("ut", 12), -1.0)
     quant("x0", 0, P, whole("ct", 4 * P))
     quant("v0", P + K, P + 160, zero(512))
     for t in range(R):
@@ -320,80 +324,90 @@ def rank_program(g, core, T, topo):
             move_pair("v%d" % t, P + K, "v0", P + K, 128)
     fill(Z("pm", 0, 17), LOW)
     fill(Z("dg", 32, 33), 95.5)
-    const("ne", "G", Z("ne", 32, 64), 0)
-    const("d0a", "G", Z("d0", 0, 32), 1)
-    const("d0b", "G", Z("d0", 32, 33), -1)
-    const("d0c", "G", Z("d0", 48, 64), 0)
-    const("d1", "G", Z("d1", 32, 48), 0)
-    iota(whole("cw", 256), [[0, 8], [1, 16], [0, 2]], 1, 0)
+    for b in range(2):
+        lin("cw%d" % b, "V", A("cw", b, 256, 2), A("er", 0, 256, 2), 1.0, 1.0)
     iota(whole("mw", 16), [[1, 16]], 0, 0)
-    iota(Z("nk", 0, 16), [[-1, 16]], 0, 0)
-    iota(whole("mwb", 12), [[2, 12]], -12, 0)
+    lin("nk", "S", Z("nk", 0, 16), Z("mw", 0, 16), -1.0)
+    lin("mwb", "S", whole("mwb", 13), whole("mw", 13), 2.0, -12.0)
     eye = A("st", 3, 515, 4)
     sel(eye, A("oneb", 0, 128), [[-1, 128]], Op.is_equal, 0, 1)
-    iota(whole("rb", 128), [[0, 8], [1, 4], [0, 4]], 0, 0)
-    sel(Z("up32", 0, 32), Z("oneb", 0, 32), [[1, 32]], Op.is_gt, 0, -1)
 
     def columns():
+        iota(whole("rb", 128), [[0, 8], [1, 4], [0, 4]], 0, 0)
+        sel(Z("up32", 0, 32), Z("oneb", 0, 32), [[1, 32]], Op.is_gt, 0, -1)
         lin("c7", "S", cf(7), c_lo, -1.0, c_g)
         lin("c10", "S", cf(10), c_lo, 1.0, 1.0)
         lin("c9", "S", cf(9), cf(7), 1.0, 240.0)
-        lin("c11", "S", cf(11), c_g, -BIG, 95.5 * BIG)
         lin("c15", "S", cf(15), c_g, -HUGE, 95.5 * HUGE)
         lin("c12", "S", cf(12), c_g, -1.0, -0.5)
         lin("c4", "S", cf(4), c_b, 1.0, -68.0)
         for b in range(2):
             ts(A("k1", b, 512, 4), whole("rb", 128), c_b, None, Op.is_equal)
-            sel(A("k1", 2 + b, 512, 4), A("oneb", 0, 128), [[0, 4], [1, 32]], Op.is_gt, 0, -1)
+        sel(A("k1", 2, 512, 4), A("oneb", 0, 128), [[0, 4], [1, 32]], Op.is_gt, 0, -1)
+        lin("k13", "V", A("k1", 3, 512, 4), A("k1", 2, 512, 4))
         quant("kc", 256, 384, whole("k1", 512))
         for b in range(4):
             quant("eb", 128 * b, 128 * b + 128, A("st", 3 - b, 515 - b))
 
     def later():
+        const("ne", "G", Z("ne", 32, 64), 0)
+        const("d0a", "G", Z("d0", 0, 32), 1)
+        const("d0b", "G", Z("d0", 32, 33), -1)
+        const("d0c", "G", Z("d0", 48, 64), 0)
+        const("d1", "G", Z("d1", 32, 48), 0)
         ts(Z("d16", 32, 40), Z("mw", 0, 8), A("cf", 20, 21, 1, 0, L), 16.0, Op.is_equal, Op.mult)
         lin("d16", "S", Z("d16", 0, 32), Z("st", 3, 131, 4), 16.0)
         lin("dm", "S", Z("dm", 0, 40), Z("d16", 0, 40), 61.5, -1000.0)
         const("wf0", "G", A("wft", 0, 512, 4), 1)
-        iota(A("wft", 2, 512, 4), [[0, 8], [1, 16]], 0, 0)
+        const("wf1", "V", A("wft", 1, 512, 2), 0)
+        lin("wf2", "V", A("wft", 2, 512, 4), A("cw", 0, 256, 2), 1.0, -1.0)
         lin("zz0", "S", A("zz", XF, XF + 48, 4, 32, 33), A("mw", 0, 12, 1, 32, 33), 16.0)
         lin("zz2", "S", A("zz", XF + 2, XF + 48, 4, 32, 33), A("oneb", 0, 12, 1, 32, 33))
 
     def candidates():
         iota(whole("kr", P), [[2, P]], -P, 0)
+        lin("cx", "V", whole("cx", 256), whole("cw", 256), 2.0, -34.0)
+        lin("m32", "S", whole("m32", 12), whole("mw", 12), 32.0, -193.0)
+        lin("c21", "S", cf(21), cf(0), 1.0, 48.0)
+        lin("c22", "S", cf(22), c_lo, 1.0, -16.0)
+        lin("c23", "S", cf(23), c_p, 0.0, 1.0)
+        lin("c23b", "S", A("cf", 23, 24, 1, 64, 96), A("cf", 16, 17, 1, 64, 96), 0.0, -1.0)
+        lin("c24", "S", cf(24), cf(23), -1.0)
+        lin("c25", "S", cf(25), cf(23), 0.5)
         lin("c13", "S", cf(13), c_lo, -2.0, -1.0)
         lin("c14", "S", cf(14), cf(0), 2.0)
         for b in (2, 3):
-            sel(A("c2t", b, 512, 4), A("oneb", 0, 128), [[0, 128]], Op.is_equal, -32, 1)
+            lin("cy%d" % b, "V", A("c2t", b, 512, 4, 32, 33), A("oneb", 0, 128, 1, 32, 33))
             lin("xc%d" % b, "S", A("zz", b - 2, 128, 4, 32, 33), A("oneb", 0, 32, 1, 32, 33))
-        iota(A("c2t", 2, 512, 4, 0, 1), [[0, 8], [1, 16]], 0, 0)
+        lin("cy0", "V", A("c2t", 2, 512, 4, 0, 1), A("cw", 0, 256, 2, 0, 1), 1.0, -1.0)
         iota(A("c2t", 3, 512, 4, 0, 1), [[1, 8], [0, 16]], 0, 0)
-        iota(A("wc", 2, 512, 4), [[0, 8], [-1, 16]], 0, 0)
+        lin("wc32", "V", A("wc", 2, 512, 4, 32, 33), A("cw", 0, 256, 2, 32, 33), -1.0, 1.0)
         lin("wc2", "S", A("wc", 2, 512, 4, 0, 1), A("oneb", 0, 128, 1, 0, 1), 1.0 / 256)
+        lin("wc3", "S", A("wc", 3, 512, 4, 0, 1), A("oneb", 0, 128, 1, 0, 1), 1.0 / 16)
         for m in range(2):
-            const("wc%d" % m, "G", A("wc", 3, 512, 4), -16 * m)
-            lin("wd%d" % m, "S", A("wc", 3, 512, 4, 0, 1), A("oneb", 0, 128, 1, 0, 1), 1.0 / 16)
+            lin("wd%d" % m, "V", A("wc", 3, 512, 4, 32, 33), A("oneb", 0, 128, 1, 32, 33), -16.0 * m)
             quant("wk", 128 * m, 128 * m + 128, whole("wc", 512))
         for b in range(2):
-            const("x3%d" % b, "G", A("wc", b, 512, 4), (-224, -2)[b])
+            lin("x3%d" % b, "V", A("wc", b, 512, 4, 32, 33), A("oneb", 0, 128, 1, 32, 33), (-224.0, -2.0)[b])
             const("x2%d" % b, "G", Z("wc", b, 512, 4), 2)
-            sel(Z("wc", 2 + b, 512, 4), Z("oneb", 0, 128), [[-31, 2], [0, 2], [1, 32]], Op.is_ge, 31, -1)
+        sel(Z("wc", 2, 512, 4), Z("oneb", 0, 128), [[-31, 2], [0, 2], [1, 32]], Op.is_ge, 31, -1)
+        lin("x22", "V", Z("wc", 258, 384, 4), Z("wc", 258, 384, 4), -1.0)
+        lin("x23", "V", Z("wc", 3, 512, 4), Z("wc", 2, 512, 4))
         quant("kc", 384, 512, whole("wc", 512))
 
-    def place(t, part):
+    def place(t):
         c = "sc%d" % t
 
         def sc(k):
             return Z(c, k, k + 1)
-        if part == 1:
-            ts(sc(23), sc(1), 17.0, sc(9), Op.subtract, Op.mult)
-            lin("p24%d" % t, "V", sc(24), sc(5), -0.5)
-            lin("p25%d" % t, "V", sc(25), sc(5), -97.0, sc(23))
-            tt(Z("dg", 0, 32), Z("cr%d" % t, 0, 32), Z("st", 3, 131, 4), Op.mult)
-            red(sc(20), Z("dg", 0, 33), Op.add)
-            act(junk(3, P, 0, L), Z("gi%d" % t, 0, P), Act.Sign, bias=sc(20), scale=-1.0 / (HUGE if t in ADD else BIG), acc=sc(22))
-        else:
-            act(Z("tgb", t, t + 1), sc(22), scale=sc(24), bias=sc(25))
-            dma("Y", T.tg[t:t + 1, :], T.tgb[0:L, t:t + 1], [Z("tgb", t, t + 1)], [], 4)
+        ts(sc(23), sc(1), 17.0, sc(9), Op.subtract, Op.mult)
+        lin("p24%d" % t, "V", sc(24), sc(5), -0.5)
+        lin("p25%d" % t, "V", sc(25), sc(5), -97.0, sc(23))
+        tt(Z("dg", 0, 32), Z("cr%d" % t, 0, 32), Z("st", 3, 131, 4), Op.mult)
+        red(sc(20), Z("dg", 0, 33), Op.add)
+        act(junk(3, P, 0, L), Z("gi%d" % t, 0, P), Act.Sign, bias=sc(20), scale=-1.0 / HUGE, acc=sc(22))
+        act(Z("tgb", t, t + 1), sc(22), scale=sc(24), bias=sc(25))
+        dma("Y", T.tg[t:t + 1, :], T.tgb[0:L, t:t + 1], [Z("tgb", t, t + 1)], [], 4)
 
     def differences(tile, banks, x, u):
         pair = []
@@ -402,12 +416,12 @@ def rank_program(g, core, T, topo):
             pair.append(mm(banks[h], (u, 0, 128), (x, 0, P), False, True))
         pair[2]["after"].setdefault(pair[1]["n"], False)
         for h in range(2):
-            tt(A(tile, h, 4 * P, 4), A(banks[h], 0, P), whole("th%d" % h, P), Op.is_gt)
+            tt(A(tile, h, 4 * P, 4, 64 * h), A(banks[h], 0, P, 1, 64 * h), A("th%d" % h, 0, P, 1, 64 * h), Op.is_gt)
 
     for t in range(R):
         x, v, n, u, nx, c, cr, gi = "x%d" % t, "v%d" % t, "n%d" % t, "u%d" % t, "x%d" % (t + 1), "sc%d" % t, "cr%d" % t, "gi%d" % t
         last = t == R - 1
-        ahead = t + 1 in CAND
+        ahead = not last
         land, at = ("cd%d" % (t + 1), 64) if ahead else (v, P)
 
         def sc(k):
@@ -415,16 +429,16 @@ def rank_program(g, core, T, topo):
 
         def sca(k, p0=0, p1=128):
             return A(c, k, k + 1, 1, p0, p1)
-        if t not in CAND:
+        if t == 0:
             differences("cmt", ("b0", "b1"), x, u)
             for h in range(2):
-                scan(A("rk%d" % h, 0, P), A("cmt", h, 4 * P, 4), zero(P), 0.0, Op.add, Op.add)
-                ts(A("et", h, 512, 2), whole("er", 256), A("rk%d" % h, P - 1, P), None, Op.is_equal)
+                scan(A("rk%d" % h, 0, P, 1, 64 * h), A("cmt", h, 4 * P, 4, 64 * h), zero(P, 64 * h), 0.0, Op.add, Op.add)
+                ts(A("et", h, 512, 2, 64 * h), A("er", 0, 256, 1, 64 * h), A("rk%d" % h, P - 1, P, 1, 64 * h), None, Op.is_equal)
             quant("e", 0, 128, whole("et", 512))
             mm("b2", ("e", 0, 128), JT)
             for m in range(2):
                 ts(A("ol", m, m + 1), A("b2", m, m + 1), A("b2", m + 2, m + 3), None, Op.add)
-            src, wide, edge = x, P, -159.5 * BIG
+            src, wide = x, P
         else:
             cd = "cd%d" % t
             mm("b6", (u, 0, 128), (cd, 0, 128), True, False)
@@ -438,12 +452,10 @@ def rank_program(g, core, T, topo):
             mm("b1", ("c2", 0, 128), W0)
             ts(sca(42), A("b1", 0, 1), 32.0, None, Op.is_lt)
             ts(A("cmt", 0, 4 * P, 4), whole("kr", P), A("kb", 0, 1), sca(42), Op.is_equal, Op.mult)
-            src, wide, edge = cd, 128, -0.5 * BIG
+            src, wide = cd, 128
         pick_codes(A(n + "q", 0, K), A(src + "q", 0, wide), A("ol", 0, 2))
         pick("n%d" % t, "S", A(n + "s", 0, K), A(src + "s", 0, wide), A("ol", 0, 2))
         quant("cm", 0, P, whole("cmt", 4 * P))
-        if t > 0:
-            place(t - 1, 1)
         dst = T.cores[rank ^ (1 << t)]
         rid, pid = topo.addr(dst, core)
         mask, en = topo.mask(core, dst), len(topo.engines(core, dst))
@@ -456,98 +468,96 @@ def rank_program(g, core, T, topo):
         fly["after"].update({m1["n"]: False, m2["n"]: False})
         move_pair(v, 0, x, 0, P)
         if t == 0:
+            k0 = len(nodes)
             columns()
             later()
-            if CAND:
-                candidates()
+            candidates()
+            for m in nodes[k0:]:
+                if m["q"] == "G" or m["k"] == "const":
+                    m["after"][m2["n"]] = False
         if ahead:
             query(t + 1)
             differences("cm2", ("b3", "b5"), x, "u%d" % (t + 1))
             quant("uu", 0, P, whole("cm2", 4 * P))
-            mm("b3", NEG, ("uu", 0, P))
-            lin("cm1", "S", A("cmt", 1, 4 * P, 4), zero(P))
-            act(whole("sg", P), A("b3", 0, P), Act.Sign, bias=-127.5, scale=-1.0 / BIG)
-            scan(whole("go", P), whole("sg", P), A("oneb", 0, P), cf(13), Op.add, Op.add)
+            mm("b3", ONES, ("uu", 0, P))
+            if t == 0:
+                lin("cm1%d" % t, "S", A("cmt", 1, 4 * P, 4, 64), zero(P, 64))
+            i, o, on_v = A("b3", 0, P), whole("sg", P), MOVE.get("sg%d" % t, "S") == "V"
+            if on_v:
+                add("V", [i], [o], "lin", lambda i=i, o=o: V.tensor_scalar(ap(o), ap(i), 127.5, 2.0, Op.is_gt, Op.mult), tag="sg%d" % t)
+            else:
+                add("S", [i], [o], "lin", lambda i=i, o=o: S.activation(ap(o), ap(i), Act.Sign, bias=-127.5), tag="sg%d" % t)
+            scan(whole("go", P), o, zero(P) if on_v else A("oneb", 0, P), cf(13), Op.add, Op.add)
             for m in range(4):
-                act(junk(4 + m, P), whole("go", P), Act.Sign, bias=32.0 * m, scale=-1.0, acc=sca(32 + m))
+                e = min(16 * m, 48 - 16 * m)
+                act(junk(4 + m, P - 2 * e), A("go", e, P - e), Act.Sign, bias=32.0 * m, scale=-1.0, acc=sca(32 + m))
             own_key = A("kb", 0, 1, 1, 0, 64)
             act(junk(8, P, 0, 64), A("go", 0, P, 1, 0, 64), Act.Sign, bias=cf(14, 64), scale=-1.0, acc=own_key)
             ts(whole("oo", 4), A(c, 32, 36), 0.5, 96.0, Op.mult, Op.add)
             pick_codes(A(land + "q", 0, 64), A(x + "q", 0, P), whole("oo", 4))
             pick("os%d" % t, "S", A(land + "s", 0, 64), A(x + "s", 0, P), whole("oo", 4))
             pick("pl%d" % t, "S", A("pl", 0, 64), whole("kr", P), whole("oo", 4))
-        mm("b4", NEG, ("cm", 0, P))
-        if t in ADD:
-            unit, row, first = HUGE, whole("mr", P), cf(15)
-            ts(row, A("b4", 0, P), edge, unit, Op.is_lt, Op.mult)
         else:
-            unit, row, first = BIG, A("mkt", 0, 4 * P, 4), cf(11)
-            ts(row, A("b4", 0, P), edge, unit, Op.is_lt, Op.mult)
-            for b in range(1, 4):
-                lin("mk%d%d" % (t, b), "VVSV"[b], A("mkt", b, 4 * P, 4), row)
-            quant("mk", 0, P, whole("mkt", 4 * P))
-        scan(A(gi, 0, P), row, zero(P), first, Op.add, Op.add)
-        act(junk(0, 12), A(gi, 15, P, 16), Act.Sign, bias=96.0, scale=-1.0 / unit, acc=sca(10))
-        act(junk(1, P), A(gi, 0, P), Act.Sign, bias=96.0, scale=-1.0 / unit, acc=sca(11))
+            lin("f2%d" % t, "S", A("zz", XF, XF + 48, 2, 64, 128), zero(24, 64, 128))
+        mm("b4", ONES, ("cm", 0, P))
+        if t > 0:
+            lin("mr%d" % t, "S", whole("mr", P), A("b4", 0, P), HUGE)
+        else:
+            ts(whole("mr", P), A("b4", 0, P), 159.5, HUGE, Op.is_gt, Op.mult)
+        scan(A(gi, 0, P), whole("mr", P), zero(P), cf(15), Op.add, Op.add)
+        if not ahead:
+            act(junk(0, 12), A(gi, 15, P, 16), Act.Sign, bias=96.0, scale=-1.0 / HUGE, acc=sca(10))
+        act(junk(1, P), A(gi, 0, P), Act.Sign, bias=96.0, scale=-1.0 / HUGE, acc=sca(11))
         for b in range(4):
             bank = ("b6", "b7", "b0", "b1")[b]
             mm(bank, ("eb", 128 * b, 128 * b + 128), (x, 0, P))
             lin("hd%d%d" % (t, b), "S", A("hd", b, 4 * P, 4), A(bank, 0, P), 0.5)
-        for k in range(0 if t in ADD else 3):
-            mm("b5", NEG, ("mk", 0, P), k == 0, False)
-        ts(A("ohb", 0, 12), A("mwb", 0, 12), sca(10), None, Op.is_equal)
-        ts(Z("ohh", 0, 12), Z("mwb", 0, 12), sc(10), 0.5, Op.is_equal, Op.mult)
-        lin("s12%d" % t, "V", sc(12), sc(10), -8.0, 112.0)
-        lin("s13%d" % t, "V", sca(13), sca(10), -16.0, sca(11))
-        lin("s14%d" % t, "V", sca(14), sca(13), 0.5, 1.0)
-        lin("s15%d" % t, "V", sc(15), sc(13), -0.5, 16.0)
-        lin("s16%d" % t, "V", sca(16), sca(13), -0.5)
-        ts(A("wft", 1, 512, 2), whole("cw", 256), sca(14), None, Op.is_equal)
-        lin("z35%d" % t, "S", A("zz", XF + 3, XF + 48, 4, 64, 96), A("ohb", 0, 12, 1, 64, 96), sca(16, 64, 96))
-        ts(Z("d0", 33, 48), Z("mw", 1, 16), sc(15), None, Op.is_lt)
-        ts(Z("d1", 48, 64), Z("nk", 0, 16), sc(15), 0.0, Op.add, Op.max)
-        if not last and not ahead:
-            query(t + 1)
-        if last:
+        if not ahead:
+            ts(A("ohb", 0, 12), A("mwb", 0, 12), sca(10), None, Op.is_equal)
+            ts(Z("ohh", 0, 12), Z("mwb", 0, 12), sc(10), 0.5, Op.is_equal, Op.mult)
+            lin("s12%d" % t, "V", sc(12), sc(10), -8.0, 112.0)
+            lin("s13%d" % t, "V", sca(13), sca(10), -16.0, sca(11))
+            lin("s14%d" % t, "V", sca(14), sca(13), 0.5, 1.0)
+            lin("s15%d" % t, "V", sc(15), sc(13), -0.5, 16.0)
+            lin("s16%d" % t, "V", sca(16), sca(13), -0.5)
+            ts(A("wft", 1, 512, 2), whole("cw", 256), sca(14), None, Op.is_equal)
+            lin("z35%d" % t, "S", A("zz", XF + 3, XF + 48, 4, 64, 96), A("ohb", 0, 12, 1, 64, 96), sca(16, 64, 96))
+            ts(Z("d0", 33, 48), Z("mw", 1, 16), sc(15), None, Op.is_lt)
+            ts(Z("d1", 48, 64), Z("nk", 0, 16), sc(15), 0.0, Op.add, Op.max)
             quant("w", 0, 128, whole("wt", 512))
             mm("b2", ("w", 0, 128), (x, 0, P))
             lin("yw0", "S", A("yw", 0, P), A("b2", 0, P))
-        if t > 0:
-            place(t - 1, 2)
-        if ahead:
-            lin("bc%d" % t, "S", A("bc", 0, 32, 1, 0, 64), zero(32, 0, 64), 1.0, sca(11, 0, 64))
-            turn(A("lr", 0, 32, 1, 0, 64), A("bc", 0, 32, 1, 0, 64))
+        else:
             for k in range(2):
-                lin("ky%d%d" % (t, k), "S", sca(36 + k, 0, 64), own_key, 1.0, (-1.0, 1.0)[k])
-                act(junk(9, 32, 0, 64) if k else junk(0, 32, 0, 64), A("lr", 0, 32, 1, 0, 64), Act.Sign, bias=sca(36 + k, 0, 64), scale=-1.0,
+                lin("bc%d%d" % (t, k), "S", A("bc", 32 * k, 32 * k + 32, 1, 0, 64), A("oneb", 0, 32, 1, 0, 64), (1.0, -1.0)[k], sca(11, 0, 64))
+            turn(A("lr", 0, 64, 1, 0, 64), A("bc", 0, 64, 1, 0, 64))
+            for k in range(2):
+                act(junk(9, 32, 0, 64) if k else junk(0, 32, 0, 64), A("lr", 32 * k, 32 * k + 32, 1, 0, 64), Act.Sign, bias=own_key, scale=-1.0,
                     acc=sca(28 + k, 0, 64))
             ts(sca(30, 0, 64), sca(29, 0, 64), sca(28, 0, 64), -500.0, Op.subtract, Op.mult)
             ts(A("hq", 32, 33, 1, 0, 64), sca(30, 0, 64), sca(28, 0, 64), 1160.0, Op.add, Op.add)
 
-        mm("b5", (land, at, at + 128), (x, 0, P), t in ADD, True)
+        mm("b5", (land, at, at + 128), (x, 0, P))
         for b in range(4):
             mm(("b6", "b7", "b4", "b1")[b], ("eb", 128 * b, 128 * b + 128), (land, at, at + 128))
-
-        def half(b):
-            lin("ha%d%d" % (t, b), "S", A("ha", b, 128, 4), A(("b6", "b7", "b4", "b1")[b], 0, K), 0.5)
-        if t in ADD:
-            tt(Z("zm", 0, P), A("b5", 0, P, 1, 0, L), Z("mr", 0, P), Op.subtract)
-        scan(Z("pm", 17, 17 + P), Z("zm" if t in ADD else "b5", 0, P), zero(P, 0, L), LOW, Op.max, Op.add)
+        tt(Z("zm", 0, P), A("b5", 0, P, 1, 0, L), Z("mr", 0, P), Op.subtract)
+        scan(Z("pm", 17, 17 + P), Z("zm", 0, P), zero(P, 0, L), LOW, Op.max, Op.add)
         top = Z("pm", P + 16, P + 17)
         act(Z("uut", 2, 4 * (17 + P), 4), Z("pm", 0, 17 + P), Act.Sign, bias=top, scale=-1.0, acc=sc(1))
         act(junk(2, 12, 0, L), Z("pm", 16, 1 + P, 16), Act.Sign, bias=top, scale=-1.0, acc=sc(0))
         lo = 0 if ahead else 32
         act(Z("zz", 4 * lo + 1, XF, 4), Z("dm", lo, 40), Act.Relu, scale=sc(0), bias=sc(1))
         lin("xo%d" % t, "V", Z("zz", 4 * lo, XF, 4), Z("d16", lo, 40), sc(0))
-        lin("tb%d" % t, "S", Z("tb", 0, 32), Z("up32", 0, 32), sc(1))
-        lin("s3%d" % t, "S", sc(3), sc(0), -16.0, sc(1))
-        ts(Z("oha", 0, 12), Z("mw", 1, 13), sc(0), None, Op.is_equal)
-        lin("s2%d" % t, "S", sc(2), sc(0), -16.0, cf(9, L))
-        lin("xa0%d" % t, "S", Z("xa", 0, 24, 2), Z("oha", 0, 12), sc(2))
-        lin("s4%d" % t, "S", sc(4), sc(3), -1.0, cf(10, L))
-        lin("xa1%d" % t, "S", Z("xa", 1, 24, 2), Z("oha", 0, 12), sc(4))
+        if not ahead:
+            lin("tb%d" % t, "S", Z("tb", 0, 32), Z("up32", 0, 32), sc(1))
+            lin("s3%d" % t, "S", sc(3), sc(0), -16.0, sc(1))
+            ts(Z("oha", 0, 12), Z("mw", 1, 13), sc(0), None, Op.is_equal)
+            lin("s2%d" % t, "S", sc(2), sc(0), -16.0, cf(9, L))
+            lin("xa0%d" % t, "S", Z("xa", 0, 24, 2), Z("oha", 0, 12), sc(2))
+            lin("s4%d" % t, "S", sc(4), sc(3), -1.0, cf(10, L))
+            lin("xa1%d" % t, "S", Z("xa", 1, 24, 2), Z("oha", 0, 12), sc(4))
         for b in range(4):
-            half(b)
+            lin("ha%d%d" % (t, b), "S", A("ha", b, 128, 4), A(("b6", "b7", "b4", "b1")[b], 0, K), 0.5)
         quant("xo", 0, 128, A("zz", 0, 512))
         mm("b3", X1, ("xo", 0, 128))
         ts(A("om", 0, 8), A("b3", 32, 40), 4.0, cf(4), Op.mult, Op.add)
@@ -562,14 +572,13 @@ def rank_program(g, core, T, topo):
             mm("b5", X1, ("uu", 0, P))
             mm("b2", X2, ("uu", 0, P))
             act(junk(4, P), A("b5", 0, P), Act.Sign, bias=0.5, scale=-1.0, acc=sca(17))
-            act(junk(5, P), A("b2", 0, P), Act.Sign, bias=0.5, scale=-1.0, acc=sca(18))
-            act(junk(6, P), A(gi, 0, P), Act.Sign, bias=sca(17), scale=-2.0 / unit, acc=sca(19))
-            turn(A("kb", 0, 32, 1, 96, 128), A("b0", 0, 32, 1, 96, 128))
+            act(junk(5, P), A("b2", 0, P), Act.Sign, bias=cf(25), scale=-1.0, acc=sca(18))
+            act(junk(6, P), A(gi, 0, P), Act.Sign, bias=sca(17), scale=-2.0 / HUGE, acc=sca(19))
+            turn(A("kb", 0, 32, 1, 64, 128), A("b0", 0, 32, 1, 64, 128))
             ts(A("hq", 0, 32, 1, 0, 64), A("b0", 0, 32, 1, 0, 64), A("kb", 0, 1, 1, 0, 64), 4000.0, Op.not_equal, Op.mult)
             red(sca(27, 0, 64), A("hq", 0, 33, 1, 0, 64), Op.min)
-            ts(sca(21, 0, 64), sca(18, 0, 64), sca(27, 0, 64), -HUGE, Op.is_gt, Op.mult)
-            ts(sca(21, 64, 96), sca(18, 64, 96), sca(17, 64, 96), -HUGE, Op.not_equal, Op.mult)
-            ts(sca(21, 96, 128), sca(18, 96, 128), sca(17, 96, 128), -HUGE, Op.is_equal, Op.mult)
+            lin("xd%d" % t, "S", sca(27, 64, 128), sca(17, 64, 128), A("cf", 23, 24, 1, 64, 128), A("cf", 24, 25, 1, 64, 128))
+            ts(sca(21), sca(18), sca(27), -HUGE, Op.is_gt, Op.mult)
             lin("bl%d" % t, "S", A("bc", 64, 96), zero(32), 1.0, sca(19))
             turn(A("pl", 64, 96), A("bc", 64, 96))
             lin("kl%d" % t, "S", A("kb", 0, 1, 1, 64, 96), sca(19, 64, 96))
@@ -577,20 +586,40 @@ def rank_program(g, core, T, topo):
             lin("t0%d" % t, "S", A("th2", 0, 96), whole("pl", 96), TINY, sca(26))
             lin("t1%d" % t, "S", A("th2", 96, 128), A("b0", 0, 32), TINY, sca(26))
             ts(A("c2t", 1, 512, 4), eye, sca(21), -32.0 / HUGE, Op.mult, Op.mult)
-        turn(Z("tt", 0, 32), Z("tb", 0, 32))
-        ts(Z("ne", 0, 32), Z("tt", 0, 32), sc(1), None, Op.is_equal)
-        ts(Z("wft", 0, 512, 2), Z("cw", 0, 256), sc(3), None, Op.is_equal)
-        scan(Z("ms", 0, 64), Z("ne", 0, 64), zero(64, 0, L), 0.0, Op.max, Op.max)
-        lin("s9%d" % t, "S", sc(9), Z("ms", 31, 32), -1.0, 1.0)
-        lin("s5%d" % t, "S", sc(5), Z("ms", 31, 32))
-        lin("zx%d" % t, "S", Z("zz", XF, XF + 48, 2), Z("xa", 0, 24), sc(9))
+
+            def up(k):
+                return sca(k, 64, 128)
+            key = A("kb", 0, 1, 1, 64, 128)
+            act(junk(0, 12, 64, 128), A("m32", 0, 12, 1, 64, 128), Act.Sign, bias=key, scale=-1.0, acc=up(10))
+            lin("u12%d" % t, "S", up(12), up(10), -16.0, key)
+            lin("u13%d" % t, "S", up(13), up(10), -8.0, A("cf", 21, 22, 1, 64, 128))
+            lin("u14%d" % t, "S", up(14), up(12), -0.5, A("cf", 22, 23, 1, 64, 128))
+            lin("u15%d" % t, "S", up(15), up(21), 1.0 / HUGE, 1.0)
+            ts(A("ohb", 0, 12, 1, 64, 128), A("mwb", 1, 13, 1, 64, 128), up(10), up(15), Op.is_equal, Op.mult)
+            ts(A("wft", 0, 512, 2, 64, 128), A("cx", 0, 256, 1, 64, 128), up(12), None, Op.is_equal)
+            for b in range(2):
+                lin("ux%d%d" % (t, b), "S", A("zz", XF + 2 * b, XF + 48, 4, 64, 128), A("ohb", 0, 12, 1, 64, 128), up(13 + b))
+            aim = A("kb", 1, 2, 1, 64, 96)
+            ts(sca(23, 64, 96), sca(19, 64, 96), aim, -0.5, Op.add, Op.mult)
+            ts(sca(24, 64, 96), sca(23, 64, 96), -193.0, sca(15, 64, 96), Op.add, Op.mult)
+            lin("u25%d" % t, "S", sca(25, 64, 96), aim, 0.5, 96.0)
+            lin("utg%d" % t, "S", A("tgb", t, t + 1, 1, 64, 96), sca(24, 64, 96), 1.0, sca(25, 64, 96))
+            dma("Y", T.tg[t:t + 1, :], T.tgb[64:96, t:t + 1], [A("tgb", t, t + 1, 1, 64, 96)], [], 4)
+        else:
+            turn(Z("tt", 0, 32), Z("tb", 0, 32))
+            ts(Z("ne", 0, 32), Z("tt", 0, 32), sc(1), None, Op.is_equal)
+            ts(Z("wft", 0, 512, 2), Z("cw", 0, 256), sc(3), None, Op.is_equal)
+            scan(Z("ms", 0, 64), Z("ne", 0, 64), zero(64, 0, L), 0.0, Op.max, Op.max)
+            lin("s9%d" % t, "S", sc(9), Z("ms", 31, 32), -1.0, 1.0)
+            lin("s5%d" % t, "S", sc(5), Z("ms", 31, 32))
+            lin("zx%d" % t, "S", Z("zz", XF, XF + 48, 2), Z("xa", 0, 24), sc(9))
+            turn(Z("d1", 0, 32), Z("ms", 32, 64))
+            scan(Z(cr, 0, 64), Z("d0", 0, 64), Z("d1", 0, 64), cf(12, L), Op.mult, Op.add)
+            act(junk(10, 64, 0, L), Z(cr, 0, 64), Act.Sign, scale=-1.0, acc=sc(7))
+            ts(sc(6), Z(cr, 31, 32), 0.0, sc(12), Op.is_gt, Op.mult)
+            lin("z1%d" % t, "V", Z("zz", XF + 1, XF + 48, 4), Z("ohb", 0, 12), sc(6))
+            lin("z3%d" % t, "S", Z("zz", XF + 3, XF + 48, 4), Z("ohh", 0, 12), sc(7))
         quant("wf", 0, 128, whole("wft", 512))
-        turn(Z("d1", 0, 32), Z("ms", 32, 64))
-        scan(Z(cr, 0, 64), Z("d0", 0, 64), Z("d1", 0, 64), cf(12, L), Op.mult, Op.add)
-        act(junk(10, 64, 0, L), Z(cr, 0, 64), Act.Sign, scale=-1.0, acc=sc(7))
-        ts(sc(6), Z(cr, 31, 32), 0.0, sc(12), Op.is_gt, Op.mult)
-        lin("z1%d" % t, "V", Z("zz", XF + 1, XF + 48, 4), Z("ohb", 0, 12), sc(6))
-        lin("z3%d" % t, "S", Z("zz", XF + 3, XF + 48, 4), Z("ohh", 0, 12), sc(7))
         quant("xf", 0, 128, A("zz", XF, XF + 512))
         mm("b3" if ahead else "b2", ("wf", 0, 128), ("xf", 0, 128))
         copy(A("of", 0, 12), A("b3" if ahead else "b2", 0, 12))
@@ -606,9 +635,8 @@ def rank_program(g, core, T, topo):
                 pick("yo%d" % a, "S", A("yo", 16 * a, 16 * b), A("yw", 0, 256), A("of", a, b))
                 pick("xs3%d" % a, "VS"[a // 6], A(nx + "s", 16 * a, 16 * b), A(v + "s", 0, 256), A("of", a, b))
             dma("Y", T.oc[:, :], T.x3q[:, 0:P].bitcast(dt.uint8), [A("x3q", 0, P)], [], 4 * P)
-            dma(MOVE.get("oy", "Y"), T.y[:, :], T.yo[:, 0:P], [A("yo", 0, P)], [], 4 * P)
+            dma("Y", T.y[:, :], T.yo[:, 0:P], [A("yo", 0, P)], [], 4 * P)
             for k in range(4):
-                dma(MOVE.get("oz%d" % k, "YS"[k % 2]), T.osc[4 * k:4 * k + 4, :], T.x3s[32 * k:32 * k + 4, 0:P], [A("x3s", 0, P)], [], 8)
-            place(t, 1)
-            place(t, 2)
+                dma("YS"[k % 2], T.osc[4 * k:4 * k + 4, :], T.x3s[32 * k:32 * k + 4, 0:P], [A("x3s", 0, P)], [], 8)
+            place(t)
     emit()

from concourse.mybir import dt, AluOpType as Op, AxisListType, ActivationFunctionType as Act

N, P, K, R = 8, 192, 32, 3
CAND = (1, 2)
TINY = 2.0 ** -100
LOW = -1e29
HUGE = 2.0 ** 80
XF, Z0 = 160, 208
ORDER = """
6 1 2 0 27 7 10 9 11 23 22 20 21 5 24 25 26 58 29 121 28 41 43 49 3 36 40 39 44 42 37 4 38 30 32 33 31 48 46 45 34 152 150 148 126 47 88 59 125 120 91 154 64 65 66 67 35 12 157 18 17 13 51 16 159 53 158 54 50 85 15 52 149 117 151 93 122 89 113 155 128 92 153 136 133 134 289 60 8 68 69 63 129 131 109 124 70 72 71 73 56 135 74 75 80 156 77 76 137 78 138 119 115 285 79 123 118 61 180 160 161 162 163 181 100 284 139 182 164 186 165 99 166 102 283 108 290 101 184 183 62 288 287 130 110 142 292 187 114 185 81 82 86 95 167 190 188 169 170 191 286 192 193 291 189 96 97 83 199 144 105 141 143 107 111 103 116 132 87 112 203 200 202 201 204 94 194 172 175 171 145 196 195 205 206 140 98 221 197 146 207 222 173 209 208 224 174 226 210 211 147 214 168 213 176 198 212 215 223 225 216 230 229 217 232 228 227 231 177 233 234 236 178 179 294 293 14 84 55 218 220 219 235 237 240 245 241 239 246 238 263 264 265 242 127 243 244 248 249 252 247 266 255 256 267 269 268 270 257 272 258 271 275 259 273 276 260 262 261 295 296 297 298 278 279 57 274 280 250 277 299 300 251 301 314 318 320 315 319 90 333 316 321 302 338 253 339 317 303 327 326 334 324 336 304 341 340 355 309 342 307 328 325 343 330 329 356 335 322 337 305 323 348 346 347 331 345 344 332 358 306 360 357 349 359 308 362 361 364 363 350 366 365 310 351 311 370 368 312 367 352 313 369 371 379 375 384 373 385 374 380 397 398 372 377 376 382 378 383 399 381 400 401 403 406 389 390 402 391 404 407 405 408 409 282 254 353 354 281 19 392 417 410 396 386 394 411 418 412 413 395 393 387 104 419 442 420 421 422 434 423 424 414 427 428 435 437 445 443 432 431 106 450 436 451 444 439 452 429 440 430 438 441 425 446 448 449 456 453 454 457 465 426 459 455 472 467 473 474 468 447 475 458 479 461 463 466 476 433 477 464 462 469 480 485 460 481 482 478 483 484 504 470 506 471 486 507 489 503 505 490 508 509 416 415 510 388 487 488 494 491 495 492 497 498 496 493 502 500 501 499
"""
MOVE = {_w[:-1]: _w[-1] for _w in """
cz3V cw0S cw1S d0aV d0cV dmV wf1G wf2S cxS cy2S cy3S cy0S wc32S wc3V wd0S wd1S x22S r10S r11S r12S q13S r13S cm10V hd03V xo0S ha02V ha03V bk0V t10V u150V utg0V q21S r21S q22S r22S q23S hd12V hd13V ha10V ha11V ha12V ha13V xd1V bk1V t11V utg1V hd20V hd23V s122S s132S s142S s162S tb2V z12S yw1V p242S
""".split()}

MXC, U8, F32, BF, I32, U16 = "float8_e4m3fn_x4", "uint8", "float32", "bfloat16", "int32", "uint16"
SCRATCH = {}


def _buf(name, cols, dtype, where="sbuf"):
    SCRATCH[name] = (where, [128, cols], dtype)


def _pair(name, cols):
    _buf(name + "q", cols, MXC)
    _buf(name + "s", cols, U8)


for _t in range(R):
    _pair("x%d" % _t, P)
    _pair("v%d" % _t, P + 160)
    _pair("n%d" % _t, K)
    _pair("u%d" % _t, 320)
    _buf("sc%d" % _t, 48, F32)
    _buf("cr%d" % _t, 64, F32)
    _buf("gi%d" % _t, P, BF)
    if _t in CAND:
        _pair("cd%d" % _t, 224)
_pair("x3", P)
for _n, _c in (("w", 128), ("eb", 512), ("kc", 512), ("e", 128), ("cm", P), ("xo", 128), ("wf", 128), ("xf", 128),
               ("uu", P), ("c2", 128), ("wk", 256)):
    _pair(_n, _c)
for _n, _c in (("ct", 4 * P), ("ut", 16), ("wt", 512), ("ub", 1280), ("st", 520), ("k1", 512), ("et", 512), ("cmt", 4 * P),
               ("zz", Z0 + 4 * P), ("wft", 512), ("mt", 512), ("oneb", 512), ("er", 256), ("cw", 256), ("rb", 128),
               ("rk", 2 * P), ("th", 512), ("up32", 32), ("un", 16), ("cm2", 4 * P), ("uut", 840), ("c2t", 512), ("wc", 512),
               ("kr", P), ("cx", 256), ("sg", 3 * P), ("jk", 2240)):
    _buf(_n, _c, BF)
for _n, _c in (("mw", 64), ("d0", 64), ("d1", 64), ("ms", 64), ("d16", 40), ("dm", 40), ("cf", 32), ("oh", 48),
               ("zm", P), ("pm", 216), ("tb", 64), ("ne", 64), ("dg", 40), ("xa", 24), ("hd", 4 * P), ("ha", 128),
               ("yw", 256), ("yo", P), ("tgb", 16), ("kb", 32), ("pl", 96), ("bc", 200), ("th2", 128)):
    _buf(_n, _c, F32)
_buf("ic", 16, I32)
_buf("ol", 2, U16)
_buf("om", 8, U16)
_buf("of", 12, U16)
_buf("oo", 4, U16)
for _n in range(8):
    _buf("b%d" % _n, 512, F32, "psum")
SHARE = {"rk0": ("rk", 0), "rk1": ("rk", P), "th0": ("th", 64), "th1": ("th", 0), "thn": ("th", 256), "go": ("sg", P), "mr": ("sg", 2 * P),
         "ohb": ("oh", 0), "ohh": ("oh", 16), "oha": ("oh", 32), "tt": ("tb", 32), "lr": ("bc", 136), "mwb": ("mw", 16), "m32": ("mw", 32),
         "nk": ("mw", 48), "hq": ("bc", 96)}

SEMAPHORES = ["sv", "ss", "stn", "sg"] + ["dm%d" % k for k in range(48)] + ["arr%d" % k for k in range(R)] + ["sent%d" % k for k in range(R)]


def _cross(a, b):
    if a[1] >= b[2] or b[1] >= a[2] or a[3] >= b[4] or b[3] >= a[4]:
        return False
    m = min(a[5], b[5])
    if m > 1 and a[5] % m == 0 and b[5] % m == 0:
        return (a[3] - b[3]) % m == 0
    return True


def _within(a, b):
    if not (a[1] <= b[1] and b[2] <= a[2] and a[3] <= b[3] and b[4] <= a[4]):
        return False
    return a[5] == 1 or (a[5] == b[5] and (a[3] - b[3]) % a[5] == 0)


def rank_program(g, core, T, topo):
    rank = T.rank_of(core)
    if rank is None:
        return
    queue = {"V": g.vector, "S": g.scalar, "T": g.tensor, "G": g, "Y": g.sync}
    own = {"V": "sv", "S": "ss", "T": "stn", "G": "sg"}
    log = {}
    nodes = []
    dmas = [0]

    def A(name, c0, c1, step=1, p0=0, p1=128):
        name, at = SHARE.get(name, (name, 0))
        return (name, p0, p1, at + c0, at + c1, step)

    def ap(x):
        return T[x[0]][x[1]:x[2], x[3]:x[4]:x[5]] if x[5] > 1 else T[x[0]][x[1]:x[2], x[3]:x[4]]

    def psum(x):
        return SCRATCH[x[0]][0] == "psum"

    def add(q, reads, writes, kind, issue, sem=None, val=0, tag=None):
        after = {}
        node = {"q": q, "n": len(nodes), "after": after, "k": kind, "r": reads, "w": writes, "issue": issue, "sem": sem, "val": val, "tag": tag}
        for views, w in ((reads, False), (writes, True)):
            for x in views:
                for y, m, yw in log.get(x[0], []):
                    if psum(x):
                        if q == "T" and m["q"] == "T":
                            after.setdefault(m["n"], False)
                        elif q != m["q"] or w or yw or tag or m["tag"]:
                            after[m["n"]] = True
                    elif (w or yw) and _cross(x, y):
                        after[m["n"]] = True
        for x in writes:
            log[x[0]] = [e for e in log.get(x[0], []) if not _within(x, e[0]) or (psum(x) and q == "T" and e[1]["q"] == "T")]
        for views, w in ((reads, False), (writes, True)):
            for x in views:
                log.setdefault(x[0], []).append((x, node, w))
        nodes.append(node)
        return node

    def dma(q, out, in_, reads, writes, size):
        dmas[0] += 1
        return add(q, reads, writes, ("dma", size), lambda: queue[q].dma_start(out, in_), "dm%d" % (dmas[0] - 1), 16)

    def emit():
        count = {"V": 0, "S": 0, "T": 0, "G": 0}
        known = {q: {} for q in queue}
        every = {}
        done = [int(k) for k in ORDER.split()]
        at = {k: i for i, k in enumerate(done)}
        assert sorted(done) == list(range(len(nodes))) and all(at[d] < at[m["n"]] for m in nodes for d in m["after"])
        for k in done:
            m = nodes[k]
            q = m["q"]
            if q in queue:
                for d in sorted(m["after"], reverse=True, key=lambda i: at[i]):
                    o = nodes[d]
                    if not m["after"][d] or known[q].get(o["sem"], 0) >= o["val"]:
                        continue
                    queue[q].wait_ge(T.sem[o["sem"]], o["val"])
                    for s, v in list(o["clock"].items()) + [(o["sem"], o["val"])]:
                        known[q][s] = max(known[q].get(s, 0), v)
            if m["sem"] is None:
                count[q] += 1
                m["sem"], m["val"] = own[q], count[q]
                m["issue"]().then_inc(T.sem[own[q]], 1)
            elif m["issue"] is not None:
                ins = m["issue"]()
                if m["sem"][0:4] != "sent":
                    ins.then_inc(T.sem[m["sem"]], 16)
            m["clock"] = dict(known.get(q, {}))
            every.pop(m["sem"], None)
            every[m["sem"]] = m["val"]
        for s in every:
            g.wait_ge(T.sem[s], every[s])

    V, S = g.vector, g.scalar

    def val(s):
        return ap(s) if isinstance(s, tuple) else s

    def fill(x, v):
        add("V", [], [x], "fill", lambda: V.memset(ap(x), v))

    def copy(o, i):
        add("V", [i], [o], "v", lambda: V.tensor_copy(ap(o), ap(i)))

    def ts(o, i, s1, s2, op0, op1=None):
        rd = [i] + [s for s in (s1, s2) if isinstance(s, tuple)]
        if op1 is None:
            add("V", rd, [o], "v", lambda: V.tensor_scalar(ap(o), ap(i), val(s1), None, op0))
        else:
            add("V", rd, [o], "v", lambda: V.tensor_scalar(ap(o), ap(i), val(s1), val(s2), op0, op1))

    def tt(o, i0, i1, op):
        add("V", [i0, i1], [o], "tt", lambda: V.tensor_tensor(ap(o), ap(i0), ap(i1), op))

    def red(o, i, op, size=False):
        if size:
            add("V", [i], [o], "red", lambda: V.tensor_reduce(ap(o), ap(i), AxisListType.X, op, apply_absolute_value=True))
        else:
            add("V", [i], [o], "red", lambda: V.tensor_reduce(ap(o), ap(i), AxisListType.X, op))

    def scan(o, d0, d1, init, op0, op1):
        rd = [d0, d1] + ([init] if isinstance(init, tuple) else [])
        add("V", rd, [o], "scan", lambda: V.tensor_tensor_scan(ap(o), ap(d0), ap(d1), val(init), op0, op1))

    def turn(o, i):
        add("V", [i], [o], "v", lambda: V.transpose(ap(o), ap(i)))

    def act(o, i, f=Act.Identity, bias=0.0, scale=1.0, acc=None):
        rd = [i] + [s for s in (bias, scale) if isinstance(s, tuple)]
        if acc is None:
            add("S", rd, [o], "act", lambda: S.activation(ap(o), ap(i), f, bias=val(bias), scale=val(scale)))
        else:
            add("S", rd, [o, acc], "acc", lambda: S.activation(ap(o), ap(i), f, bias=val(bias), scale=val(scale), accum_out=ap(acc)))

    def lin(tag, q, o, i, scale=1.0, bias=0.0):
        rd = [i] + [s for s in (bias, scale) if isinstance(s, tuple)]
        if MOVE.get(tag, q) == "S":
            add("S", rd, [o], "lin", lambda: S.activation(ap(o), ap(i), Act.Identity, bias=val(bias), scale=val(scale)), tag=tag)
        else:
            add("V", rd, [o], "lin", lambda: V.tensor_scalar(ap(o), ap(i), val(scale), val(bias), Op.mult, Op.add), tag=tag)

    def quant(n, c0, c1, i):
        q, s = A(n + "q", c0, c1), A(n + "s", c0, c1)
        add("V", [i], [q, s], "quant", lambda: V.quantize_mx(ap(q), ap(s), ap(i)))

    def mm(o, l, r, start=True, stop=True):
        lq, ls, rq, rs = A(l[0] + "q", l[1], l[2]), A(l[0] + "s", l[1], l[2]), A(r[0] + "q", r[1], r[2]), A(r[0] + "s", r[1], r[2])
        x = A(o, 0, r[2] - r[1])
        return add("T", [lq, ls, rq, rs], [x], "mm", lambda: g.tensor.matmul_mx(ap(x), ap(lq), ap(ls), ap(rq), ap(rs), start, stop))

    def pick_codes(o, i, off):
        add("V", [i, off], [o], "pick", lambda: V.tensor_copy(ap(o).bitcast(dt.uint32), ap(i).bitcast(dt.uint32).indirect(ap(off))))

    def pick(tag, q, o, i, off):
        if MOVE.get(tag, q) == "S":
            add("S", [i, off], [o], "pick", lambda: S.activation(ap(o), ap(i).indirect(ap(off)), Act.Copy), tag=tag)
        else:
            add("V", [i, off], [o], "pick", lambda: V.tensor_copy(ap(o), ap(i).indirect(ap(off))), tag=tag)

    def iota(o, pattern, base, cm):
        if SCRATCH[o[0]][2] != I32:
            add("G", [], [o], "iota", lambda: g.iota(ap(o), pattern, base, cm, allow_small_or_imprecise_dtypes=True))
        else:
            add("G", [], [o], "iota", lambda: g.iota(ap(o), pattern, base, cm))

    def const(tag, q, o, v):
        if MOVE.get(tag, q) == "V":
            add("V", [], [o], "const", lambda: V.memset(ap(o), float(v)), tag=tag)
        else:
            n = (o[4] - o[3] + o[5] - 1) // o[5]
            add("G", [], [o], "const", lambda: g.iota(ap(o), [[0, n]], v, 0, allow_small_or_imprecise_dtypes=True), tag=tag)

    def sel(o, i, pattern, op, base, cm):
        add("G", [i], [o], "sel", lambda: g.affine_select(ap(o), ap(i), pattern, op, 0.0, base, cm))

    def move(o, i, q="Y"):
        code = SCRATCH[o[0]][2] == MXC
        n = (o[4] - o[3]) * {MXC: 4, U8: 1, BF: 2, F32: 4}[SCRATCH[o[0]][2]]
        return dma(q, ap(o).bitcast(dt.uint8) if code else ap(o), ap(i).bitcast(dt.uint8) if code else ap(i), [i], [o], n)

    def move_pair(o, a, i, b, n):
        move(A(o + "q", a, a + n), A(i + "q", b, b + n))
        move(A(o + "s", a, a + n), A(i + "s", b, b + n))

    L = 32

    def whole(n, c):
        return A(n, 0, c)

    def Z(n, c0, c1, step=1):
        return A(n, c0, c1, step, 0, L)

    def cf(k, p1=128):
        return A("cf", k, k + 1, 1, 0, p1)

    def zero(n, p0=0, p1=128):
        return A("zz", Z0, Z0 + n, 1, p0, p1)

    def junk(k, n, p0=0, p1=128):
        return A("jk", 200 * k, 200 * k + n, 1, p0, p1)

    lc = dma("Y", T.ct[:, :], T.c[:, :], [], [whole("ct", 4 * P)], 8 * P)
    dma("S", T.ut[:, 0:16], T.u[:, 0:16], [], [whole("ut", 16)], 32)

    fill(A("zz", Z0, Z0 + 4 * P), 0.0)
    fill(A("zz", 0, Z0), 0.0)
    fill(whole("thn", 256), -TINY)
    fill(whole("oneb", 512), 1.0)
    iota(A("ic", 0, 1), [[0, 1]], 0, 1)
    iota(whole("er", 256), [[0, 8], [1, 16], [16, 2]], 0, 0)
    sel(whole("th1", 256), whole("thn", 256), [[-1, 256]], Op.is_gt, 64, 1)
    lin("cz1", "S", A("cmt", 1, 4 * P, 4, 0, 64), zero(P, 0, 64))
    lin("ez1", "S", A("et", 1, 512, 2, 0, 64), zero(256, 0, 64))
    for b in (2, 3):
        lin("cz%d" % b, "S", A("cmt", b, 4 * P, 4), zero(P))
    tiles = [whole("st", 520), A("mt", 128, 512), A("uut", 64, 64 + 4 * P), whole("cm2", 4 * P), whole("c2t", 512)]
    for x in tiles:
        move(x, zero(x[4] - x[3]))["after"][lc["n"]] = True
    move(whole("wc", 512), whole("oneb", 512))["after"][lc["n"]] = True
    dma("Y", T.wt[:, :], T.w[:, :], [], [whole("wt", 512)], 1024)["after"][lc["n"]] = True
    for k, m in ((1, 15), (2, 31), (3, 3)):
        ts(A("ic", k, k + 1), A("ic", 0, 1), m, None, Op.bitwise_and)
    ts(A("ic", 4, 5), A("ic", 0, 1), 2, 7, Op.arith_shift_right, Op.bitwise_and)
    copy(A("cf", 16, 21), A("ic", 0, 5))
    c_p, c_lo, c_g, c_b, c_m = (cf(k) for k in range(16, 21))
    lin("c0", "S", cf(0), c_lo, -1.0, c_p)
    lin("c1", "S", cf(1), c_lo)
    fill(A("cf", 2, 4, 1, 0, 64), 0.0)
    lin("c2", "S", A("cf", 2, 3, 1, 64, 128), A("cf", 0, 1, 1, 64, 128), 1.0, 64.0)
    lin("c3", "S", A("cf", 3, 4, 1, 64, 128), A("cf", 17, 18, 1, 64, 128))
    for e, k in ((0, 0), (6, 0), (8, 1), (14, 1)):
        lin("jt%d" % e, "S", A("zz", e, e + 2), A("cf", k, 4, 2))
    quant("kc", 0, 128, whole("zz", 512))
    fill(A("zz", 0, 16), 0.0)
    quant("kc", 128, 256, whole("oneb", 512))
    JT, ONES, X1, X2, W0, W1 = ("kc", 0, 128), ("kc", 128, 256), ("kc", 256, 384), ("kc", 384, 512), ("wk", 0, 128), ("wk", 128, 256)

    def query(t):
        n = P if t == 0 else 128
        for b in range(4):
            one = A("ut", 4 * t + b, 4 * t + b + 1)
            lin("q%d%d" % (t, b), "V" if t > 0 or b < 2 else "S", A("ub", 512 + b, 512 + 4 * n, 4), zero(n), 1.0, one)
            if t == 0:
                ts(A("ub", b, 512, 4), A("oneb", 0, 128), one, -1.0, Op.mult, Op.mult)
            else:
                lin("r%d%d" % (t, b), "V", A("ub", b, 512, 4), zero(128), 1.0, A("un", 4 * t + b, 4 * t + b + 1))
        quant("u%d" % t, 0, 128, A("ub", 0, 512))
        quant("u%d" % t, 128, 128 + n, A("ub", 512, 512 + 4 * n))
        if n < P:
            move_pair("u%d" % t, 256, "u%d" % t, 128, 64)

    query(0)
    lin("un", "S", whole("un", 12), whole("ut", 12), -1.0)
    quant("x0", 0, P, whole("ct", 4 * P))
    quant("v0", P + K, P + 160, zero(512))
    for t in range(R):
        if t + 1 in CAND:
            move_pair("cd%d" % (t + 1), 96, "v0", P + K, 128)
        elif t > 0:
            move_pair("v%d" % t, P + K, "v0", P + K, 128)
    fill(Z("pm", 0, 17), LOW)
    fill(Z("dg", 32, 33), 95.5)
    for b in range(2):
        lin("cw%d" % b, "V", A("cw", b, 256, 2), A("er", 0, 256, 2), 1.0, 1.0)
    iota(whole("mw", 16), [[1, 16]], 0, 0)
    lin("nk", "S", Z("nk", 0, 16), Z("mw", 0, 16), -1.0)
    lin("mwb", "S", whole("mwb", 13), whole("mw", 13), 2.0, -12.0)
    eye = A("st", 3, 515, 4)
    sel(eye, A("oneb", 0, 128), [[-1, 128]], Op.is_equal, 0, 1)

    def columns():
        iota(whole("rb", 128), [[0, 8], [1, 4], [0, 4]], 0, 0)
        sel(Z("up32", 0, 32), Z("oneb", 0, 32), [[1, 32]], Op.is_gt, 0, -1)
        lin("c7", "S", cf(7), c_lo, -1.0, c_g)
        lin("c10", "S", cf(10), c_lo, 1.0, 1.0)
        lin("c9", "S", cf(9), cf(7), 1.0, 240.0)
        lin("c15", "S", cf(15), c_g, -HUGE, 95.5 * HUGE)
        lin("c12", "S", cf(12), c_g, -1.0, -0.5)
        lin("c4", "S", cf(4), c_b, 1.0, -68.0)
        for b in range(2):
            ts(A("k1", b, 512, 4), whole("rb", 128), c_b, None, Op.is_equal)
        sel(A("k1", 2, 512, 4), A("oneb", 0, 128), [[0, 4], [1, 32]], Op.is_gt, 0, -1)
        lin("k13", "V", A("k1", 3, 512, 4), A("k1", 2, 512, 4))
        quant("kc", 256, 384, whole("k1", 512))
        for b in range(4):
            quant("eb", 128 * b, 128 * b + 128, A("st", 3 - b, 515 - b))

    def later():
        const("ne", "G", Z("ne", 32, 64), 0)
        const("d0a", "G", Z("d0", 0, 32), 1)
        const("d0b", "G", Z("d0", 32, 33), -1)
        const("d0c", "G", Z("d0", 48, 64), 0)
        const("d1", "G", Z("d1", 32, 48), 0)
        ts(Z("d16", 32, 40), Z("mw", 0, 8), A("cf", 20, 21, 1, 0, L), 16.0, Op.is_equal, Op.mult)
        lin("d16", "S", Z("d16", 0, 32), Z("st", 3, 131, 4), 16.0)
        lin("dm", "S", Z("dm", 0, 40), Z("d16", 0, 40), 61.5, -1000.0)
        const("wf0", "G", A("wft", 0, 512, 4), 1)
        const("wf1", "V", A("wft", 1, 512, 2), 0)
        lin("wf2", "V", A("wft", 2, 512, 4), A("cw", 0, 256, 2), 1.0, -1.0)
        lin("zz0", "S", A("zz", XF, XF + 48, 4, 32, 33), A("mw", 0, 12, 1, 32, 33), 16.0)
        lin("zz2", "S", A("zz", XF + 2, XF + 48, 4, 32, 33), A("oneb", 0, 12, 1, 32, 33))

    def candidates():
        iota(whole("kr", P), [[2, P]], -P, 0)
        lin("cx", "V", whole("cx", 256), whole("cw", 256), 2.0, -34.0)
        lin("m32", "S", whole("m32", 12), whole("mw", 12), 32.0, -193.0)
        lin("c21", "S", cf(21), cf(0), 1.0, 48.0)
        lin("c22", "S", cf(22), c_lo, 1.0, -16.0)
        lin("c23", "S", cf(23), c_p, 0.0, 1.0)
        lin("c23b", "S", A("cf", 23, 24, 1, 64, 96), A("cf", 16, 17, 1, 64, 96), 0.0, -1.0)
        lin("c24", "S", cf(24), cf(23), -1.0)
        lin("c25", "S", cf(25), cf(23), 0.5)
        lin("c13", "S", cf(13), c_lo, -2.0, -1.0)
        lin("c14", "S", cf(14), cf(0), 2.0)
        for b in (2, 3):
            lin("cy%d" % b, "V", A("c2t", b, 512, 4, 32, 33), A("oneb", 0, 128, 1, 32, 33))
            lin("xc%d" % b, "S", A("zz", b - 2, 128, 4, 32, 33), A("oneb", 0, 32, 1, 32, 33))
        lin("cy0", "V", A("c2t", 2, 512, 4, 0, 1), A("cw", 0, 256, 2, 0, 1), 1.0, -1.0)
        iota(A("c2t", 3, 512, 4, 0, 1), [[1, 8], [0, 16]], 0, 0)
        lin("wc32", "V", A("wc", 2, 512, 4, 32, 33), A("cw", 0, 256, 2, 32, 33), -1.0, 1.0)
        lin("wc2", "S", A("wc", 2, 512, 4, 0, 1), A("oneb", 0, 128, 1, 0, 1), 1.0 / 256)
        lin("wc3", "S", A("wc", 3, 512, 4, 0, 1), A("oneb", 0, 128, 1, 0, 1), 1.0 / 16)
        for m in range(2):
            lin("wd%d" % m, "V", A("wc", 3, 512, 4, 32, 33), A("oneb", 0, 128, 1, 32, 33), -16.0 * m)
            quant("wk", 128 * m, 128 * m + 128, whole("wc", 512))
        for b in range(2):
            lin("x3%d" % b, "V", A("wc", b, 512, 4, 32, 33), A("oneb", 0, 128, 1, 32, 33), (-224.0, -2.0)[b])
            const("x2%d" % b, "G", Z("wc", b, 512, 4), 2)
        sel(Z("wc", 2, 512, 4), Z("oneb", 0, 128), [[-31, 2], [0, 2], [1, 32]], Op.is_ge, 31, -1)
        lin("x22", "V", Z("wc", 258, 384, 4), Z("wc", 258, 384, 4), -1.0)
        lin("x23", "V", Z("wc", 3, 512, 4), Z("wc", 2, 512, 4))
        quant("kc", 384, 512, whole("wc", 512))

    def place(t):
        c = "sc%d" % t

        def sc(k):
            return Z(c, k, k + 1)
        ts(sc(23), sc(1), 17.0, sc(9), Op.subtract, Op.mult)
        lin("p24%d" % t, "V", sc(24), sc(5), -0.5)
        lin("p25%d" % t, "V", sc(25), sc(5), -97.0, sc(23))
        tt(Z("dg", 0, 32), Z("cr%d" % t, 0, 32), Z("st", 3, 131, 4), Op.mult)
        red(sc(20), Z("dg", 0, 33), Op.add)
        act(junk(3, P, 0, L), Z("gi%d" % t, 0, P), Act.Sign, bias=sc(20), scale=-1.0 / HUGE, acc=sc(22))
        act(Z("tgb", t, t + 1), sc(22), scale=sc(24), bias=sc(25))
        dma("Y", T.tg[t:t + 1, :], T.tgb[0:L, t:t + 1], [Z("tgb", t, t + 1)], [], 4)

    def differences(tile, banks, x, u):
        pair = []
        for h in range(2):
            pair.append(mm(banks[h], (x, 64 * h, 64 * h + 128), (u, 128, 320), True, False))
            pair.append(mm(banks[h], (u, 0, 128), (x, 0, P), False, True))
        pair[2]["after"].setdefault(pair[1]["n"], False)
        for h in range(2):
            tt(A(tile, h, 4 * P, 4, 64 * h), A(banks[h], 0, P, 1, 64 * h), A("th%d" % h, 0, P, 1, 64 * h), Op.is_gt)

    for t in range(R):
        x, v, n, u, nx, c, cr, gi = "x%d" % t, "v%d" % t, "n%d" % t, "u%d" % t, "x%d" % (t + 1), "sc%d" % t, "cr%d" % t, "gi%d" % t
        last = t == R - 1
        ahead = not last
        land, at = ("cd%d" % (t + 1), 64) if ahead else (v, P)

        def sc(k):
            return Z(c, k, k + 1)

        def sca(k, p0=0, p1=128):
            return A(c, k, k + 1, 1, p0, p1)
        if t == 0:
            differences("cmt", ("b0", "b1"), x, u)
            for h in range(2):
                scan(A("rk%d" % h, 0, P, 1, 64 * h), A("cmt", h, 4 * P, 4, 64 * h), zero(P, 64 * h), 0.0, Op.add, Op.add)
                ts(A("et", h, 512, 2, 64 * h), A("er", 0, 256, 1, 64 * h), A("rk%d" % h, P - 1, P, 1, 64 * h), None, Op.is_equal)
            quant("e", 0, 128, whole("et", 512))
            mm("b2", ("e", 0, 128), JT)
            for m in range(2):
                ts(A("ol", m, m + 1), A("b2", m, m + 1), A("b2", m + 2, m + 3), None, Op.add)
            src, wide = x, P
        else:
            cd = "cd%d" % t
            mm("b6", (u, 0, 128), (cd, 0, 128), True, False)
            mm("b6", (cd, 0, 128), (u, 128, 256), False, True)
            tt(A("c2t", 0, 512, 4), A("b6", 0, 128), whole("th2", 128), Op.is_lt)
            quant("c2", 0, 128, whole("c2t", 512))
            for m in range(2):
                mm(("b7", "b4")[m], (W0, W1)[m], ("c2", 0, 128))
                red(sca(40 + m), A(("b7", "b4")[m], 0, 128), Op.min, True)
            ts(A("ol", 0, 2), A(c, 40, 42), 256.0, None, Op.mult)
            mm("b1", ("c2", 0, 128), W0)
            ts(sca(42), A("b1", 0, 1), 32.0, None, Op.is_lt)
            ts(A("cmt", 0, 4 * P, 4), whole("kr", P), A("kb", 0, 1), sca(42), Op.is_equal, Op.mult)
            src, wide = cd, 128
        pick_codes(A(n + "q", 0, K), A(src + "q", 0, wide), A("ol", 0, 2))
        pick("n%d" % t, "S", A(n + "s", 0, K), A(src + "s", 0, wide), A("ol", 0, 2))
        quant("cm", 0, P, whole("cmt", 4 * P))
        dst = T.cores[rank ^ (1 << t)]
        rid, pid = topo.addr(dst, core)
        mask, en = topo.mask(core, dst), len(topo.engines(core, dst))
        to = (T.sem["arr%d" % t], T.sem["sent%d" % t], pid, rid, mask)
        vq, nq, vs, ns = T[land + "q"][:, at:at + K], T[n + "q"][:, 0:K], T[land + "s"][:, at:at + K], T[n + "s"][:, 0:K]
        m1 = add("G", [A(n + "q", 0, K)], [], "send", lambda vq=vq, nq=nq, to=to: g.remote_dma(vq.bitcast(dt.uint8), nq.bitcast(dt.uint8), *to), "sent%d" % t, 2 * en)
        m2 = add("G", [A(n + "s", 0, K)], [], "send", lambda vs=vs, ns=ns, to=to: g.remote_dma(vs, ns, *to), "sent%d" % t, 2 * en)
        m2["after"][m1["n"]] = False
        fly = add("arrive", [], [A(land + "q", at, at + K), A(land + "s", at, at + K)], "fly", None, "arr%d" % t, 2 * en)
        fly["after"].update({m1["n"]: False, m2["n"]: False})
        move_pair(v, 0, x, 0, P)
        if t == 0:
            k0 = len(nodes)
            columns()
            later()
            candidates()
            for m in nodes[k0:]:
                if m["q"] == "G" or m["k"] == "const":
                    m["after"][m2["n"]] = False
        if ahead:
            query(t + 1)
            differences("cm2", ("b3", "b5"), x, "u%d" % (t + 1))
            quant("uu", 0, P, whole("cm2", 4 * P))
            mm("b3", ONES, ("uu", 0, P))
            if t == 0:
                lin("cm1%d" % t, "S", A("cmt", 1, 4 * P, 4, 64), zero(P, 64))
            i, o, on_v = A("b3", 0, P), whole("sg", P), MOVE.get("sg%d" % t, "S") == "V"
            if on_v:
                add("V", [i], [o], "lin", lambda i=i, o=o: V.tensor_scalar(ap(o), ap(i), 127.5, 2.0, Op.is_gt, Op.mult), tag="sg%d" % t)
            else:
                add("S", [i], [o], "lin", lambda i=i, o=o: S.activation(ap(o), ap(i), Act.Sign, bias=-127.5), tag="sg%d" % t)
            scan(whole("go", P), o, zero(P) if on_v else A("oneb", 0, P), cf(13), Op.add, Op.add)
            for m in range(4):
                e = min(16 * m, 48 - 16 * m)
                act(junk(4 + m, P - 2 * e), A("go", e, P - e), Act.Sign, bias=32.0 * m, scale=-1.0, acc=sca(32 + m))
            own_key = A("kb", 0, 1, 1, 0, 64)
            act(junk(8, P, 0, 64), A("go", 0, P, 1, 0, 64), Act.Sign, bias=cf(14, 64), scale=-1.0, acc=own_key)
            ts(whole("oo", 4), A(c, 32, 36), 0.5, 96.0, Op.mult, Op.add)
            pick_codes(A(land + "q", 0, 64), A(x + "q", 0, P), whole("oo", 4))
            pick("os%d" % t, "S", A(land + "s", 0, 64), A(x + "s", 0, P), whole("oo", 4))
            pick("pl%d" % t, "S", A("pl", 0, 64), whole("kr", P), whole("oo", 4))
        else:
            lin("f2%d" % t, "S", A("zz", XF, XF + 48, 2, 64, 128), zero(24, 64, 128))
        mm("b4", ONES, ("cm", 0, P))
        if t > 0:
            lin("mr%d" % t, "S", whole("mr", P), A("b4", 0, P), HUGE)
        else:
            ts(whole("mr", P), A("b4", 0, P), 159.5, HUGE, Op.is_gt, Op.mult)
        scan(A(gi, 0, P), whole("mr", P), zero(P), cf(15), Op.add, Op.add)
        if not ahead:
            act(junk(0, 12), A(gi, 15, P, 16), Act.Sign, bias=96.0, scale=-1.0 / HUGE, acc=sca(10))
        act(junk(1, P), A(gi, 0, P), Act.Sign, bias=96.0, scale=-1.0 / HUGE, acc=sca(11))
        for b in range(4):
            bank = ("b6", "b7", "b0", "b1")[b]
            mm(bank, ("eb", 128 * b, 128 * b + 128), (x, 0, P))
            lin("hd%d%d" % (t, b), "S", A("hd", b, 4 * P, 4), A(bank, 0, P), 0.5)
        if not ahead:
            ts(A("ohb", 0, 12), A("mwb", 0, 12), sca(10), None, Op.is_equal)
            ts(Z("ohh", 0, 12), Z("mwb", 0, 12), sc(10), 0.5, Op.is_equal, Op.mult)
            lin("s12%d" % t, "V", sc(12), sc(10), -8.0, 112.0)
            lin("s13%d" % t, "V", sca(13), sca(10), -16.0, sca(11))
            lin("s14%d" % t, "V", sca(14), sca(13), 0.5, 1.0)
            lin("s15%d" % t, "V", sc(15), sc(13), -0.5, 16.0)
            lin("s16%d" % t, "V", sca(16), sca(13), -0.5)
            ts(A("wft", 1, 512, 2), whole("cw", 256), sca(14), None, Op.is_equal)
            lin("z35%d" % t, "S", A("zz", XF + 3, XF + 48, 4, 64, 96), A("ohb", 0, 12, 1, 64, 96), sca(16, 64, 96))
            ts(Z("d0", 33, 48), Z("mw", 1, 16), sc(15), None, Op.is_lt)
            ts(Z("d1", 48, 64), Z("nk", 0, 16), sc(15), 0.0, Op.add, Op.max)
            quant("w", 0, 128, whole("wt", 512))
            mm("b2", ("w", 0, 128), (x, 0, P))
            lin("yw0", "S", A("yw", 0, P), A("b2", 0, P))
        else:
            for k in range(2):
                lin("bc%d%d" % (t, k), "S", A("bc", 32 * k, 32 * k + 32, 1, 0, 64), A("oneb", 0, 32, 1, 0, 64), (1.0, -1.0)[k], sca(11, 0, 64))
            turn(A("lr", 0, 64, 1, 0, 64), A("bc", 0, 64, 1, 0, 64))
            for k in range(2):
                act(junk(9, 32, 0, 64) if k else junk(0, 32, 0, 64), A("lr", 32 * k, 32 * k + 32, 1, 0, 64), Act.Sign, bias=own_key, scale=-1.0,
                    acc=sca(28 + k, 0, 64))
            ts(sca(30, 0, 64), sca(29, 0, 64), sca(28, 0, 64), -500.0, Op.subtract, Op.mult)
            ts(A("hq", 32, 33, 1, 0, 64), sca(30, 0, 64), sca(28, 0, 64), 1160.0, Op.add, Op.add)

        mm("b5", (land, at, at + 128), (x, 0, P))
        for b in range(4):
            mm(("b6", "b7", "b4", "b1")[b], ("eb", 128 * b, 128 * b + 128), (land, at, at + 128))
        tt(Z("zm", 0, P), A("b5", 0, P, 1, 0, L), Z("mr", 0, P), Op.subtract)
        scan(Z("pm", 17, 17 + P), Z("zm", 0, P), zero(P, 0, L), LOW, Op.max, Op.add)
        top = Z("pm", P + 16, P + 17)
        act(Z("uut", 2, 4 * (17 + P), 4), Z("pm", 0, 17 + P), Act.Sign, bias=top, scale=-1.0, acc=sc(1))
        act(junk(2, 12, 0, L), Z("pm", 16, 1 + P, 16), Act.Sign, bias=top, scale=-1.0, acc=sc(0))
        lo = 0 if ahead else 32
        act(Z("zz", 4 * lo + 1, XF, 4), Z("dm", lo, 40), Act.Relu, scale=sc(0), bias=sc(1))
        lin("xo%d" % t, "V", Z("zz", 4 * lo, XF, 4), Z("d16", lo, 40), sc(0))
        if not ahead:
            lin("tb%d" % t, "S", Z("tb", 0, 32), Z("up32", 0, 32), sc(1))
            lin("s3%d" % t, "S", sc(3), sc(0), -16.0, sc(1))
            ts(Z("oha", 0, 12), Z("mw", 1, 13), sc(0), None, Op.is_equal)
            lin("s2%d" % t, "S", sc(2), sc(0), -16.0, cf(9, L))
            lin("xa0%d" % t, "S", Z("xa", 0, 24, 2), Z("oha", 0, 12), sc(2))
            lin("s4%d" % t, "S", sc(4), sc(3), -1.0, cf(10, L))
            lin("xa1%d" % t, "S", Z("xa", 1, 24, 2), Z("oha", 0, 12), sc(4))
        for b in range(4):
            lin("ha%d%d" % (t, b), "S", A("ha", b, 128, 4), A(("b6", "b7", "b4", "b1")[b], 0, K), 0.5)
        quant("xo", 0, 128, A("zz", 0, 512))
        mm("b3", X1, ("xo", 0, 128))
        ts(A("om", 0, 8), A("b3", 32, 40), 4.0, cf(4), Op.mult, Op.add)
        ho, hi_, of, ha = A("mt", 0, 128), A("hd", 0, 4 * P), A("om", 0, 8), A("ha", 0, 128)
        add("V", [hi_, of, ha], [ho], "pick", lambda ho=ho, hi_=hi_, of=of, ha=ha: V.tensor_tensor(ap(ho), ap(hi_).indirect(ap(of)), ap(ha), Op.add))
        quant(land, at + K, at + 160, whole("mt", 512))
        if ahead:
            move_pair(v, P, land, at, 64)
            ts(Z("uut", 67, 64 + 4 * P, 4), Z("pm", 17, 17 + P), top, -1.0, Op.is_lt, Op.mult)
            quant("uu", 0, P, A("uut", 64, 64 + 4 * P))
            mm("b0", X2, ("xo", 0, 128))
            mm("b5", X1, ("uu", 0, P))
            mm("b2", X2, ("uu", 0, P))
            act(junk(4, P), A("b5", 0, P), Act.Sign, bias=0.5, scale=-1.0, acc=sca(17))
            act(junk(5, P), A("b2", 0, P), Act.Sign, bias=cf(25), scale=-1.0, acc=sca(18))
            act(junk(6, P), A(gi, 0, P), Act.Sign, bias=sca(17), scale=-2.0 / HUGE, acc=sca(19))
            turn(A("kb", 0, 32, 1, 64, 128), A("b0", 0, 32, 1, 64, 128))
            ts(A("hq", 0, 32, 1, 0, 64), A("b0", 0, 32, 1, 0, 64), A("kb", 0, 1, 1, 0, 64), 4000.0, Op.not_equal, Op.mult)
            red(sca(27, 0, 64), A("hq", 0, 33, 1, 0, 64), Op.min)
            lin("xd%d" % t, "S", sca(27, 64, 128), sca(17, 64, 128), A("cf", 23, 24, 1, 64, 128), A("cf", 24, 25, 1, 64, 128))
            ts(sca(21), sca(18), sca(27), -HUGE, Op.is_gt, Op.mult)
            lin("bl%d" % t, "S", A("bc", 64, 96), zero(32), 1.0, sca(19))
            turn(A("pl", 64, 96), A("bc", 64, 96))
            lin("kl%d" % t, "S", A("kb", 0, 1, 1, 64, 96), sca(19, 64, 96))
            lin("bk%d" % t, "S", sca(26), A("kb", 0, 1), -TINY, sca(21))
            lin("t0%d" % t, "S", A("th2", 0, 96), whole("pl", 96), TINY, sca(26))
            lin("t1%d" % t, "S", A("th2", 96, 128), A("b0", 0, 32), TINY, sca(26))
            ts(A("c2t", 1, 512, 4), eye, sca(21), -32.0 / HUGE, Op.mult, Op.mult)

            def up(k):
                return sca(k, 64, 128)
            key = A("kb", 0, 1, 1, 64, 128)
            act(junk(0, 12, 64, 128), A("m32", 0, 12, 1, 64, 128), Act.Sign, bias=key, scale=-1.0, acc=up(10))
            lin("u12%d" % t, "S", up(12), up(10), -16.0, key)
            lin("u13%d" % t, "S", up(13), up(10), -8.0, A("cf", 21, 22, 1, 64, 128))
            lin("u14%d" % t, "S", up(14), up(12), -0.5, A("cf", 22, 23, 1, 64, 128))
            lin("u15%d" % t, "S", up(15), up(21), 1.0 / HUGE, 1.0)
            ts(A("ohb", 0, 12, 1, 64, 128), A("mwb", 1, 13, 1, 64, 128), up(10), up(15), Op.is_equal, Op.mult)
            ts(A("wft", 0, 512, 2, 64, 128), A("cx", 0, 256, 1, 64, 128), up(12), None, Op.is_equal)
            for b in range(2):
                lin("ux%d%d" % (t, b), "S", A("zz", XF + 2 * b, XF + 48, 4, 64, 128), A("ohb", 0, 12, 1, 64, 128), up(13 + b))
            aim = A("kb", 1, 2, 1, 64, 96)
            ts(sca(23, 64, 96), sca(19, 64, 96), aim, -0.5, Op.add, Op.mult)
            ts(sca(24, 64, 96), sca(23, 64, 96), -193.0, sca(15, 64, 96), Op.add, Op.mult)
            lin("u25%d" % t, "S", sca(25, 64, 96), aim, 0.5, 96.0)
            lin("utg%d" % t, "S", A("tgb", t, t + 1, 1, 64, 96), sca(24, 64, 96), 1.0, sca(25, 64, 96))
            dma("Y", T.tg[t:t + 1, :], T.tgb[64:96, t:t + 1], [A("tgb", t, t + 1, 1, 64, 96)], [], 4)
        else:
            turn(Z("tt", 0, 32), Z("tb", 0, 32))
            ts(Z("ne", 0, 32), Z("tt", 0, 32), sc(1), None, Op.is_equal)
            ts(Z("wft", 0, 512, 2), Z("cw", 0, 256), sc(3), None, Op.is_equal)
            scan(Z("ms", 0, 64), Z("ne", 0, 64), zero(64, 0, L), 0.0, Op.max, Op.max)
            lin("s9%d" % t, "S", sc(9), Z("ms", 31, 32), -1.0, 1.0)
            lin("s5%d" % t, "S", sc(5), Z("ms", 31, 32))
            lin("zx%d" % t, "S", Z("zz", XF, XF + 48, 2), Z("xa", 0, 24), sc(9))
            turn(Z("d1", 0, 32), Z("ms", 32, 64))
            scan(Z(cr, 0, 64), Z("d0", 0, 64), Z("d1", 0, 64), cf(12, L), Op.mult, Op.add)
            act(junk(10, 64, 0, L), Z(cr, 0, 64), Act.Sign, scale=-1.0, acc=sc(7))
            ts(sc(6), Z(cr, 31, 32), 0.0, sc(12), Op.is_gt, Op.mult)
            lin("z1%d" % t, "V", Z("zz", XF + 1, XF + 48, 4), Z("ohb", 0, 12), sc(6))
            lin("z3%d" % t, "S", Z("zz", XF + 3, XF + 48, 4), Z("ohh", 0, 12), sc(7))
        quant("wf", 0, 128, whole("wft", 512))
        quant("xf", 0, 128, A("zz", XF, XF + 512))
        mm("b3" if ahead else "b2", ("wf", 0, 128), ("xf", 0, 128))
        copy(A("of", 0, 12), A("b3" if ahead else "b2", 0, 12))
        if not last:
            for a, b in ((0, 8), (8, 12)):
                pick_codes(A(nx + "q", 16 * a, 16 * b), A(v + "q", 0, 256), A("of", a, b))
                pick("xs%d%d" % (t, a), "S", A(nx + "s", 16 * a, 16 * b), A(v + "s", 0, 256), A("of", a, b))
        else:
            mm("b3", ("w", 0, 128), (v, P, P + 128))
            lin("yw1", "S", A("yw", P, P + 64), A("b3", 0, 64))
            for a, b in ((0, 6), (6, 12)):
                pick_codes(A(nx + "q", 16 * a, 16 * b), A(v + "q", 0, 256), A("of", a, b))
                pick("yo%d" % a, "S", A("yo", 16 * a, 16 * b), A("yw", 0, 256), A("of", a, b))
                pick("xs3%d" % a, "VS"[a // 6], A(nx + "s", 16 * a, 16 * b), A(v + "s", 0, 256), A("of", a, b))
            dma("Y", T.oc[:, :], T.x3q[:, 0:P].bitcast(dt.uint8), [A("x3q", 0, P)], [], 4 * P)
            dma("Y", T.y[:, :], T.yo[:, 0:P], [A("yo", 0, P)], [], 4 * P)
            for k in range(4):
                dma("YS"[k % 2], T.osc[4 * k:4 * k + 4, :], T.x3s[32 * k:32 * k + 4, 0:P], [A("x3s", 0, P)], [], 8)
            place(t)
    emit()
